import numpy as np
import ml_dtypes


def mxq(x, axis, fmt="e4m3"):
    dtype, down = {"e4m3": (ml_dtypes.float8_e4m3fn, 7), "e5m2": (ml_dtypes.float8_e5m2, 14)}[fmt]
    v = np.moveaxis(np.asarray(x, np.float32).astype(ml_dtypes.bfloat16).astype(np.float64), axis, -1)
    blocks = v.reshape(v.shape[:-1] + (-1, 32))
    amax = np.abs(blocks).max(-1, keepdims=True)
    byte = np.maximum(np.where(amax > 0, np.frexp(amax)[1] - 1 + 127, 0) - down, 1)
    scale = np.exp2(byte - 127.0)
    codes = (blocks / scale).astype(np.float32).astype(dtype).astype(np.float64)
    return np.moveaxis((codes * scale).reshape(v.shape), -1, axis)


WIDE = False


def mx_kscale(k):
    if not WIDE:
        return np.ones(k)
    levels = np.array([10, -10, 5, -5, 0])
    if k % 512:
        return np.exp2(np.random.permutation(np.resize(levels, k // 32))).repeat(32)
    a = np.empty((k // 512, 16))
    for p in range(k // 512):
        a[p, :8] = np.random.permutation(np.resize(levels, 8))
        for g in range(8):
            far = levels[np.abs(levels - a[p, g]) >= 10]
            a[p, g + 8] = far[np.random.randint(len(far))]
    return np.exp2(a.ravel()).repeat(32)


def f64(x):
    return np.asarray(x).astype(np.float64)


def striped(idx):
    return np.tile(idx.reshape(-1, 16).T, (8, 1)).astype(np.uint16)


def unstriped(offs):
    return offs[:16].T.reshape(-1).astype(np.int64)


E2M1 = np.array([0.0, 0.5, 1.0, 1.5, 2.0, 3.0, 4.0, 6.0, -0.0, -0.5, -1.0, -1.5, -2.0, -3.0, -4.0, -6.0])


def pack_weight(w, fmt):
    k, n = w.shape
    w = f64(np.asarray(w, np.float32).astype(ml_dtypes.bfloat16)).reshape(k // 32, 32, n)
    amax = np.abs(w).max(1)
    if fmt == "e4m3":
        byte = np.frexp(amax)[1] - 1 + 127 - 7
    else:
        mant, ex = np.frexp(amax / 6.0)
        byte = np.where(mant > 0.5, ex, ex - 1) + 127
    byte = np.clip(np.where(amax > 0, byte, 1), 1, 254)
    scaled = (w * np.exp2(127.0 - byte)[:, None, :]).reshape(k, n).astype(np.float32)
    by_word = np.ascontiguousarray(scaled.reshape(k // 512, 128, 4, n).transpose(0, 1, 3, 2))
    if fmt == "e4m3":
        words = by_word.astype(ml_dtypes.float8_e4m3fn).view(np.uint8)
    else:
        c = by_word.astype(ml_dtypes.float4_e2m1fn).view(np.uint8) & 0xF
        words = (c[..., 0::2] | (c[..., 1::2] << 4)).reshape(k // 512, 128, 2 * n)
    return np.ascontiguousarray(words), np.ascontiguousarray(byte.astype(np.uint8).reshape(k // 512, 16, n))


def unpack_weight(words, scales, fmt):
    g, _, n = scales.shape
    words = np.ascontiguousarray(words).reshape(g, 128, n, -1)
    if fmt == "e4m3":
        vals = words.view(ml_dtypes.float8_e4m3fn).astype(np.float64)
    else:
        nib = np.empty((g, 128, n, 4), np.uint8)
        nib[..., 0::2] = words & 0xF
        nib[..., 1::2] = words >> 4
        vals = E2M1[nib]
    vals = vals * np.repeat(np.exp2(scales.astype(np.float64) - 127.0), 8, axis=1)[..., None]
    return vals.transpose(0, 1, 3, 2).reshape(g * 512, n)


def gelu(v):
    return 0.5 * v * (1.0 + np.tanh(np.sqrt(2.0 / np.pi) * (v + 0.044715 * v**3)))


K, C, H, N, T, T2, S = 1024, 512, 1024, 512, 2048, 2048, 1024

def setup_inputs():
    n = np.random.standard_normal
    s = mx_kscale(K)[:, None]
    s2 = mx_kscale(C)[:, None]
    u = mx_kscale(H)[:, None]
    tab_words, tab_scales = pack_weight(n((K, T)) * s, "e4m3")
    tab2_words, tab2_scales = pack_weight(n((C, T2)) * s2, "e4m3")
    wb4_words, wb4_scales = pack_weight(0.5 * n((C, H)) / np.sqrt(C) / s2, "e2m1")
    w8_words, w8_scales = pack_weight(n((H, N)) / np.sqrt(H) / u, "e4m3")
    return {
        "tab_words": tab_words, "tab_scales": tab_scales,
        "tab2_words": tab2_words, "tab2_scales": tab2_scales,
        "offs": striped(np.random.permutation(T)[:S]),
        "offs2": striped(np.random.permutation(T2)[:S]),
        "wa": (n((K, H)) / np.sqrt(K) / s * u.T).astype(np.float32),
        "wb4_words": wb4_words, "wb4_scales": wb4_scales,
        "gT": (0.7 * n((H, T)) * u).astype(np.float32),
        "w8_words": w8_words, "w8_scales": w8_scales,
        "bias": (0.5 * n(N)).astype(np.float32),
    }

def reference(tab_words, tab_scales, tab2_words, tab2_scales, offs, offs2, wa, wb4_words, wb4_scales, gT, w8_words, w8_scales, bias):
    v = unpack_weight(tab_words, tab_scales, "e4m3")[:, unstriped(offs)]
    v2 = unpack_weight(tab2_words, tab2_scales, "e4m3")[:, unstriped(offs2)]
    g = f64(gT)[:, unstriped(offs)]
    wb = unpack_weight(wb4_words, wb4_scales, "e2m1")
    w = unpack_weight(w8_words, w8_scales, "e4m3")
    a = mxq(f64(wa), 0, "e4m3").T @ v
    b = wb.T @ v2
    h = a * np.exp(b) + g
    y = w.T @ mxq(h, 0, "e4m3")
    return y + f64(bias)[:, None]

@@ -1,0 +1,244 @@
+from contextlib import ExitStack
+
+import concourse.mybir as mybir
+from concourse.masks import make_identity
+
+K, C, H, N, T, S = 1024, 512, 1024, 512, 2048, 1024
+FLOPS = 2 * S * (K * H + C * H + H * N)
+
+F32 = mybir.dt.float32
+BF16 = mybir.dt.bfloat16
+I32 = mybir.dt.int32
+U32 = mybir.dt.uint32
+U16 = mybir.dt.uint16
+U8 = mybir.dt.uint8
+FP8X4 = mybir.dt.float8_e4m3fn_x4
+FP4X4 = mybir.dt.float4_e2m1fn_x4
+ACT = mybir.ActivationFunctionType
+ALU = mybir.AluOpType
+
+P = 128
+PACK = 4
+PASS = P * PACK
+BANK = 512
+RING = 10
+LAST_CHUNKS = (512, 256, 256)
+
+
+def tile_list_speaker_affine_flow_kernel(
+    tc, tab_words, tab_scales, tab2_words, tab2_scales, offs, offs2, wa,
+    wb4_words, wb4_scales, gT, w8_words, w8_scales, bias, out,
+):
+    nc = tc.nc
+    with ExitStack() as ctx:
+        keep = ctx.enter_context(tc.tile_pool(name="keep", bufs=1))
+        ring = ctx.enter_context(tc.tile_pool(name="ring", bufs=RING))
+        stage = ctx.enter_context(tc.tile_pool(name="stage", bufs=2))
+        outs = ctx.enter_context(tc.tile_pool(name="outs", bufs=6))
+        psum_a = ctx.enter_context(tc.psum_pool(name="psum_a", bufs=3))
+        psum_b = ctx.enter_context(tc.psum_pool(name="psum_b", bufs=2))
+        psum_y = ctx.enter_context(tc.psum_pool(name="psum_y", bufs=3))
+
+        def kept(shape, dtype, name):
+            return keep.tile(shape, dtype, name=name, align_bytes=64)
+
+        idx = keep.tile([P, S // 16], U16, name="idx")
+        idx2 = keep.tile([P, S // 16], U16, name="idx2")
+        tab_plane = kept([P, T], U8, "tab_plane")
+        tab2_plane = kept([P, T], U8, "tab2_plane")
+        wb_plane = kept([P, H], U8, "wb_plane")
+        w8_plane = kept([P, N], U8, "w8_plane")
+        wb_words = kept([P, 2 * H], U8, "wb_words")
+        w8_codes = kept([P, H // PASS, N], U32, "w8_codes")
+        bias_sb = kept([P, N // P], F32, "bias_sb")
+
+        nc.vector.memset(tab2_plane[:].bitcast(I32), 0)
+        nc.vector.memset(tab_plane[:].bitcast(I32), 0)
+        nc.gpsimd.memset(wb_plane[:].bitcast(I32), 0)
+        nc.gpsimd.memset(w8_plane[:].bitcast(I32), 0)
+        bias_rows = kept([P, P], F32, "bias_rows")
+        identity = kept([P, P], F32, "identity")
+        nc.gpsimd.memset(bias_rows[:], 0.0)
+        make_identity(nc, identity[:])
+
+        def load_plane(queue, plane, scales):
+            rows = 4 * scales.shape[0]
+            for q in range(4):
+                queue.dma_start(
+                    out=plane[32 * q : 32 * q + rows, :].bitcast(I32),
+                    in_=scales[:, 4 * q : 4 * q + 4, :].bitcast(I32),
+                )
+
+        def load_words(words):
+            window = ring.tile([P, T], U32, name="ring")
+            nc.sync.dma_start(out=window[:].bitcast(I32), in_=words.rearrange("p t i -> p (t i)").bitcast(I32))
+            return window
+
+        def load_wa(a, c):
+            raw = ring.tile([P, PACK, PASS], F32, name="ring")
+            rows = wa[c * PASS : (c + 1) * PASS, a * PASS : (a + 1) * PASS]
+            nc.sync.dma_start(out=raw[:], in_=rows.rearrange("(p i) r -> p i r", i=PACK))
+            return raw
+
+        g_planes = gT.rearrange("(a p t) c -> a t p c", p=P, t=PACK)
+
+        def load_g(a, t):
+            window = ring.tile([P, T], F32, name="ring")
+            nc.sync.dma_start(out=window[:], in_=g_planes[a, t])
+            return window
+
+        nc.sync.dma_start(idx2[:], offs2)
+        nc.sync.dma_start(idx[:], offs)
+        load_plane(nc.sync, tab2_plane, tab2_scales)
+        tab2_window = load_words(tab2_words[0])
+        tab_window = [load_words(tab_words[0])]
+        load_plane(nc.sync, tab_plane, tab_scales)
+        tab_window.append(load_words(tab_words[1]))
+        nc.sync.dma_start(out=wb_words[:].bitcast(I32), in_=wb4_words[0].bitcast(I32))
+        load_plane(nc.sync, wb_plane, wb4_scales)
+        wa_raw, g_window = {}, {}
+        for a in range(H // PASS):
+            wa_raw[a, 0] = load_wa(a, 0)
+            g_window[a, 0] = load_g(a, 0)
+            wa_raw[a, 1] = load_wa(a, 1)
+            g_window[a, 1] = load_g(a, 1)
+            if a == 1:
+                nc.sync.dma_start(
+                    out=w8_codes[:].bitcast(I32),
+                    in_=w8_words.rearrange("a p n i -> p a (n i)").bitcast(I32),
+                )
+                load_plane(nc.sync, w8_plane, w8_scales)
+                nc.sync.dma_start(out=bias_rows[0 : N // P, :], in_=bias.rearrange("(q p) -> q p", p=P))
+            g_window[a, 2] = load_g(a, 2)
+            g_window[a, 3] = load_g(a, 3)
+
+        v2_scales = kept([P, S], U8, "v2_scales")
+        v2_codes = kept([P, S], U32, "v2_codes")
+        v_scales = kept([P, S], U8, "v_scales")
+        v_codes = [kept([P, S], U32, "v_codes%d" % c) for c in range(K // PASS)]
+        wb_scales = kept([P, H], U8, "wb_scales")
+        wb_codes = kept([P, 2 * H], U8, "wb_codes")
+
+        nc.vector.tensor_copy(v2_scales[:], tab2_plane[:].indirect(idx2[:]))
+        nc.vector.tensor_copy(v2_codes[:], tab2_window[:].indirect(idx2[:]))
+        nc.vector.tensor_copy(v_scales[:], tab_plane[:].indirect(idx[:]))
+        nc.vector.tensor_copy(v_codes[0][:], tab_window[0][:].indirect(idx[:]))
+        nc.vector.tensor_copy(v_codes[1][:], tab_window[1][:].indirect(idx[:]))
+        nc.vector.tensor_copy(
+            wb_codes[:].bitcast(U16).rearrange("p (a t m) -> p a t m", t=PACK, m=P),
+            wb_words[:].bitcast(U16).rearrange("p (a m t) -> p a t m", t=PACK, m=P),
+        )
+        nc.vector.tensor_copy(
+            wb_scales[:].rearrange("p (a t m) -> p a t m", t=PACK, m=P),
+            wb_plane[:].rearrange("p (a m t) -> p a t m", t=PACK, m=P),
+        )
+
+        h_codes = [kept([P, S], U32, "h_codes%d" % a) for a in range(H // PASS)]
+        h_scales = [kept([P, S], U8, "h_scales%d" % a) for a in range(H // PASS)]
+
+        def quantise_wa(a, c):
+            grouped = stage.tile([P, PASS * PACK], BF16, name="wa_grouped", align_bytes=64)
+            nc.scalar.copy(
+                grouped[:].rearrange("p (t m i) -> p m i t", t=PACK, i=PACK),
+                wa_raw[a, c][:].rearrange("p i (m t) -> p m i t", t=PACK),
+            )
+            codes = kept([P, PASS], U32, "wa_codes%d%d" % (a, c))
+            scales = kept([P, PASS], U8, "wa_scales%d%d" % (a, c))
+            nc.vector.quantize_mx(out=codes[:].bitcast(FP8X4), scales=scales[:], in_=grouped[:])
+            return codes, scales
+
+        def gather_g(a, t, g, j0, width):
+            offsets = idx[:, j0 // 16 : (j0 + width) // 16]
+            nc.vector.tensor_copy(g[:, t, j0 : j0 + width], g_window[a, t][:].indirect(offsets))
+
+        def scaled_frames(a, t, wa_q, scaled, j0, width):
+            cols = slice(j0, j0 + width)
+            r0 = a * PASS + t * P
+            b_sum = psum_b.tile([P, width], F32, name="b_sum")
+            nc.tensor.matmul_mx(
+                out=b_sum[:],
+                lhsT=wb_codes[:, 2 * r0 : 2 * (r0 + P)].bitcast(FP4X4),
+                lhsT_scale=wb_scales[:, r0 : r0 + P],
+                rhs=v2_codes[:, cols].bitcast(FP8X4),
+                rhs_scale=v2_scales[:, cols],
+                start=True,
+                stop=True,
+            )
+            nc.scalar.activation(scaled[:, t, cols], b_sum[:], ACT.Exp)
+            a_sum = psum_a.tile([P, width], F32, name="a_sum")
+            for c in range(K // PASS):
+                codes, scales = wa_q[c]
+                nc.tensor.matmul_mx(
+                    out=a_sum[:],
+                    lhsT=codes[:, t * P : (t + 1) * P].bitcast(FP8X4),
+                    lhsT_scale=scales[:, t * P : (t + 1) * P],
+                    rhs=v_codes[c][:, cols].bitcast(FP8X4),
+                    rhs_scale=v_scales[4 * c :, cols],
+                    start=(c == 0),
+                    stop=(c == K // PASS - 1),
+                )
+            nc.vector.tensor_tensor(scaled[:, t, cols], a_sum[:], scaled[:, t, cols], ALU.mult)
+
+        def add_shift(scaled, g, j0, width):
+            h = stage.tile([P, width * PACK], BF16, name="h", align_bytes=64)
+            cols = slice(j0, j0 + width)
+            nc.vector.tensor_tensor(
+                h[:].rearrange("p (c i t) -> p c t i", i=2, t=PACK),
+                scaled[:, :, cols].rearrange("p t (c i) -> p c t i", i=2),
+                g[:, :, cols].rearrange("p t (c i) -> p c t i", i=2),
+                ALU.add,
+            )
+            return h
+
+        def quantise_h(a, h, j0, width):
+            cols = slice(j0, j0 + width)
+            nc.vector.quantize_mx(out=h_codes[a][:, cols].bitcast(FP8X4), scales=h_scales[a][:, cols], in_=h[:])
+
+        def features(j0, width):
+            cols = slice(j0, j0 + width)
+            for q in range(N // P):
+                y_sum = psum_y.tile([P, width], F32, name="y_sum")
+                for a in range(H // PASS):
+                    nc.tensor.matmul_mx(
+                        out=y_sum[:],
+                        lhsT=w8_codes[:, a, q * P : (q + 1) * P].bitcast(FP8X4),
+                        lhsT_scale=w8_plane[4 * a :, q * P : (q + 1) * P],
+                        rhs=h_codes[a][:, cols].bitcast(FP8X4),
+                        rhs_scale=h_scales[a][:, cols],
+                        start=(a == 0),
+                        stop=(a == H // PASS - 1),
+                    )
+                y = outs.tile([P, width], F32, name="y")
+                nc.scalar.activation(y[:], y_sum[:], ACT.Identity, bias=bias_sb[:, q : q + 1])
+                nc.sync.dma_start(out=out[q * P : (q + 1) * P, cols], in_=y[:])
+
+        g = [kept([P, PACK, S], F32, "g%d" % a) for a in range(H // PASS)]
+        scaled = [kept([P, PACK, S], F32, "scaled%d" % a) for a in range(H // PASS)]
+
+        gather_g(0, 0, g[0], 0, S)
+        wa_q = [quantise_wa(0, c) for c in range(K // PASS)]
+        for t in range(PACK):
+            if t > 0:
+                gather_g(0, t, g[0], 0, S)
+            for j0 in range(0, S, BANK):
+                scaled_frames(0, t, wa_q, scaled[0], j0, BANK)
+        wa_q = [quantise_wa(1, c) for c in range(K // PASS)]
+        bias_t = psum_y.tile([P, P], F32, name="y_sum")
+        nc.tensor.transpose(bias_t[:], bias_rows[:], identity[:])
+        nc.scalar.copy(bias_sb[:], bias_t[:, 0 : N // P])
+        pending = [(0, add_shift(scaled[0], g[0], j0, BANK), j0, BANK) for j0 in range(0, S, BANK)]
+        j0 = 0
+        for width in LAST_CHUNKS:
+            for t in range(PACK):
+                gather_g(1, t, g[1], j0, width)
+                for a, h, h0, h_width in pending:
+                    quantise_h(a, h, h0, h_width)
+                    if a == 1:
+                        features(h0, h_width)
+                pending = []
+                scaled_frames(1, t, wa_q, scaled[1], j0, width)
+            pending = [(1, add_shift(scaled[1], g[1], j0, width), j0, width)]
+            j0 += width
+        for a, h, h0, h_width in pending:
+            quantise_h(a, h, h0, h_width)
+            features(h0, h_width)

@@ -21,7 +21,7 @@ P = 128
 PACK = 4
 PASS = P * PACK
 BANK = 512
-RING = 10
+RING = 9
 LAST_CHUNKS = (512, 256, 256)
 
 
@@ -36,8 +36,8 @@ def tile_list_speaker_affine_flow_kernel(
         stage = ctx.enter_context(tc.tile_pool(name="stage", bufs=2))
         outs = ctx.enter_context(tc.tile_pool(name="outs", bufs=6))
         psum_a = ctx.enter_context(tc.psum_pool(name="psum_a", bufs=3))
-        psum_b = ctx.enter_context(tc.psum_pool(name="psum_b", bufs=2))
         psum_y = ctx.enter_context(tc.psum_pool(name="psum_y", bufs=3))
+        psum_h = ctx.enter_context(tc.psum_pool(name="psum_h", bufs=2))
 
         def kept(shape, dtype, name):
             return keep.tile(shape, dtype, name=name, align_bytes=64)
@@ -52,8 +52,8 @@ def tile_list_speaker_affine_flow_kernel(
         w8_codes = kept([P, H // PASS, N], U32, "w8_codes")
         bias_sb = kept([P, N // P], F32, "bias_sb")
 
-        nc.vector.memset(tab2_plane[:].bitcast(I32), 0)
-        nc.vector.memset(tab_plane[:].bitcast(I32), 0)
+        nc.gpsimd.memset(tab2_plane[:].bitcast(I32), 0)
+        nc.gpsimd.memset(tab_plane[:].bitcast(I32), 0)
         nc.gpsimd.memset(wb_plane[:].bitcast(I32), 0)
         nc.gpsimd.memset(w8_plane[:].bitcast(I32), 0)
         bias_rows = kept([P, P], F32, "bias_rows")
@@ -80,68 +80,83 @@ def tile_list_speaker_affine_flow_kernel(
             nc.sync.dma_start(out=raw[:], in_=rows.rearrange("(p i) r -> p i r", i=PACK))
             return raw
 
-        g_planes = gT.rearrange("(a p t) c -> a t p c", p=P, t=PACK)
+        g_planes = [
+            gT[0:PASS, :].rearrange("(t p) c -> t p c", p=P),
+            gT[PASS : 2 * PASS, :].rearrange("(p t) c -> t p c", t=PACK),
+        ]
 
         def load_g(a, t):
             window = ring.tile([P, T], F32, name="ring")
-            nc.sync.dma_start(out=window[:], in_=g_planes[a, t])
+            nc.sync.dma_start(out=window[:], in_=g_planes[a][t])
             return window
 
         nc.sync.dma_start(idx2[:], offs2)
         nc.sync.dma_start(idx[:], offs)
+        nc.sync.dma_start(out=wb_words[:].bitcast(I32), in_=wb4_words[0].bitcast(I32))
         load_plane(nc.sync, tab2_plane, tab2_scales)
         tab2_window = load_words(tab2_words[0])
         tab_window = [load_words(tab_words[0])]
         load_plane(nc.sync, tab_plane, tab_scales)
         tab_window.append(load_words(tab_words[1]))
-        nc.sync.dma_start(out=wb_words[:].bitcast(I32), in_=wb4_words[0].bitcast(I32))
         load_plane(nc.sync, wb_plane, wb4_scales)
         wa_raw, g_window = {}, {}
-        for a in range(H // PASS):
-            wa_raw[a, 0] = load_wa(a, 0)
-            g_window[a, 0] = load_g(a, 0)
-            wa_raw[a, 1] = load_wa(a, 1)
-            g_window[a, 1] = load_g(a, 1)
-            if a == 1:
-                nc.sync.dma_start(
-                    out=w8_codes[:].bitcast(I32),
-                    in_=w8_words.rearrange("a p n i -> p a (n i)").bitcast(I32),
-                )
-                load_plane(nc.sync, w8_plane, w8_scales)
-                nc.sync.dma_start(out=bias_rows[0 : N // P, :], in_=bias.rearrange("(q p) -> q p", p=P))
-            g_window[a, 2] = load_g(a, 2)
-            g_window[a, 3] = load_g(a, 3)
+        wa_raw[0, 0] = load_wa(0, 0)
+        wa_raw[0, 1] = load_wa(0, 1)
+        g_window[0, 0] = load_g(0, 0)
+        g_window[0, 1] = load_g(0, 1)
+        wa_raw[1, 0] = load_wa(1, 0)
+        wa_raw[1, 1] = load_wa(1, 1)
+        g_window[0, 2] = load_g(0, 2)
+        g_window[0, 3] = load_g(0, 3)
+        g_window[1, 0] = load_g(1, 0)
+        g_window[1, 1] = load_g(1, 1)
+        nc.sync.dma_start(
+            out=w8_codes[:].bitcast(I32),
+            in_=w8_words.rearrange("a p n i -> p a (n i)").bitcast(I32),
+        )
+        load_plane(nc.sync, w8_plane, w8_scales)
+        nc.sync.dma_start(out=bias_rows[0 : N // P, :], in_=bias.rearrange("(q p) -> q p", p=P))
+        g_window[1, 2] = load_g(1, 2)
+        g_window[1, 3] = load_g(1, 3)
 
         v2_scales = kept([P, S], U8, "v2_scales")
         v2_codes = kept([P, S], U32, "v2_codes")
         v_scales = kept([P, S], U8, "v_scales")
         v_codes = [kept([P, S], U32, "v_codes%d" % c) for c in range(K // PASS)]
-        wb_scales = kept([P, H], U8, "wb_scales")
-        wb_codes = kept([P, 2 * H], U8, "wb_codes")
 
         nc.vector.tensor_copy(v2_scales[:], tab2_plane[:].indirect(idx2[:]))
         nc.vector.tensor_copy(v2_codes[:], tab2_window[:].indirect(idx2[:]))
         nc.vector.tensor_copy(v_scales[:], tab_plane[:].indirect(idx[:]))
         nc.vector.tensor_copy(v_codes[0][:], tab_window[0][:].indirect(idx[:]))
         nc.vector.tensor_copy(v_codes[1][:], tab_window[1][:].indirect(idx[:]))
+
+        wb_codes = kept([P, 2 * PASS], U8, "wb_codes")
+        wb_scales = kept([P, PASS], U8, "wb_scales")
         nc.vector.tensor_copy(
-            wb_codes[:].bitcast(U16).rearrange("p (a t m) -> p a t m", t=PACK, m=P),
-            wb_words[:].bitcast(U16).rearrange("p (a m t) -> p a t m", t=PACK, m=P),
+            wb_codes[:].bitcast(U16).rearrange("p (t m) -> p t m", t=PACK),
+            wb_words[:, 2 * PASS :].bitcast(U16).rearrange("p (m t) -> p t m", t=PACK),
         )
         nc.vector.tensor_copy(
-            wb_scales[:].rearrange("p (a t m) -> p a t m", t=PACK, m=P),
-            wb_plane[:].rearrange("p (a m t) -> p a t m", t=PACK, m=P),
+            wb_scales[:].rearrange("p (t m) -> p t m", t=PACK),
+            wb_plane[:, PASS:].rearrange("p (m t) -> p t m", t=PACK),
         )
+        wb_half = [(wb_words, wb_plane), (wb_codes, wb_scales)]
 
         h_codes = [kept([P, S], U32, "h_codes%d" % a) for a in range(H // PASS)]
         h_scales = [kept([P, S], U8, "h_scales%d" % a) for a in range(H // PASS)]
 
         def quantise_wa(a, c):
             grouped = stage.tile([P, PASS * PACK], BF16, name="wa_grouped", align_bytes=64)
-            nc.scalar.copy(
-                grouped[:].rearrange("p (t m i) -> p m i t", t=PACK, i=PACK),
-                wa_raw[a, c][:].rearrange("p i (m t) -> p m i t", t=PACK),
-            )
+            if a == 0:
+                nc.scalar.copy(
+                    grouped[:].rearrange("p (m e i) -> p m i e", e=2, i=PACK),
+                    wa_raw[a, c][:].rearrange("p i (m e) -> p m i e", e=2),
+                )
+            else:
+                nc.scalar.copy(
+                    grouped[:].rearrange("p (t m i) -> p m i t", t=PACK, i=PACK),
+                    wa_raw[a, c][:].rearrange("p i (m t) -> p m i t", t=PACK),
+                )
             codes = kept([P, PASS], U32, "wa_codes%d%d" % (a, c))
             scales = kept([P, PASS], U8, "wa_scales%d%d" % (a, c))
             nc.vector.quantize_mx(out=codes[:].bitcast(FP8X4), scales=scales[:], in_=grouped[:])
@@ -151,20 +166,24 @@ def tile_list_speaker_affine_flow_kernel(
             offsets = idx[:, j0 // 16 : (j0 + width) // 16]
             nc.vector.tensor_copy(g[:, t, j0 : j0 + width], g_window[a, t][:].indirect(offsets))
 
-        def scaled_frames(a, t, wa_q, scaled, j0, width):
+        def speaker_scale(a, t, scaled, j0, width):
             cols = slice(j0, j0 + width)
-            r0 = a * PASS + t * P
-            b_sum = psum_b.tile([P, width], F32, name="b_sum")
+            r0 = t * P
+            words, plane = wb_half[a]
+            b_sum = psum_y.tile([P, width], F32, name="y_sum")
             nc.tensor.matmul_mx(
                 out=b_sum[:],
-                lhsT=wb_codes[:, 2 * r0 : 2 * (r0 + P)].bitcast(FP4X4),
-                lhsT_scale=wb_scales[:, r0 : r0 + P],
+                lhsT=words[:, 2 * r0 : 2 * (r0 + P)].bitcast(FP4X4),
+                lhsT_scale=plane[:, r0 : r0 + P],
                 rhs=v2_codes[:, cols].bitcast(FP8X4),
                 rhs_scale=v2_scales[:, cols],
                 start=True,
                 stop=True,
             )
             nc.scalar.activation(scaled[:, t, cols], b_sum[:], ACT.Exp)
+
+        def scaled_frames(a, t, wa_q, scaled, j0, width):
+            cols = slice(j0, j0 + width)
             a_sum = psum_a.tile([P, width], F32, name="a_sum")
             for c in range(K // PASS):
                 codes, scales = wa_q[c]
@@ -179,8 +198,20 @@ def tile_list_speaker_affine_flow_kernel(
                 )
             nc.vector.tensor_tensor(scaled[:, t, cols], a_sum[:], scaled[:, t, cols], ALU.mult)
 
-        def add_shift(scaled, g, j0, width):
-            h = stage.tile([P, width * PACK], BF16, name="h", align_bytes=64)
+        def add_shift(t, scaled, g, h_t, j0, width):
+            blocks = width // P
+            total = psum_h.tile([P, blocks, P], F32, name="total")
+            for jt in range(blocks):
+                cols = slice(j0 + jt * P, j0 + (jt + 1) * P)
+                nc.tensor.matmul(total[:, jt, :], g[:, t, cols], identity[:], start=True, stop=False, is_transpose=True)
+                nc.tensor.matmul(total[:, jt, :], scaled[:, t, cols], identity[:], start=False, stop=True, is_transpose=True)
+            nc.scalar.copy(
+                h_t[:, :, j0 // P : j0 // P + blocks, 64 * t : 64 * (t + 1)].rearrange("j u b (p e) -> j u b p e", e=2),
+                total[:].rearrange("j b (p u e) -> j u b p e", u=2, e=2),
+            )
+
+        def add_interleaved(scaled, g, j0, width):
+            h = stage.tile([P, width * PACK], BF16, name="h", align_bytes=64, bufs=3)
             cols = slice(j0, j0 + width)
             nc.vector.tensor_tensor(
                 h[:].rearrange("p (c i t) -> p c t i", i=2, t=PACK),
@@ -188,6 +219,21 @@ def tile_list_speaker_affine_flow_kernel(
                 g[:, :, cols].rearrange("p t (c i) -> p c t i", i=2),
                 ALU.add,
             )
+            return h
+
+        def turn_back(h_t, j0, width, on_vector):
+            h = stage.tile([P, width * PACK], BF16, name="h", align_bytes=64, bufs=3)
+            words = h_t[:].bitcast(F32)
+            for b0 in range(0, width // P, 2):
+                turned = psum_a.tile([P, 2, 2, P], F32, name="a_sum")
+                for b in range(2):
+                    for u in range(2):
+                        nc.tensor.transpose(turned[:, b, u, :], words[:, u, j0 // P + b0 + b, :], identity[:])
+                copy = nc.vector.tensor_copy if on_vector else nc.scalar.copy
+                copy(
+                    h[:, b0 * P * PACK : (b0 + 2) * P * PACK].bitcast(F32).rearrange("p (b j u) -> p b j u", b=2, u=2),
+                    turned[:].rearrange("p b u j -> p b j u"),
+                )
             return h
 
         def quantise_h(a, h, j0, width):
@@ -209,35 +255,46 @@ def tile_list_speaker_affine_flow_kernel(
                         stop=(a == H // PASS - 1),
                     )
                 y = outs.tile([P, width], F32, name="y")
-                nc.scalar.activation(y[:], y_sum[:], ACT.Identity, bias=bias_sb[:, q : q + 1])
+                if j0 + width == S and q % 2 == 1:
+                    nc.vector.tensor_scalar_add(y[:], y_sum[:], bias_sb[:, q : q + 1])
+                else:
+                    nc.scalar.activation(y[:], y_sum[:], ACT.Identity, bias=bias_sb[:, q : q + 1])
                 nc.sync.dma_start(out=out[q * P : (q + 1) * P, cols], in_=y[:])
 
         g = [kept([P, PACK, S], F32, "g%d" % a) for a in range(H // PASS)]
         scaled = [kept([P, PACK, S], F32, "scaled%d" % a) for a in range(H // PASS)]
 
-        gather_g(0, 0, g[0], 0, S)
+        units = [(t, j0) for t in range(PACK) for j0 in range(0, S, BANK)]
+        h_t = kept([P, 2, S // P, 2 * P], BF16, "h_t")
         wa_q = [quantise_wa(0, c) for c in range(K // PASS)]
-        for t in range(PACK):
-            if t > 0:
-                gather_g(0, t, g[0], 0, S)
-            for j0 in range(0, S, BANK):
-                scaled_frames(0, t, wa_q, scaled[0], j0, BANK)
+        for t, j0 in units:
+            speaker_scale(0, t, scaled[0], j0, BANK)
+        for t, j0 in units:
+            scaled_frames(0, t, wa_q, scaled[0], j0, BANK)
         wa_q = [quantise_wa(1, c) for c in range(K // PASS)]
+        for t, j0 in units:
+            speaker_scale(1, t, scaled[1], j0, BANK)
+        for t in range(PACK):
+            gather_g(0, t, g[0], 0, S)
+            for j0 in range(0, S, BANK):
+                add_shift(t, scaled[0], g[0], h_t, j0, BANK)
+        for t, j0 in units:
+            scaled_frames(1, t, wa_q, scaled[1], j0, BANK)
+        first_h = [turn_back(h_t, j0, BANK, False) for j0 in range(0, S, BANK)]
         bias_t = psum_y.tile([P, P], F32, name="y_sum")
         nc.tensor.transpose(bias_t[:], bias_rows[:], identity[:])
         nc.scalar.copy(bias_sb[:], bias_t[:, 0 : N // P])
-        pending = [(0, add_shift(scaled[0], g[0], j0, BANK), j0, BANK) for j0 in range(0, S, BANK)]
+        pending = [(0, first_h[j0 // BANK], j0, BANK) for j0 in range(0, S, BANK)]
         j0 = 0
         for width in LAST_CHUNKS:
             for t in range(PACK):
                 gather_g(1, t, g[1], j0, width)
-                for a, h, h0, h_width in pending:
-                    quantise_h(a, h, h0, h_width)
-                    if a == 1:
-                        features(h0, h_width)
-                pending = []
-                scaled_frames(1, t, wa_q, scaled[1], j0, width)
-            pending = [(1, add_shift(scaled[1], g[1], j0, width), j0, width)]
+                if t == 0:
+                    for a, h, h0, h_width in pending:
+                        quantise_h(a, h, h0, h_width)
+                        if a == 1:
+                            features(h0, h_width)
+            pending = [(1, add_interleaved(scaled[1], g[1], j0, width), j0, width)]
             j0 += width
         for a, h, h0, h_width in pending:
             quantise_h(a, h, h0, h_width)

@@ -90,23 +90,23 @@ def tile_list_speaker_affine_flow_kernel(
             nc.sync.dma_start(out=window[:], in_=g_planes[a][t])
             return window
 
+        tab_window, wa_raw, g_window = {}, {}, {}
         nc.sync.dma_start(idx2[:], offs2)
         nc.sync.dma_start(idx[:], offs)
         nc.sync.dma_start(out=wb_words[:].bitcast(I32), in_=wb4_words[0].bitcast(I32))
         load_plane(nc.sync, tab2_plane, tab2_scales)
         tab2_window = load_words(tab2_words[0])
-        tab_window = [load_words(tab_words[0])]
-        load_plane(nc.sync, tab_plane, tab_scales)
-        tab_window.append(load_words(tab_words[1]))
         load_plane(nc.sync, wb_plane, wb4_scales)
-        wa_raw, g_window = {}, {}
         wa_raw[0, 0] = load_wa(0, 0)
+        load_plane(nc.sync, tab_plane, tab_scales)
+        tab_window[0] = load_words(tab_words[0])
         wa_raw[0, 1] = load_wa(0, 1)
+        tab_window[1] = load_words(tab_words[1])
         g_window[0, 0] = load_g(0, 0)
         g_window[0, 1] = load_g(0, 1)
         wa_raw[1, 0] = load_wa(1, 0)
-        wa_raw[1, 1] = load_wa(1, 1)
         g_window[0, 2] = load_g(0, 2)
+        wa_raw[1, 1] = load_wa(1, 1)
         g_window[0, 3] = load_g(0, 3)
         g_window[1, 0] = load_g(1, 0)
         g_window[1, 1] = load_g(1, 1)
@@ -145,18 +145,21 @@ def tile_list_speaker_affine_flow_kernel(
         h_codes = [kept([P, S], U32, "h_codes%d" % a) for a in range(H // PASS)]
         h_scales = [kept([P, S], U8, "h_scales%d" % a) for a in range(H // PASS)]
 
-        def quantise_wa(a, c):
+        def round_wa(a, c):
             grouped = stage.tile([P, PASS * PACK], BF16, name="wa_grouped", align_bytes=64)
             if a == 0:
                 nc.scalar.copy(
-                    grouped[:].rearrange("p (m e i) -> p m i e", e=2, i=PACK),
-                    wa_raw[a, c][:].rearrange("p i (m e) -> p m i e", e=2),
+                    grouped[:].rearrange("p (m e i) -> p m i e", e=4, i=PACK),
+                    wa_raw[a, c][:].rearrange("p i (m e) -> p m i e", e=4),
                 )
             else:
                 nc.scalar.copy(
                     grouped[:].rearrange("p (t m i) -> p m i t", t=PACK, i=PACK),
                     wa_raw[a, c][:].rearrange("p i (m t) -> p m i t", t=PACK),
                 )
+            return grouped
+
+        def quantise_wa(a, c, grouped):
             codes = kept([P, PASS], U32, "wa_codes%d%d" % (a, c))
             scales = kept([P, PASS], U8, "wa_scales%d%d" % (a, c))
             nc.vector.quantize_mx(out=codes[:].bitcast(FP8X4), scales=scales[:], in_=grouped[:])
@@ -266,20 +269,35 @@ def tile_list_speaker_affine_flow_kernel(
 
         units = [(t, j0) for t in range(PACK) for j0 in range(0, S, BANK)]
         h_t = kept([P, 2, S // P, 2 * P], BF16, "h_t")
-        wa_q = [quantise_wa(0, c) for c in range(K // PASS)]
+        wa_q = [[], []]
         for t, j0 in units:
             speaker_scale(0, t, scaled[0], j0, BANK)
+        r00 = round_wa(0, 0)
+        r01 = round_wa(0, 1)
+        wa_q[0].append(quantise_wa(0, 0, r00))
+        gather_g(0, 0, g[0], 0, S)
+        wa_q[0].append(quantise_wa(0, 1, r01))
+        gather_g(0, 1, g[0], 0, S)
         for t, j0 in units:
-            scaled_frames(0, t, wa_q, scaled[0], j0, BANK)
-        wa_q = [quantise_wa(1, c) for c in range(K // PASS)]
+            scaled_frames(0, t, wa_q[0], scaled[0], j0, BANK)
+        for j0 in range(0, S, BANK):
+            add_shift(0, scaled[0], g[0], h_t, j0, BANK)
+        for j0 in range(0, S, BANK):
+            add_shift(1, scaled[0], g[0], h_t, j0, BANK)
+        r10 = round_wa(1, 0)
+        r11 = round_wa(1, 1)
         for t, j0 in units:
             speaker_scale(1, t, scaled[1], j0, BANK)
-        for t in range(PACK):
-            gather_g(0, t, g[0], 0, S)
-            for j0 in range(0, S, BANK):
-                add_shift(t, scaled[0], g[0], h_t, j0, BANK)
+        gather_g(0, 2, g[0], 0, S)
+        for j0 in range(0, S, BANK):
+            add_shift(2, scaled[0], g[0], h_t, j0, BANK)
+        gather_g(0, 3, g[0], 0, S)
+        for j0 in range(0, S, BANK):
+            add_shift(3, scaled[0], g[0], h_t, j0, BANK)
+        wa_q[1].append(quantise_wa(1, 0, r10))
+        wa_q[1].append(quantise_wa(1, 1, r11))
         for t, j0 in units:
-            scaled_frames(1, t, wa_q, scaled[1], j0, BANK)
+            scaled_frames(1, t, wa_q[1], scaled[1], j0, BANK)
         first_h = [turn_back(h_t, j0, BANK, False) for j0 in range(0, S, BANK)]
         bias_t = psum_y.tile([P, P], F32, name="y_sum")
         nc.tensor.transpose(bias_t[:], bias_rows[:], identity[:])

@@ -21,7 +21,8 @@ P = 128
 PACK = 4
 PASS = P * PACK
 BANK = 512
-RING = 9
+RING = 10
+ADD_WIDTH = 512
 LAST_CHUNKS = (512, 256, 256)
 
 
@@ -35,9 +36,8 @@ def tile_list_speaker_affine_flow_kernel(
         ring = ctx.enter_context(tc.tile_pool(name="ring", bufs=RING))
         stage = ctx.enter_context(tc.tile_pool(name="stage", bufs=2))
         outs = ctx.enter_context(tc.tile_pool(name="outs", bufs=6))
-        psum_a = ctx.enter_context(tc.psum_pool(name="psum_a", bufs=3))
-        psum_y = ctx.enter_context(tc.psum_pool(name="psum_y", bufs=3))
-        psum_h = ctx.enter_context(tc.psum_pool(name="psum_h", bufs=2))
+        psum_a = ctx.enter_context(tc.psum_pool(name="psum_a", bufs=4))
+        psum_y = ctx.enter_context(tc.psum_pool(name="psum_y", bufs=4))
 
         def kept(shape, dtype, name):
             return keep.tile(shape, dtype, name=name, align_bytes=64)
@@ -80,14 +80,11 @@ def tile_list_speaker_affine_flow_kernel(
             nc.sync.dma_start(out=raw[:], in_=rows.rearrange("(p i) r -> p i r", i=PACK))
             return raw
 
-        g_planes = [
-            gT[0:PASS, :].rearrange("(t p) c -> t p c", p=P),
-            gT[PASS : 2 * PASS, :].rearrange("(p t) c -> t p c", t=PACK),
-        ]
+        g_planes = gT.rearrange("(a p t) c -> a t p c", p=P, t=PACK)
 
         def load_g(a, t):
             window = ring.tile([P, T], F32, name="ring")
-            nc.sync.dma_start(out=window[:], in_=g_planes[a][t])
+            nc.sync.dma_start(out=window[:], in_=g_planes[a, t])
             return window
 
         tab_window, wa_raw, g_window = {}, {}, {}
@@ -96,12 +93,12 @@ def tile_list_speaker_affine_flow_kernel(
         nc.sync.dma_start(out=wb_words[:].bitcast(I32), in_=wb4_words[0].bitcast(I32))
         load_plane(nc.sync, tab2_plane, tab2_scales)
         tab2_window = load_words(tab2_words[0])
+        tab_window[0] = load_words(tab_words[0])
+        load_plane(nc.sync, tab_plane, tab_scales)
+        tab_window[1] = load_words(tab_words[1])
         load_plane(nc.sync, wb_plane, wb4_scales)
         wa_raw[0, 0] = load_wa(0, 0)
-        load_plane(nc.sync, tab_plane, tab_scales)
-        tab_window[0] = load_words(tab_words[0])
         wa_raw[0, 1] = load_wa(0, 1)
-        tab_window[1] = load_words(tab_words[1])
         g_window[0, 0] = load_g(0, 0)
         g_window[0, 1] = load_g(0, 1)
         wa_raw[1, 0] = load_wa(1, 0)
@@ -123,43 +120,32 @@ def tile_list_speaker_affine_flow_kernel(
         v2_codes = kept([P, S], U32, "v2_codes")
         v_scales = kept([P, S], U8, "v_scales")
         v_codes = [kept([P, S], U32, "v_codes%d" % c) for c in range(K // PASS)]
+        wb_scales = kept([P, H], U8, "wb_scales")
+        wb_codes = kept([P, 2 * H], U8, "wb_codes")
 
         nc.vector.tensor_copy(v2_scales[:], tab2_plane[:].indirect(idx2[:]))
         nc.vector.tensor_copy(v2_codes[:], tab2_window[:].indirect(idx2[:]))
         nc.vector.tensor_copy(v_scales[:], tab_plane[:].indirect(idx[:]))
         nc.vector.tensor_copy(v_codes[0][:], tab_window[0][:].indirect(idx[:]))
         nc.vector.tensor_copy(v_codes[1][:], tab_window[1][:].indirect(idx[:]))
-
-        wb_codes = kept([P, 2 * PASS], U8, "wb_codes")
-        wb_scales = kept([P, PASS], U8, "wb_scales")
         nc.vector.tensor_copy(
-            wb_codes[:].bitcast(U16).rearrange("p (t m) -> p t m", t=PACK),
-            wb_words[:, 2 * PASS :].bitcast(U16).rearrange("p (m t) -> p t m", t=PACK),
+            wb_codes[:].bitcast(U16).rearrange("p (a t m) -> p a t m", t=PACK, m=P),
+            wb_words[:].bitcast(U16).rearrange("p (a m t) -> p a t m", t=PACK, m=P),
         )
         nc.vector.tensor_copy(
-            wb_scales[:].rearrange("p (t m) -> p t m", t=PACK),
-            wb_plane[:, PASS:].rearrange("p (m t) -> p t m", t=PACK),
+            wb_scales[:].rearrange("p (a t m) -> p a t m", t=PACK, m=P),
+            wb_plane[:].rearrange("p (a m t) -> p a t m", t=PACK, m=P),
         )
-        wb_half = [(wb_words, wb_plane), (wb_codes, wb_scales)]
 
         h_codes = [kept([P, S], U32, "h_codes%d" % a) for a in range(H // PASS)]
         h_scales = [kept([P, S], U8, "h_scales%d" % a) for a in range(H // PASS)]
 
-        def round_wa(a, c):
+        def quantise_wa(a, c):
             grouped = stage.tile([P, PASS * PACK], BF16, name="wa_grouped", align_bytes=64)
-            if a == 0:
-                nc.scalar.copy(
-                    grouped[:].rearrange("p (m e i) -> p m i e", e=4, i=PACK),
-                    wa_raw[a, c][:].rearrange("p i (m e) -> p m i e", e=4),
-                )
-            else:
-                nc.scalar.copy(
-                    grouped[:].rearrange("p (t m i) -> p m i t", t=PACK, i=PACK),
-                    wa_raw[a, c][:].rearrange("p i (m t) -> p m i t", t=PACK),
-                )
-            return grouped
-
-        def quantise_wa(a, c, grouped):
+            nc.scalar.copy(
+                grouped[:].rearrange("p (t m i) -> p m i t", t=PACK, i=PACK),
+                wa_raw[a, c][:].rearrange("p i (m t) -> p m i t", t=PACK),
+            )
             codes = kept([P, PASS], U32, "wa_codes%d%d" % (a, c))
             scales = kept([P, PASS], U8, "wa_scales%d%d" % (a, c))
             nc.vector.quantize_mx(out=codes[:].bitcast(FP8X4), scales=scales[:], in_=grouped[:])
@@ -171,13 +157,12 @@ def tile_list_speaker_affine_flow_kernel(
 
         def speaker_scale(a, t, scaled, j0, width):
             cols = slice(j0, j0 + width)
-            r0 = t * P
-            words, plane = wb_half[a]
+            r0 = a * PASS + t * P
             b_sum = psum_y.tile([P, width], F32, name="y_sum")
             nc.tensor.matmul_mx(
                 out=b_sum[:],
-                lhsT=words[:, 2 * r0 : 2 * (r0 + P)].bitcast(FP4X4),
-                lhsT_scale=plane[:, r0 : r0 + P],
+                lhsT=wb_codes[:, 2 * r0 : 2 * (r0 + P)].bitcast(FP4X4),
+                lhsT_scale=wb_scales[:, r0 : r0 + P],
                 rhs=v2_codes[:, cols].bitcast(FP8X4),
                 rhs_scale=v2_scales[:, cols],
                 start=True,
@@ -199,21 +184,22 @@ def tile_list_speaker_affine_flow_kernel(
                     start=(c == 0),
                     stop=(c == K // PASS - 1),
                 )
-            nc.vector.tensor_tensor(scaled[:, t, cols], a_sum[:], scaled[:, t, cols], ALU.mult)
+            nc.vector.tensor_tensor(scaled[:, t, cols], scaled[:, t, cols], a_sum[:], ALU.mult)
 
-        def add_shift(t, scaled, g, h_t, j0, width):
-            blocks = width // P
-            total = psum_h.tile([P, blocks, P], F32, name="total")
-            for jt in range(blocks):
-                cols = slice(j0 + jt * P, j0 + (jt + 1) * P)
-                nc.tensor.matmul(total[:, jt, :], g[:, t, cols], identity[:], start=True, stop=False, is_transpose=True)
-                nc.tensor.matmul(total[:, jt, :], scaled[:, t, cols], identity[:], start=False, stop=True, is_transpose=True)
+        def add_plane(t, scaled, g, j0, width):
+            for s0 in range(j0, j0 + width, ADD_WIDTH):
+                cols = slice(s0, min(s0 + ADD_WIDTH, j0 + width))
+                nc.gpsimd.tensor_tensor(scaled[:, t, cols], scaled[:, t, cols], g[:, t, cols], ALU.add)
+
+        def round_h(scaled, j0, width):
+            h = stage.tile([P, width * PACK], BF16, name="h", align_bytes=64, bufs=3)
             nc.scalar.copy(
-                h_t[:, :, j0 // P : j0 // P + blocks, 64 * t : 64 * (t + 1)].rearrange("j u b (p e) -> j u b p e", e=2),
-                total[:].rearrange("j b (p u e) -> j u b p e", u=2, e=2),
+                h[:].rearrange("p (c i t) -> p c t i", i=4, t=PACK),
+                scaled[:, :, j0 : j0 + width].rearrange("p t (c i) -> p c t i", i=4),
             )
+            return h
 
-        def add_interleaved(scaled, g, j0, width):
+        def add_and_round(scaled, g, j0, width):
             h = stage.tile([P, width * PACK], BF16, name="h", align_bytes=64, bufs=3)
             cols = slice(j0, j0 + width)
             nc.vector.tensor_tensor(
@@ -222,21 +208,6 @@ def tile_list_speaker_affine_flow_kernel(
                 g[:, :, cols].rearrange("p t (c i) -> p c t i", i=2),
                 ALU.add,
             )
-            return h
-
-        def turn_back(h_t, j0, width, on_vector):
-            h = stage.tile([P, width * PACK], BF16, name="h", align_bytes=64, bufs=3)
-            words = h_t[:].bitcast(F32)
-            for b0 in range(0, width // P, 2):
-                turned = psum_a.tile([P, 2, 2, P], F32, name="a_sum")
-                for b in range(2):
-                    for u in range(2):
-                        nc.tensor.transpose(turned[:, b, u, :], words[:, u, j0 // P + b0 + b, :], identity[:])
-                copy = nc.vector.tensor_copy if on_vector else nc.scalar.copy
-                copy(
-                    h[:, b0 * P * PACK : (b0 + 2) * P * PACK].bitcast(F32).rearrange("p (b j u) -> p b j u", b=2, u=2),
-                    turned[:].rearrange("p b u j -> p b j u"),
-                )
             return h
 
         def quantise_h(a, h, j0, width):
@@ -267,53 +238,50 @@ def tile_list_speaker_affine_flow_kernel(
         g = [kept([P, PACK, S], F32, "g%d" % a) for a in range(H // PASS)]
         scaled = [kept([P, PACK, S], F32, "scaled%d" % a) for a in range(H // PASS)]
 
-        units = [(t, j0) for t in range(PACK) for j0 in range(0, S, BANK)]
-        h_t = kept([P, 2, S // P, 2 * P], BF16, "h_t")
-        wa_q = [[], []]
-        for t, j0 in units:
-            speaker_scale(0, t, scaled[0], j0, BANK)
-        r00 = round_wa(0, 0)
-        r01 = round_wa(0, 1)
-        wa_q[0].append(quantise_wa(0, 0, r00))
-        gather_g(0, 0, g[0], 0, S)
-        wa_q[0].append(quantise_wa(0, 1, r01))
-        gather_g(0, 1, g[0], 0, S)
-        for t, j0 in units:
-            scaled_frames(0, t, wa_q[0], scaled[0], j0, BANK)
+        def first_half(wa_q, j0):
+            for t in range(PACK):
+                scaled_frames(0, t, wa_q, scaled[0], j0, BANK)
+            for t in range(PACK):
+                gather_g(0, t, g[0], j0, BANK)
+                add_plane(t, scaled[0], g[0], j0, BANK)
+
+        def second_half(j0, width):
+            for t in range(PACK):
+                gather_g(1, t, g[1], j0, width)
+                add_plane(t, scaled[1], g[1], j0, width)
+
+        wa_q0 = [quantise_wa(0, c) for c in range(K // PASS)]
         for j0 in range(0, S, BANK):
-            add_shift(0, scaled[0], g[0], h_t, j0, BANK)
+            for t in range(PACK):
+                speaker_scale(0, t, scaled[0], j0, BANK)
+        first_half(wa_q0, 0)
+        wa_q1 = [quantise_wa(1, c) for c in range(K // PASS)]
         for j0 in range(0, S, BANK):
-            add_shift(1, scaled[0], g[0], h_t, j0, BANK)
-        r10 = round_wa(1, 0)
-        r11 = round_wa(1, 1)
-        for t, j0 in units:
-            speaker_scale(1, t, scaled[1], j0, BANK)
-        gather_g(0, 2, g[0], 0, S)
-        for j0 in range(0, S, BANK):
-            add_shift(2, scaled[0], g[0], h_t, j0, BANK)
-        gather_g(0, 3, g[0], 0, S)
-        for j0 in range(0, S, BANK):
-            add_shift(3, scaled[0], g[0], h_t, j0, BANK)
-        wa_q[1].append(quantise_wa(1, 0, r10))
-        wa_q[1].append(quantise_wa(1, 1, r11))
-        for t, j0 in units:
-            scaled_frames(1, t, wa_q[1], scaled[1], j0, BANK)
-        first_h = [turn_back(h_t, j0, BANK, False) for j0 in range(0, S, BANK)]
+            for t in range(PACK):
+                speaker_scale(1, t, scaled[1], j0, BANK)
+        for t in range(PACK):
+            scaled_frames(1, t, wa_q1, scaled[1], 0, BANK)
         bias_t = psum_y.tile([P, P], F32, name="y_sum")
         nc.tensor.transpose(bias_t[:], bias_rows[:], identity[:])
         nc.scalar.copy(bias_sb[:], bias_t[:, 0 : N // P])
-        pending = [(0, first_h[j0 // BANK], j0, BANK) for j0 in range(0, S, BANK)]
-        j0 = 0
-        for width in LAST_CHUNKS:
-            for t in range(PACK):
-                gather_g(1, t, g[1], j0, width)
-                if t == 0:
-                    for a, h, h0, h_width in pending:
-                        quantise_h(a, h, h0, h_width)
-                        if a == 1:
-                            features(h0, h_width)
-            pending = [(1, add_interleaved(scaled[1], g[1], j0, width), j0, width)]
-            j0 += width
-        for a, h, h0, h_width in pending:
-            quantise_h(a, h, h0, h_width)
-            features(h0, h_width)
+        h00 = round_h(scaled[0], 0, BANK)
+        second_half(0, BANK)
+        quantise_h(0, h00, 0, BANK)
+        h10 = round_h(scaled[1], 0, BANK)
+        quantise_h(1, h10, 0, BANK)
+        features(0, BANK)
+        first_half(wa_q0, BANK)
+        for t in range(PACK):
+            scaled_frames(1, t, wa_q1, scaled[1], BANK, BANK)
+        h01 = round_h(scaled[0], BANK, BANK)
+        second_half(BANK, 256)
+        quantise_h(0, h01, BANK, BANK)
+        h11 = round_h(scaled[1], BANK, 256)
+        for t in range(PACK):
+            gather_g(1, t, g[1], 768, 256)
+            if t == 1:
+                quantise_h(1, h11, BANK, 256)
+                features(BANK, 256)
+        h12 = add_and_round(scaled[1], g[1], 768, 256)
+        quantise_h(1, h12, 768, 256)
+        features(768, 256)

@@ -22,7 +22,6 @@ PACK = 4
 PASS = P * PACK
 BANK = 512
 RING = 10
-ADD_WIDTH = 512
 LAST_CHUNKS = (512, 256, 256)
 
 
@@ -94,27 +93,27 @@ def tile_list_speaker_affine_flow_kernel(
         load_plane(nc.sync, tab2_plane, tab2_scales)
         tab2_window = load_words(tab2_words[0])
         tab_window[0] = load_words(tab_words[0])
-        load_plane(nc.sync, tab_plane, tab_scales)
         tab_window[1] = load_words(tab_words[1])
-        load_plane(nc.sync, wb_plane, wb4_scales)
         wa_raw[0, 0] = load_wa(0, 0)
-        wa_raw[0, 1] = load_wa(0, 1)
+        load_plane(nc.sync, tab_plane, tab_scales)
         g_window[0, 0] = load_g(0, 0)
+        wa_raw[0, 1] = load_wa(0, 1)
+        load_plane(nc.sync, wb_plane, wb4_scales)
         g_window[0, 1] = load_g(0, 1)
         wa_raw[1, 0] = load_wa(1, 0)
-        g_window[0, 2] = load_g(0, 2)
         wa_raw[1, 1] = load_wa(1, 1)
+        g_window[0, 2] = load_g(0, 2)
         g_window[0, 3] = load_g(0, 3)
         g_window[1, 0] = load_g(1, 0)
         g_window[1, 1] = load_g(1, 1)
+        g_window[1, 2] = load_g(1, 2)
         nc.sync.dma_start(
             out=w8_codes[:].bitcast(I32),
             in_=w8_words.rearrange("a p n i -> p a (n i)").bitcast(I32),
         )
         load_plane(nc.sync, w8_plane, w8_scales)
-        nc.sync.dma_start(out=bias_rows[0 : N // P, :], in_=bias.rearrange("(q p) -> q p", p=P))
-        g_window[1, 2] = load_g(1, 2)
         g_window[1, 3] = load_g(1, 3)
+        nc.sync.dma_start(out=bias_rows[0 : N // P, :], in_=bias.rearrange("(q p) -> q p", p=P))
 
         v2_scales = kept([P, S], U8, "v2_scales")
         v2_codes = kept([P, S], U32, "v2_codes")
@@ -186,10 +185,9 @@ def tile_list_speaker_affine_flow_kernel(
                 )
             nc.vector.tensor_tensor(scaled[:, t, cols], scaled[:, t, cols], a_sum[:], ALU.mult)
 
-        def add_plane(t, scaled, g, j0, width):
-            for s0 in range(j0, j0 + width, ADD_WIDTH):
-                cols = slice(s0, min(s0 + ADD_WIDTH, j0 + width))
-                nc.gpsimd.tensor_tensor(scaled[:, t, cols], scaled[:, t, cols], g[:, t, cols], ALU.add)
+        def add_plane(engine, t, j0):
+            cols = slice(j0, j0 + BANK)
+            engine.tensor_tensor(scaled[0][:, t, cols], scaled[0][:, t, cols], g[0][:, t, cols], ALU.add)
 
         def round_h(scaled, j0, width):
             h = stage.tile([P, width * PACK], BF16, name="h", align_bytes=64, bufs=3)
@@ -238,50 +236,49 @@ def tile_list_speaker_affine_flow_kernel(
         g = [kept([P, PACK, S], F32, "g%d" % a) for a in range(H // PASS)]
         scaled = [kept([P, PACK, S], F32, "scaled%d" % a) for a in range(H // PASS)]
 
-        def first_half(wa_q, j0):
-            for t in range(PACK):
-                scaled_frames(0, t, wa_q, scaled[0], j0, BANK)
-            for t in range(PACK):
-                gather_g(0, t, g[0], j0, BANK)
-                add_plane(t, scaled[0], g[0], j0, BANK)
-
-        def second_half(j0, width):
-            for t in range(PACK):
-                gather_g(1, t, g[1], j0, width)
-                add_plane(t, scaled[1], g[1], j0, width)
-
-        wa_q0 = [quantise_wa(0, c) for c in range(K // PASS)]
-        for j0 in range(0, S, BANK):
-            for t in range(PACK):
-                speaker_scale(0, t, scaled[0], j0, BANK)
-        first_half(wa_q0, 0)
-        wa_q1 = [quantise_wa(1, c) for c in range(K // PASS)]
-        for j0 in range(0, S, BANK):
-            for t in range(PACK):
-                speaker_scale(1, t, scaled[1], j0, BANK)
-        for t in range(PACK):
-            scaled_frames(1, t, wa_q1, scaled[1], 0, BANK)
+        units = [(t, j0) for t in range(PACK) for j0 in range(0, S, BANK)]
+        wa_q = [quantise_wa(0, c) for c in range(K // PASS)]
+        for t, j0 in units:
+            speaker_scale(0, t, scaled[0], j0, BANK)
+        gather_g(0, 0, g[0], 0, S)
+        gather_g(0, 1, g[0], 0, S)
+        for t, j0 in units:
+            scaled_frames(0, t, wa_q, scaled[0], j0, BANK)
+        for n, (t, j0) in enumerate(units[:4]):
+            add_plane(nc.vector if n in (3,) else nc.gpsimd, t, j0)
+        wa_q = [quantise_wa(1, c) for c in range(K // PASS)]
+        for t, j0 in units:
+            speaker_scale(1, t, scaled[1], j0, BANK)
+        gather_g(0, 2, g[0], 0, S)
+        gather_g(0, 3, g[0], 0, S)
+        for t, j0 in units:
+            scaled_frames(1, t, wa_q, scaled[1], j0, BANK)
+        for n, (t, j0) in enumerate(units[4:]):
+            add_plane(nc.vector if n in () else nc.gpsimd, t, j0)
         bias_t = psum_y.tile([P, P], F32, name="y_sum")
         nc.tensor.transpose(bias_t[:], bias_rows[:], identity[:])
         nc.scalar.copy(bias_sb[:], bias_t[:, 0 : N // P])
-        h00 = round_h(scaled[0], 0, BANK)
-        second_half(0, BANK)
-        quantise_h(0, h00, 0, BANK)
-        h10 = round_h(scaled[1], 0, BANK)
-        quantise_h(1, h10, 0, BANK)
-        features(0, BANK)
-        first_half(wa_q0, BANK)
-        for t in range(PACK):
-            scaled_frames(1, t, wa_q1, scaled[1], BANK, BANK)
-        h01 = round_h(scaled[0], BANK, BANK)
-        second_half(BANK, 256)
-        quantise_h(0, h01, BANK, BANK)
-        h11 = round_h(scaled[1], BANK, 256)
-        for t in range(PACK):
-            gather_g(1, t, g[1], 768, 256)
-            if t == 1:
-                quantise_h(1, h11, BANK, 256)
-                features(BANK, 256)
-        h12 = add_and_round(scaled[1], g[1], 768, 256)
-        quantise_h(1, h12, 768, 256)
+        first_h = [round_h(scaled[0], j0, BANK) for j0 in range(0, S, BANK)]
+        gather_g(1, 0, g[1], 0, 512)
+        gather_g(1, 1, g[1], 0, 512)
+        quantise_h(0, first_h[0], 0, BANK)
+        gather_g(1, 2, g[1], 0, 512)
+        quantise_h(0, first_h[1], 512, BANK)
+        gather_g(1, 3, g[1], 0, 512)
+        gather_g(1, 0, g[1], 512, 256)
+        h0 = add_and_round(scaled[1], g[1], 0, 512)
+        gather_g(1, 1, g[1], 512, 256)
+        quantise_h(1, h0, 0, 512)
+        features(0, 512)
+        gather_g(1, 2, g[1], 512, 256)
+        gather_g(1, 3, g[1], 512, 256)
+        gather_g(1, 0, g[1], 768, 256)
+        h1 = add_and_round(scaled[1], g[1], 512, 256)
+        gather_g(1, 1, g[1], 768, 256)
+        quantise_h(1, h1, 512, 256)
+        features(512, 256)
+        gather_g(1, 2, g[1], 768, 256)
+        gather_g(1, 3, g[1], 768, 256)
+        h2 = add_and_round(scaled[1], g[1], 768, 256)
+        quantise_h(1, h2, 768, 256)
         features(768, 256)

@@ -47,7 +47,6 @@ def tile_list_speaker_affine_flow_kernel(
         tab2_plane = kept([P, T], U8, "tab2_plane")
         wb_plane = kept([P, H], U8, "wb_plane")
         w8_plane = kept([P, N], U8, "w8_plane")
-        wb_words = kept([P, 2 * H], U8, "wb_words")
         w8_codes = kept([P, H // PASS, N], U32, "w8_codes")
         bias_sb = kept([P, N // P], F32, "bias_sb")
 
@@ -87,56 +86,56 @@ def tile_list_speaker_affine_flow_kernel(
             return window
 
         tab_window, wa_raw, g_window = {}, {}, {}
+        wb_rows = wb4_words[0].bitcast(I32)
+        wb_words = [kept([P, 2 * PASS], U8, "wb_words%d" % a) for a in range(H // PASS)]
+
+        def load_wb(a):
+            nc.sync.dma_start(out=wb_words[a][:].bitcast(I32), in_=wb_rows[:, a * PASS // 2 : (a + 1) * PASS // 2])
+
         nc.sync.dma_start(idx2[:], offs2)
         nc.sync.dma_start(idx[:], offs)
-        nc.sync.dma_start(out=wb_words[:].bitcast(I32), in_=wb4_words[0].bitcast(I32))
+        load_wb(0)
         load_plane(nc.sync, tab2_plane, tab2_scales)
         tab2_window = load_words(tab2_words[0])
-        tab_window[0] = load_words(tab_words[0])
-        tab_window[1] = load_words(tab_words[1])
-        wa_raw[0, 0] = load_wa(0, 0)
         load_plane(nc.sync, tab_plane, tab_scales)
-        g_window[0, 0] = load_g(0, 0)
+        wa_raw[0, 0] = load_wa(0, 0)
+        tab_window[0] = load_words(tab_words[0])
         wa_raw[0, 1] = load_wa(0, 1)
         load_plane(nc.sync, wb_plane, wb4_scales)
-        g_window[0, 1] = load_g(0, 1)
+        tab_window[1] = load_words(tab_words[1])
+        g_window[0, 0] = load_g(0, 0)
         wa_raw[1, 0] = load_wa(1, 0)
+        g_window[0, 1] = load_g(0, 1)
         wa_raw[1, 1] = load_wa(1, 1)
+        load_wb(1)
         g_window[0, 2] = load_g(0, 2)
         g_window[0, 3] = load_g(0, 3)
-        g_window[1, 0] = load_g(1, 0)
-        g_window[1, 1] = load_g(1, 1)
-        g_window[1, 2] = load_g(1, 2)
+        for t in range(PACK):
+            g_window[1, t] = load_g(1, t)
         nc.sync.dma_start(
             out=w8_codes[:].bitcast(I32),
             in_=w8_words.rearrange("a p n i -> p a (n i)").bitcast(I32),
         )
         load_plane(nc.sync, w8_plane, w8_scales)
-        g_window[1, 3] = load_g(1, 3)
         nc.sync.dma_start(out=bias_rows[0 : N // P, :], in_=bias.rearrange("(q p) -> q p", p=P))
 
         v2_scales = kept([P, S], U8, "v2_scales")
         v2_codes = kept([P, S], U32, "v2_codes")
         v_scales = kept([P, S], U8, "v_scales")
-        v_codes = [kept([P, S], U32, "v_codes%d" % c) for c in range(K // PASS)]
+        v_codes = [[kept([P, BANK], U32, "v_codes%d%d" % (c, b)) for b in range(S // BANK)] for c in range(K // PASS)]
         wb_scales = kept([P, H], U8, "wb_scales")
-        wb_codes = kept([P, 2 * H], U8, "wb_codes")
+        wb_codes = [kept([P, 2 * PASS], U8, "wb_codes%d" % a) for a in range(H // PASS)]
 
-        nc.vector.tensor_copy(v2_scales[:], tab2_plane[:].indirect(idx2[:]))
-        nc.vector.tensor_copy(v2_codes[:], tab2_window[:].indirect(idx2[:]))
-        nc.vector.tensor_copy(v_scales[:], tab_plane[:].indirect(idx[:]))
-        nc.vector.tensor_copy(v_codes[0][:], tab_window[0][:].indirect(idx[:]))
-        nc.vector.tensor_copy(v_codes[1][:], tab_window[1][:].indirect(idx[:]))
-        nc.vector.tensor_copy(
-            wb_codes[:].bitcast(U16).rearrange("p (a t m) -> p a t m", t=PACK, m=P),
-            wb_words[:].bitcast(U16).rearrange("p (a m t) -> p a t m", t=PACK, m=P),
-        )
-        nc.vector.tensor_copy(
-            wb_scales[:].rearrange("p (a t m) -> p a t m", t=PACK, m=P),
-            wb_plane[:].rearrange("p (a m t) -> p a t m", t=PACK, m=P),
-        )
+        def offsets(tile, j0, width):
+            return tile[:, j0 // 16 : (j0 + width) // 16]
 
-        h_codes = [kept([P, S], U32, "h_codes%d" % a) for a in range(H // PASS)]
+        def permute_wb(a):
+            nc.vector.tensor_copy(
+                wb_codes[a][:].bitcast(U16).rearrange("p (t m) -> p t m", t=PACK),
+                wb_words[a][:].bitcast(U16).rearrange("p (m t) -> p t m", t=PACK),
+            )
+
+        h_codes = {}
         h_scales = [kept([P, S], U8, "h_scales%d" % a) for a in range(H // PASS)]
 
         def quantise_wa(a, c):
@@ -150,78 +149,82 @@ def tile_list_speaker_affine_flow_kernel(
             nc.vector.quantize_mx(out=codes[:].bitcast(FP8X4), scales=scales[:], in_=grouped[:])
             return codes, scales
 
-        def gather_g(a, t, g, j0, width):
-            offsets = idx[:, j0 // 16 : (j0 + width) // 16]
-            nc.vector.tensor_copy(g[:, t, j0 : j0 + width], g_window[a, t][:].indirect(offsets))
-
-        def speaker_scale(a, t, scaled, j0, width):
+        def speaker_scale(n):
+            a, t, j0, width = units[n]
             cols = slice(j0, j0 + width)
             r0 = a * PASS + t * P
             b_sum = psum_y.tile([P, width], F32, name="y_sum")
             nc.tensor.matmul_mx(
                 out=b_sum[:],
-                lhsT=wb_codes[:, 2 * r0 : 2 * (r0 + P)].bitcast(FP4X4),
+                lhsT=wb_codes[a][:, 2 * t * P : 2 * (t + 1) * P].bitcast(FP4X4),
                 lhsT_scale=wb_scales[:, r0 : r0 + P],
                 rhs=v2_codes[:, cols].bitcast(FP8X4),
                 rhs_scale=v2_scales[:, cols],
                 start=True,
                 stop=True,
             )
-            nc.scalar.activation(scaled[:, t, cols], b_sum[:], ACT.Exp)
+            scale[n] = kept([P, width], F32, "scale%d" % n)
+            nc.scalar.activation(scale[n][:], b_sum[:], ACT.Exp)
 
-        def scaled_frames(a, t, wa_q, scaled, j0, width):
+        def scaled_frames(n):
+            a, t, j0, width = units[n]
             cols = slice(j0, j0 + width)
             a_sum = psum_a.tile([P, width], F32, name="a_sum")
             for c in range(K // PASS):
-                codes, scales = wa_q[c]
+                codes, scales = wa_q[a, c]
                 nc.tensor.matmul_mx(
                     out=a_sum[:],
                     lhsT=codes[:, t * P : (t + 1) * P].bitcast(FP8X4),
                     lhsT_scale=scales[:, t * P : (t + 1) * P],
-                    rhs=v_codes[c][:, cols].bitcast(FP8X4),
+                    rhs=v_codes[c][j0 // BANK][:, j0 % BANK : j0 % BANK + width].bitcast(FP8X4),
                     rhs_scale=v_scales[4 * c :, cols],
                     start=(c == 0),
                     stop=(c == K // PASS - 1),
                 )
-            nc.vector.tensor_tensor(scaled[:, t, cols], scaled[:, t, cols], a_sum[:], ALU.mult)
+            if n <= wide:
+                scaled = products[n % len(products)][:, 0:width]
+            else:
+                half = (n - wide - 1) % 2 * (BANK // 2)
+                scaled = products[(wide - 1) % len(products)][:, half : half + width]
+            nc.vector.tensor_tensor(scaled, scale[n][:], a_sum[:], ALU.mult)
+            return scaled
 
-        def add_plane(engine, t, j0):
-            cols = slice(j0, j0 + BANK)
-            engine.tensor_tensor(scaled[0][:, t, cols], scaled[0][:, t, cols], g[0][:, t, cols], ALU.add)
-
-        def round_h(scaled, j0, width):
-            h = stage.tile([P, width * PACK], BF16, name="h", align_bytes=64, bufs=3)
-            nc.scalar.copy(
-                h[:].rearrange("p (c i t) -> p c t i", i=4, t=PACK),
-                scaled[:, :, j0 : j0 + width].rearrange("p t (c i) -> p c t i", i=4),
-            )
-            return h
-
-        def add_and_round(scaled, g, j0, width):
-            h = stage.tile([P, width * PACK], BF16, name="h", align_bytes=64, bufs=3)
-            cols = slice(j0, j0 + width)
+        def shift(a, t, j0, width, scaled):
             nc.vector.tensor_tensor(
-                h[:].rearrange("p (c i t) -> p c t i", i=2, t=PACK),
-                scaled[:, :, cols].rearrange("p t (c i) -> p c t i", i=2),
-                g[:, :, cols].rearrange("p t (c i) -> p c t i", i=2),
-                ALU.add,
+                h_wide[a, j0][:, t, :], g_window[a, t][:].indirect(offsets(idx, j0, width)), scaled, ALU.add
+            )
+
+        def round_h(a, j0, width):
+            if (a, j0) == (1, 0):
+                h = kept([P, width * PACK], BF16, "late")
+                h_wide[1, last_starts[2]] = kept([P, PACK, LAST_CHUNKS[2]], F32, "late")
+            else:
+                h = stage.tile([P, width * PACK], BF16, name="h", align_bytes=64, bufs=3)
+            copy = nc.vector.tensor_copy if (a, j0 + width) == (1, S) else nc.scalar.copy
+            copy(
+                h[:].rearrange("p (c i t) -> p c t i", i=4, t=PACK),
+                h_wide[a, j0][:].rearrange("p t (c i) -> p c t i", i=4),
             )
             return h
 
         def quantise_h(a, h, j0, width):
             cols = slice(j0, j0 + width)
-            nc.vector.quantize_mx(out=h_codes[a][:, cols].bitcast(FP8X4), scales=h_scales[a][:, cols], in_=h[:])
+            name = "scale%d" % wide if (a, j0) == (0, BANK) else "h_codes%d_%d" % (a, j0)
+            h_codes[a, j0] = kept([P, width], U32, name)
+            nc.vector.quantize_mx(out=h_codes[a, j0][:].bitcast(FP8X4), scales=h_scales[a][:, cols], in_=h[:])
 
         def features(j0, width):
             cols = slice(j0, j0 + width)
             for q in range(N // P):
                 y_sum = psum_y.tile([P, width], F32, name="y_sum")
                 for a in range(H // PASS):
+                    base = j0 if a == 1 else j0 // BANK * BANK
+                    codes = h_codes[a, base][:, j0 - base : j0 - base + width]
                     nc.tensor.matmul_mx(
                         out=y_sum[:],
                         lhsT=w8_codes[:, a, q * P : (q + 1) * P].bitcast(FP8X4),
                         lhsT_scale=w8_plane[4 * a :, q * P : (q + 1) * P],
-                        rhs=h_codes[a][:, cols].bitcast(FP8X4),
+                        rhs=codes.bitcast(FP8X4),
                         rhs_scale=h_scales[a][:, cols],
                         start=(a == 0),
                         stop=(a == H // PASS - 1),
@@ -233,52 +236,62 @@ def tile_list_speaker_affine_flow_kernel(
                     nc.scalar.activation(y[:], y_sum[:], ACT.Identity, bias=bias_sb[:, q : q + 1])
                 nc.sync.dma_start(out=out[q * P : (q + 1) * P, cols], in_=y[:])
 
-        g = [kept([P, PACK, S], F32, "g%d" % a) for a in range(H // PASS)]
-        scaled = [kept([P, PACK, S], F32, "scaled%d" % a) for a in range(H // PASS)]
+        scale = {}
+        last_starts = [sum(LAST_CHUNKS[:n]) for n in range(len(LAST_CHUNKS))]
+        h_wide = {}
+        for j0 in range(0, S, BANK):
+            h_wide[0, j0] = kept([P, PACK, BANK], F32, "h_wide0_%d" % j0)
+        for j0, width in list(zip(last_starts, LAST_CHUNKS))[:2]:
+            h_wide[1, j0] = kept([P, PACK, width], F32, "h_wide1_%d" % j0)
 
-        units = [(t, j0) for t in range(PACK) for j0 in range(0, S, BANK)]
-        wa_q = [quantise_wa(0, c) for c in range(K // PASS)]
-        for t, j0 in units:
-            speaker_scale(0, t, scaled[0], j0, BANK)
-        gather_g(0, 0, g[0], 0, S)
-        gather_g(0, 1, g[0], 0, S)
-        for t, j0 in units:
-            scaled_frames(0, t, wa_q, scaled[0], j0, BANK)
-        for n, (t, j0) in enumerate(units[:4]):
-            add_plane(nc.vector if n in (3,) else nc.gpsimd, t, j0)
-        wa_q = [quantise_wa(1, c) for c in range(K // PASS)]
-        for t, j0 in units:
-            speaker_scale(1, t, scaled[1], j0, BANK)
-        gather_g(0, 2, g[0], 0, S)
-        gather_g(0, 3, g[0], 0, S)
-        for t, j0 in units:
-            scaled_frames(1, t, wa_q, scaled[1], j0, BANK)
-        for n, (t, j0) in enumerate(units[4:]):
-            add_plane(nc.vector if n in () else nc.gpsimd, t, j0)
-        bias_t = psum_y.tile([P, P], F32, name="y_sum")
-        nc.tensor.transpose(bias_t[:], bias_rows[:], identity[:])
-        nc.scalar.copy(bias_sb[:], bias_t[:, 0 : N // P])
-        first_h = [round_h(scaled[0], j0, BANK) for j0 in range(0, S, BANK)]
-        gather_g(1, 0, g[1], 0, 512)
-        gather_g(1, 1, g[1], 0, 512)
-        quantise_h(0, first_h[0], 0, BANK)
-        gather_g(1, 2, g[1], 0, 512)
-        quantise_h(0, first_h[1], 512, BANK)
-        gather_g(1, 3, g[1], 0, 512)
-        gather_g(1, 0, g[1], 512, 256)
-        h0 = add_and_round(scaled[1], g[1], 0, 512)
-        gather_g(1, 1, g[1], 512, 256)
-        quantise_h(1, h0, 0, 512)
-        features(0, 512)
-        gather_g(1, 2, g[1], 512, 256)
-        gather_g(1, 3, g[1], 512, 256)
-        gather_g(1, 0, g[1], 768, 256)
-        h1 = add_and_round(scaled[1], g[1], 512, 256)
-        gather_g(1, 1, g[1], 768, 256)
-        quantise_h(1, h1, 512, 256)
-        features(512, 256)
-        gather_g(1, 2, g[1], 768, 256)
-        gather_g(1, 3, g[1], 768, 256)
-        h2 = add_and_round(scaled[1], g[1], 768, 256)
-        quantise_h(1, h2, 768, 256)
-        features(768, 256)
+        products = [kept([P, BANK], F32, "product%d" % n) for n in range(3)]
+        wa_q = {}
+        nc.vector.tensor_copy(v2_scales[:], tab2_plane[:].indirect(idx2[:]))
+        nc.vector.tensor_copy(v2_codes[:], tab2_window[:].indirect(idx2[:]))
+        nc.vector.tensor_copy(v_scales[:], tab_plane[:].indirect(idx[:]))
+        wa_q[0, 0] = quantise_wa(0, 0)
+        permute_wb(0)
+        for b in range(S // BANK):
+            nc.vector.tensor_copy(v_codes[0][b][:], tab_window[0][:].indirect(offsets(idx, b * BANK, BANK)))
+        nc.vector.tensor_copy(
+            wb_scales[:].rearrange("p (a t m) -> p a t m", t=PACK, m=P),
+            wb_plane[:].rearrange("p (a m t) -> p a t m", t=PACK, m=P),
+        )
+        wa_q[0, 1] = quantise_wa(0, 1)
+        for b in range(S // BANK):
+            nc.vector.tensor_copy(v_codes[1][b][:], tab_window[1][:].indirect(offsets(idx, b * BANK, BANK)))
+
+        first = [(0, t, j0, BANK) for t in range(PACK) for j0 in range(0, S, BANK)]
+        later = list(zip(last_starts, LAST_CHUNKS))[1:]
+        second = [(1, t, 0, LAST_CHUNKS[0]) for t in range(PACK)]
+        second += [(1, (t - 1) % PACK, j0, width) for j0, width in later for t in range(PACK)]
+        units = first + second
+        wide = len(first) + PACK
+        for n in range(len(first)):
+            speaker_scale(n)
+
+        scaled = scaled_frames(0)
+        for n, (a, t, j0, width) in enumerate(units):
+            if n + 1 == len(first):
+                for m in range(len(first), len(units)):
+                    speaker_scale(m)
+                bias_t = psum_y.tile([P, P], F32, name="y_sum")
+                nc.tensor.transpose(bias_t[:], bias_rows[:], identity[:])
+                nc.scalar.copy(bias_sb[:], bias_t[:, 0 : N // P])
+            ahead = scaled_frames(n + 1) if n + 1 < len(units) else None
+            if n + 1 == wide:
+                quantise_h(0, waiting, BANK, BANK)
+            shift(a, t, j0, width, scaled)
+            scaled = ahead
+            if (a, j0) == (0, BANK) and t in (0, 1):
+                wa_q[1, t] = quantise_wa(1, t)
+            if (a, t, j0) == (0, 1, BANK):
+                permute_wb(1)
+            if (a, j0) not in [(u[0], u[2]) for u in units[n + 1 :]]:
+                h = round_h(a, j0, width)
+                if (a, j0) == (0, BANK):
+                    waiting = h
+                else:
+                    quantise_h(a, h, j0, width)
+                if a == 1:
+                    features(j0, width)

@@ -1,7 +1,6 @@
 from contextlib import ExitStack
 
 import concourse.mybir as mybir
-from concourse.masks import make_identity
 
 K, C, H, N, T, S = 1024, 512, 1024, 512, 2048, 1024
 FLOPS = 2 * S * (K * H + C * H + H * N)
@@ -21,7 +20,7 @@ P = 128
 PACK = 4
 PASS = P * PACK
 BANK = 512
-RING = 10
+RING = 9
 LAST_CHUNKS = (512, 256, 256)
 
 
@@ -34,7 +33,6 @@ def tile_list_speaker_affine_flow_kernel(
         keep = ctx.enter_context(tc.tile_pool(name="keep", bufs=1))
         ring = ctx.enter_context(tc.tile_pool(name="ring", bufs=RING))
         stage = ctx.enter_context(tc.tile_pool(name="stage", bufs=2))
-        outs = ctx.enter_context(tc.tile_pool(name="outs", bufs=6))
         psum_a = ctx.enter_context(tc.psum_pool(name="psum_a", bufs=4))
         psum_y = ctx.enter_context(tc.psum_pool(name="psum_y", bufs=4))
 
@@ -54,10 +52,6 @@ def tile_list_speaker_affine_flow_kernel(
         nc.gpsimd.memset(tab_plane[:].bitcast(I32), 0)
         nc.gpsimd.memset(wb_plane[:].bitcast(I32), 0)
         nc.gpsimd.memset(w8_plane[:].bitcast(I32), 0)
-        bias_rows = kept([P, P], F32, "bias_rows")
-        identity = kept([P, P], F32, "identity")
-        nc.gpsimd.memset(bias_rows[:], 0.0)
-        make_identity(nc, identity[:])
 
         def load_plane(queue, plane, scales):
             rows = 4 * scales.shape[0]
@@ -67,21 +61,24 @@ def tile_list_speaker_affine_flow_kernel(
                     in_=scales[:, 4 * q : 4 * q + 4, :].bitcast(I32),
                 )
 
-        def load_words(words):
-            window = ring.tile([P, T], U32, name="ring")
+        def load_words(words, pool=ring, name="ring"):
+            window = pool.tile([P, T], U32, name=name, align_bytes=64)
             nc.sync.dma_start(out=window[:].bitcast(I32), in_=words.rearrange("p t i -> p (t i)").bitcast(I32))
             return window
 
         def load_wa(a, c):
-            raw = ring.tile([P, PACK, PASS], F32, name="ring")
+            pieces = 2 if a == 0 else 1
+            raw = ring.tile([P, pieces, PACK, PASS // pieces], F32, name="ring", align_bytes=64)
             rows = wa[c * PASS : (c + 1) * PASS, a * PASS : (a + 1) * PASS]
-            nc.sync.dma_start(out=raw[:], in_=rows.rearrange("(p i) r -> p i r", i=PACK))
+            rows = rows.rearrange("(p i) (u r) -> u p i r", i=PACK, u=pieces)
+            for u in range(pieces):
+                nc.sync.dma_start(out=raw[:, u], in_=rows[u])
             return raw
 
         g_planes = gT.rearrange("(a p t) c -> a t p c", p=P, t=PACK)
 
         def load_g(a, t):
-            window = ring.tile([P, T], F32, name="ring")
+            window = ring.tile([P, T], F32, name="ring", align_bytes=64)
             nc.sync.dma_start(out=window[:], in_=g_planes[a, t])
             return window
 
@@ -102,7 +99,7 @@ def tile_list_speaker_affine_flow_kernel(
         tab_window[0] = load_words(tab_words[0])
         wa_raw[0, 1] = load_wa(0, 1)
         load_plane(nc.sync, wb_plane, wb4_scales)
-        tab_window[1] = load_words(tab_words[1])
+        tab_window[1] = load_words(tab_words[1], keep, "last_words")
         g_window[0, 0] = load_g(0, 0)
         wa_raw[1, 0] = load_wa(1, 0)
         g_window[0, 1] = load_g(0, 1)
@@ -117,13 +114,14 @@ def tile_list_speaker_affine_flow_kernel(
             in_=w8_words.rearrange("a p n i -> p a (n i)").bitcast(I32),
         )
         load_plane(nc.sync, w8_plane, w8_scales)
-        nc.sync.dma_start(out=bias_rows[0 : N // P, :], in_=bias.rearrange("(q p) -> q p", p=P))
+        with nc.allow_non_contiguous_dma(reason="one bias value for each partition and tile of rows"):
+            nc.sync.dma_start(out=bias_sb[:], in_=bias.rearrange("(q p) -> p q", p=P))
 
         v2_scales = kept([P, S], U8, "v2_scales")
         v2_codes = kept([P, S], U32, "v2_codes")
         v_scales = kept([P, S], U8, "v_scales")
         v_codes = [[kept([P, BANK], U32, "v_codes%d%d" % (c, b)) for b in range(S // BANK)] for c in range(K // PASS)]
-        wb_scales = kept([P, H], U8, "wb_scales")
+        wb_scales = {}
         wb_codes = [kept([P, 2 * PASS], U8, "wb_codes%d" % a) for a in range(H // PASS)]
 
         def offsets(tile, j0, width):
@@ -140,10 +138,12 @@ def tile_list_speaker_affine_flow_kernel(
 
         def quantise_wa(a, c):
             grouped = stage.tile([P, PASS * PACK], BF16, name="wa_grouped", align_bytes=64)
-            nc.scalar.copy(
-                grouped[:].rearrange("p (t m i) -> p m i t", t=PACK, i=PACK),
-                wa_raw[a, c][:].rearrange("p i (m t) -> p m i t", t=PACK),
-            )
+            pieces = wa_raw[a, c].shape[1]
+            for u in range(pieces):
+                nc.scalar.copy(
+                    grouped[:].rearrange("p (t u m i) -> p u m i t", t=PACK, u=pieces, i=PACK)[:, u],
+                    wa_raw[a, c][:, u].rearrange("p i (m t) -> p m i t", t=PACK),
+                )
             codes = kept([P, PASS], U32, "wa_codes%d%d" % (a, c))
             scales = kept([P, PASS], U8, "wa_scales%d%d" % (a, c))
             nc.vector.quantize_mx(out=codes[:].bitcast(FP8X4), scales=scales[:], in_=grouped[:])
@@ -152,12 +152,11 @@ def tile_list_speaker_affine_flow_kernel(
         def speaker_scale(n):
             a, t, j0, width = units[n]
             cols = slice(j0, j0 + width)
-            r0 = a * PASS + t * P
             b_sum = psum_y.tile([P, width], F32, name="y_sum")
             nc.tensor.matmul_mx(
                 out=b_sum[:],
                 lhsT=wb_codes[a][:, 2 * t * P : 2 * (t + 1) * P].bitcast(FP4X4),
-                lhsT_scale=wb_scales[:, r0 : r0 + P],
+                lhsT_scale=wb_scales[a, t],
                 rhs=v2_codes[:, cols].bitcast(FP8X4),
                 rhs_scale=v2_scales[:, cols],
                 start=True,
@@ -181,11 +180,13 @@ def tile_list_speaker_affine_flow_kernel(
                     start=(c == 0),
                     stop=(c == K // PASS - 1),
                 )
+            half = (n - wide - 1) % 2 * (BANK // 2)
             if n <= wide:
                 scaled = products[n % len(products)][:, 0:width]
-            else:
-                half = (n - wide - 1) % 2 * (BANK // 2)
+            elif n < wide + PACK:
                 scaled = products[(wide - 1) % len(products)][:, half : half + width]
+            else:
+                scaled = last_products[0][:, half : half + width]
             nc.vector.tensor_tensor(scaled, scale[n][:], a_sum[:], ALU.mult)
             return scaled
 
@@ -197,9 +198,9 @@ def tile_list_speaker_affine_flow_kernel(
         def round_h(a, j0, width):
             if (a, j0) == (1, 0):
                 h = kept([P, width * PACK], BF16, "late")
-                h_wide[1, last_starts[2]] = kept([P, PACK, LAST_CHUNKS[2]], F32, "late")
+                last_products.append(kept([P, BANK], F32, "late"))
             else:
-                h = stage.tile([P, width * PACK], BF16, name="h", align_bytes=64, bufs=3)
+                h = stage.tile([P, width * PACK], BF16, name="h", align_bytes=64)
             copy = nc.vector.tensor_copy if (a, j0 + width) == (1, S) else nc.scalar.copy
             copy(
                 h[:].rearrange("p (c i t) -> p c t i", i=4, t=PACK),
@@ -209,14 +210,19 @@ def tile_list_speaker_affine_flow_kernel(
 
         def quantise_h(a, h, j0, width):
             cols = slice(j0, j0 + width)
-            name = "scale%d" % wide if (a, j0) == (0, BANK) else "h_codes%d_%d" % (a, j0)
+            name = "scale%d" % after[a, j0] if (a, j0) in after else "h_codes%d_%d" % (a, j0)
             h_codes[a, j0] = kept([P, width], U32, name)
             nc.vector.quantize_mx(out=h_codes[a, j0][:].bitcast(FP8X4), scales=h_scales[a][:, cols], in_=h[:])
 
         def features(j0, width):
             cols = slice(j0, j0 + width)
+            y = kept([P, N // P, width], F32, "y%d" % j0)
+            group = 1
             for q in range(N // P):
-                y_sum = psum_y.tile([P, width], F32, name="y_sum")
+                if j0 + width == S:
+                    y_sum = psum_a.tile([P, width], F32, name="a_sum")
+                else:
+                    y_sum = psum_y.tile([P, width], F32, name="y_sum")
                 for a in range(H // PASS):
                     base = j0 if a == 1 else j0 // BANK * BANK
                     codes = h_codes[a, base][:, j0 - base : j0 - base + width]
@@ -229,22 +235,24 @@ def tile_list_speaker_affine_flow_kernel(
                         start=(a == 0),
                         stop=(a == H // PASS - 1),
                     )
-                y = outs.tile([P, width], F32, name="y")
                 if j0 + width == S and q % 2 == 1:
-                    nc.vector.tensor_scalar_add(y[:], y_sum[:], bias_sb[:, q : q + 1])
+                    nc.vector.tensor_scalar_add(y[:, q], y_sum[:], bias_sb[:, q : q + 1])
                 else:
-                    nc.scalar.activation(y[:], y_sum[:], ACT.Identity, bias=bias_sb[:, q : q + 1])
-                nc.sync.dma_start(out=out[q * P : (q + 1) * P, cols], in_=y[:])
+                    nc.scalar.activation(y[:, q], y_sum[:], ACT.Identity, bias=bias_sb[:, q : q + 1])
+                if (q + 1) % group == 0:
+                    rows = slice(q + 1 - group, q + 1)
+                    nc.sync.dma_start(out=out.rearrange("(q p) j -> p q j", p=P)[:, rows, cols], in_=y[:, rows])
 
         scale = {}
         last_starts = [sum(LAST_CHUNKS[:n]) for n in range(len(LAST_CHUNKS))]
         h_wide = {}
         for j0 in range(0, S, BANK):
             h_wide[0, j0] = kept([P, PACK, BANK], F32, "h_wide0_%d" % j0)
-        for j0, width in list(zip(last_starts, LAST_CHUNKS))[:2]:
+        for j0, width in zip(last_starts, LAST_CHUNKS):
             h_wide[1, j0] = kept([P, PACK, width], F32, "h_wide1_%d" % j0)
 
         products = [kept([P, BANK], F32, "product%d" % n) for n in range(3)]
+        last_products = []
         wa_q = {}
         nc.vector.tensor_copy(v2_scales[:], tab2_plane[:].indirect(idx2[:]))
         nc.vector.tensor_copy(v2_codes[:], tab2_window[:].indirect(idx2[:]))
@@ -253,13 +261,17 @@ def tile_list_speaker_affine_flow_kernel(
         permute_wb(0)
         for b in range(S // BANK):
             nc.vector.tensor_copy(v_codes[0][b][:], tab_window[0][:].indirect(offsets(idx, b * BANK, BANK)))
-        nc.vector.tensor_copy(
-            wb_scales[:].rearrange("p (a t m) -> p a t m", t=PACK, m=P),
-            wb_plane[:].rearrange("p (a m t) -> p a t m", t=PACK, m=P),
-        )
+        slots = wb_plane[:].rearrange("p (a m t) -> p a t m", t=PACK, m=P)
+        early = kept([P, 2, PACK, P], U8, "wb_scales")
+        nc.vector.tensor_copy(early[:, 0, 0:2], slots[:, 0, 0:2])
+        nc.vector.tensor_copy(early[:, 1], slots[:, 1])
         wa_q[0, 1] = quantise_wa(0, 1)
         for b in range(S // BANK):
             nc.vector.tensor_copy(v_codes[1][b][:], tab_window[1][:].indirect(offsets(idx, b * BANK, BANK)))
+        rest = kept([P, 2, P], U8, "last_words")
+        for a in range(H // PASS):
+            for t in range(PACK):
+                wb_scales[a, t] = rest[:, t - 2] if (a, t // 2) == (0, 1) else early[:, a, t]
 
         first = [(0, t, j0, BANK) for t in range(PACK) for j0 in range(0, S, BANK)]
         later = list(zip(last_starts, LAST_CHUNKS))[1:]
@@ -267,20 +279,25 @@ def tile_list_speaker_affine_flow_kernel(
         second += [(1, (t - 1) % PACK, j0, width) for j0, width in later for t in range(PACK)]
         units = first + second
         wide = len(first) + PACK
-        for n in range(len(first)):
+        after = {(0, BANK): wide, (1, BANK): wide + PACK + 2}
+        waiting = {}
+        for n in range(len(first) // 2):
             speaker_scale(n)
 
         scaled = scaled_frames(0)
+        nc.vector.tensor_copy(rest[:], slots[:, 0, 2:4])
+        for n in range(len(first) // 2, len(first)):
+            speaker_scale(n)
         for n, (a, t, j0, width) in enumerate(units):
             if n + 1 == len(first):
                 for m in range(len(first), len(units)):
                     speaker_scale(m)
-                bias_t = psum_y.tile([P, P], F32, name="y_sum")
-                nc.tensor.transpose(bias_t[:], bias_rows[:], identity[:])
-                nc.scalar.copy(bias_sb[:], bias_t[:, 0 : N // P])
             ahead = scaled_frames(n + 1) if n + 1 < len(units) else None
-            if n + 1 == wide:
-                quantise_h(0, waiting, BANK, BANK)
+            for key in after:
+                if after[key] == n + 1:
+                    quantise_h(key[0], waiting[key][0], key[1], waiting[key][1])
+                    if key[0] == 1:
+                        features(key[1], waiting[key][1])
             shift(a, t, j0, width, scaled)
             scaled = ahead
             if (a, j0) == (0, BANK) and t in (0, 1):
@@ -289,9 +306,9 @@ def tile_list_speaker_affine_flow_kernel(
                 permute_wb(1)
             if (a, j0) not in [(u[0], u[2]) for u in units[n + 1 :]]:
                 h = round_h(a, j0, width)
-                if (a, j0) == (0, BANK):
-                    waiting = h
+                if (a, j0) in after:
+                    waiting[a, j0] = (h, width)
                 else:
                     quantise_h(a, h, j0, width)
-                if a == 1:
-                    features(j0, width)
+                    if a == 1:
+                        features(j0, width)

@@ -20,7 +20,7 @@ P = 128
 PACK = 4
 PASS = P * PACK
 BANK = 512
-RING = 9
+RING = 10
 LAST_CHUNKS = (512, 256, 256)
 
 
@@ -61,14 +61,14 @@ def tile_list_speaker_affine_flow_kernel(
                     in_=scales[:, 4 * q : 4 * q + 4, :].bitcast(I32),
                 )
 
-        def load_words(words, pool=ring, name="ring"):
-            window = pool.tile([P, T], U32, name=name, align_bytes=64)
+        def load_words(words):
+            window = ring.tile([P, T], U32, name="ring", align_bytes=64)
             nc.sync.dma_start(out=window[:].bitcast(I32), in_=words.rearrange("p t i -> p (t i)").bitcast(I32))
             return window
 
-        def load_wa(a, c):
+        def load_wa(a, c, pool=ring, name="ring"):
             pieces = 2 if a == 0 else 1
-            raw = ring.tile([P, pieces, PACK, PASS // pieces], F32, name="ring", align_bytes=64)
+            raw = pool.tile([P, pieces, PACK, PASS // pieces], F32, name=name, align_bytes=64)
             rows = wa[c * PASS : (c + 1) * PASS, a * PASS : (a + 1) * PASS]
             rows = rows.rearrange("(p i) (u r) -> u p i r", i=PACK, u=pieces)
             for u in range(pieces):
@@ -83,15 +83,10 @@ def tile_list_speaker_affine_flow_kernel(
             return window
 
         tab_window, wa_raw, g_window = {}, {}, {}
-        wb_rows = wb4_words[0].bitcast(I32)
-        wb_words = [kept([P, 2 * PASS], U8, "wb_words%d" % a) for a in range(H // PASS)]
-
-        def load_wb(a):
-            nc.sync.dma_start(out=wb_words[a][:].bitcast(I32), in_=wb_rows[:, a * PASS // 2 : (a + 1) * PASS // 2])
-
+        wb_words = kept([P, 2 * H], U8, "wb_words")
         nc.sync.dma_start(idx2[:], offs2)
         nc.sync.dma_start(idx[:], offs)
-        load_wb(0)
+        nc.sync.dma_start(out=wb_words[:].bitcast(I32), in_=wb4_words[0].bitcast(I32))
         load_plane(nc.sync, tab2_plane, tab2_scales)
         tab2_window = load_words(tab2_words[0])
         load_plane(nc.sync, tab_plane, tab_scales)
@@ -99,13 +94,12 @@ def tile_list_speaker_affine_flow_kernel(
         tab_window[0] = load_words(tab_words[0])
         wa_raw[0, 1] = load_wa(0, 1)
         load_plane(nc.sync, wb_plane, wb4_scales)
-        tab_window[1] = load_words(tab_words[1], keep, "last_words")
+        tab_window[1] = load_words(tab_words[1])
         g_window[0, 0] = load_g(0, 0)
-        wa_raw[1, 0] = load_wa(1, 0)
         g_window[0, 1] = load_g(0, 1)
-        wa_raw[1, 1] = load_wa(1, 1)
-        load_wb(1)
+        wa_raw[1, 0] = load_wa(1, 0)
         g_window[0, 2] = load_g(0, 2)
+        wa_raw[1, 1] = load_wa(1, 1, keep, "last_wa")
         g_window[0, 3] = load_g(0, 3)
         for t in range(PACK):
             g_window[1, t] = load_g(1, t)
@@ -122,16 +116,10 @@ def tile_list_speaker_affine_flow_kernel(
         v_scales = kept([P, S], U8, "v_scales")
         v_codes = [[kept([P, BANK], U32, "v_codes%d%d" % (c, b)) for b in range(S // BANK)] for c in range(K // PASS)]
         wb_scales = {}
-        wb_codes = [kept([P, 2 * PASS], U8, "wb_codes%d" % a) for a in range(H // PASS)]
+        wb_codes = kept([P, 2 * H], U8, "wb_codes")
 
         def offsets(tile, j0, width):
             return tile[:, j0 // 16 : (j0 + width) // 16]
-
-        def permute_wb(a):
-            nc.vector.tensor_copy(
-                wb_codes[a][:].bitcast(U16).rearrange("p (t m) -> p t m", t=PACK),
-                wb_words[a][:].bitcast(U16).rearrange("p (m t) -> p t m", t=PACK),
-            )
 
         h_codes = {}
         h_scales = [kept([P, S], U8, "h_scales%d" % a) for a in range(H // PASS)]
@@ -152,18 +140,22 @@ def tile_list_speaker_affine_flow_kernel(
         def speaker_scale(n):
             a, t, j0, width = units[n]
             cols = slice(j0, j0 + width)
+            r0 = a * PASS + t * P
             b_sum = psum_y.tile([P, width], F32, name="y_sum")
             nc.tensor.matmul_mx(
                 out=b_sum[:],
-                lhsT=wb_codes[a][:, 2 * t * P : 2 * (t + 1) * P].bitcast(FP4X4),
+                lhsT=wb_codes[:, 2 * r0 : 2 * (r0 + P)].bitcast(FP4X4),
                 lhsT_scale=wb_scales[a, t],
                 rhs=v2_codes[:, cols].bitcast(FP8X4),
                 rhs_scale=v2_scales[:, cols],
                 start=True,
                 stop=True,
             )
-            scale[n] = kept([P, width], F32, "scale%d" % n)
-            nc.scalar.activation(scale[n][:], b_sum[:], ACT.Exp)
+            if len(first) <= n < wide:
+                scale[n] = second_scales[0][:, t]
+            else:
+                scale[n] = kept([P, width], F32, "scale%d" % n)[:]
+            nc.scalar.activation(scale[n], b_sum[:], ACT.Exp)
 
         def scaled_frames(n):
             a, t, j0, width = units[n]
@@ -181,13 +173,15 @@ def tile_list_speaker_affine_flow_kernel(
                     stop=(c == K // PASS - 1),
                 )
             half = (n - wide - 1) % 2 * (BANK // 2)
-            if n <= wide:
+            if n < wide:
                 scaled = products[n % len(products)][:, 0:width]
+            elif n == wide:
+                scaled = kept([P, width], F32, "product_wide")[:]
             elif n < wide + PACK:
                 scaled = products[(wide - 1) % len(products)][:, half : half + width]
             else:
                 scaled = last_products[0][:, half : half + width]
-            nc.vector.tensor_tensor(scaled, scale[n][:], a_sum[:], ALU.mult)
+            nc.vector.tensor_tensor(scaled, scale[n], a_sum[:], ALU.mult)
             return scaled
 
         def shift(a, t, j0, width, scaled):
@@ -252,13 +246,16 @@ def tile_list_speaker_affine_flow_kernel(
             h_wide[1, j0] = kept([P, PACK, width], F32, "h_wide1_%d" % j0)
 
         products = [kept([P, BANK], F32, "product%d" % n) for n in range(3)]
-        last_products = []
+        last_products, second_scales = [], []
         wa_q = {}
         nc.vector.tensor_copy(v2_scales[:], tab2_plane[:].indirect(idx2[:]))
         nc.vector.tensor_copy(v2_codes[:], tab2_window[:].indirect(idx2[:]))
         nc.vector.tensor_copy(v_scales[:], tab_plane[:].indirect(idx[:]))
         wa_q[0, 0] = quantise_wa(0, 0)
-        permute_wb(0)
+        nc.vector.tensor_copy(
+            wb_codes[:].bitcast(U16).rearrange("p (a t m) -> p a t m", t=PACK, m=P),
+            wb_words[:].bitcast(U16).rearrange("p (a m t) -> p a t m", t=PACK, m=P),
+        )
         for b in range(S // BANK):
             nc.vector.tensor_copy(v_codes[0][b][:], tab_window[0][:].indirect(offsets(idx, b * BANK, BANK)))
         slots = wb_plane[:].rearrange("p (a m t) -> p a t m", t=PACK, m=P)
@@ -268,10 +265,9 @@ def tile_list_speaker_affine_flow_kernel(
         wa_q[0, 1] = quantise_wa(0, 1)
         for b in range(S // BANK):
             nc.vector.tensor_copy(v_codes[1][b][:], tab_window[1][:].indirect(offsets(idx, b * BANK, BANK)))
-        rest = kept([P, 2, P], U8, "last_words")
         for a in range(H // PASS):
             for t in range(PACK):
-                wb_scales[a, t] = rest[:, t - 2] if (a, t // 2) == (0, 1) else early[:, a, t]
+                wb_scales[a, t] = early[:, a, t]
 
         first = [(0, t, j0, BANK) for t in range(PACK) for j0 in range(0, S, BANK)]
         later = list(zip(last_starts, LAST_CHUNKS))[1:]
@@ -279,31 +275,33 @@ def tile_list_speaker_affine_flow_kernel(
         second += [(1, (t - 1) % PACK, j0, width) for j0, width in later for t in range(PACK)]
         units = first + second
         wide = len(first) + PACK
-        after = {(0, BANK): wide, (1, BANK): wide + PACK + 2}
+        after = {(0, BANK): wide + 2, (1, BANK): wide + PACK + 2}
         waiting = {}
         for n in range(len(first) // 2):
             speaker_scale(n)
 
         scaled = scaled_frames(0)
-        nc.vector.tensor_copy(rest[:], slots[:, 0, 2:4])
-        for n in range(len(first) // 2, len(first)):
-            speaker_scale(n)
         for n, (a, t, j0, width) in enumerate(units):
             if n + 1 == len(first):
+                second_scales.append(kept([P, PACK, BANK], F32, "last_wa"))
                 for m in range(len(first), len(units)):
                     speaker_scale(m)
             ahead = scaled_frames(n + 1) if n + 1 < len(units) else None
-            for key in after:
-                if after[key] == n + 1:
-                    quantise_h(key[0], waiting[key][0], key[1], waiting[key][1])
-                    if key[0] == 1:
-                        features(key[1], waiting[key][1])
+            if n == 0:
+                rest = kept([P, 2, P], U8, "scale0")
+                nc.vector.tensor_copy(rest[:], slots[:, 0, 2:4])
+                wb_scales[0, 2], wb_scales[0, 3] = rest[:, 0], rest[:, 1]
+                for m in range(len(first) // 2, len(first)):
+                    speaker_scale(m)
+            if after[1, BANK] == n + 1:
+                quantise_h(1, waiting[1, BANK][0], BANK, waiting[1, BANK][1])
+                features(BANK, waiting[1, BANK][1])
             shift(a, t, j0, width, scaled)
+            if after[0, BANK] == n:
+                quantise_h(0, waiting[0, BANK][0], BANK, BANK)
             scaled = ahead
-            if (a, j0) == (0, BANK) and t in (0, 1):
-                wa_q[1, t] = quantise_wa(1, t)
-            if (a, t, j0) == (0, 1, BANK):
-                permute_wb(1)
+            if (a, j0) == (0, BANK) and t in (1, 2):
+                wa_q[1, t - 1] = quantise_wa(1, t - 1)
             if (a, j0) not in [(u[0], u[2]) for u in units[n + 1 :]]:
                 h = round_h(a, j0, width)
                 if (a, j0) in after:

@@ -61,6 +61,13 @@ def tile_list_speaker_affine_flow_kernel(
                     in_=scales[:, 4 * q : 4 * q + 4, :].bitcast(I32),
                 )
 
+        def load_scale_rows(plane, scales, rows):
+            for r in rows:
+                for a in range(scales.shape[0]):
+                    nc.sync.dma_start(
+                        out=plane[4 * a + r : P : 32, :].bitcast(I32), in_=scales[a, r : 16 : 4, :].bitcast(I32)
+                    )
+
         def load_words(words):
             window = ring.tile([P, T], U32, name="ring", align_bytes=64)
             nc.sync.dma_start(out=window[:].bitcast(I32), in_=words.rearrange("p t i -> p (t i)").bitcast(I32))
@@ -87,10 +94,11 @@ def tile_list_speaker_affine_flow_kernel(
         nc.sync.dma_start(idx2[:], offs2)
         nc.sync.dma_start(idx[:], offs)
         nc.sync.dma_start(out=wb_words[:].bitcast(I32), in_=wb4_words[0].bitcast(I32))
-        load_plane(nc.sync, tab2_plane, tab2_scales)
+        load_scale_rows(tab2_plane, tab2_scales, range(4))
         tab2_window = load_words(tab2_words[0])
-        load_plane(nc.sync, tab_plane, tab_scales)
+        load_scale_rows(tab_plane, tab_scales, (0, 1))
         wa_raw[0, 0] = load_wa(0, 0)
+        load_scale_rows(tab_plane, tab_scales, (2, 3))
         tab_window[0] = load_words(tab_words[0])
         wa_raw[0, 1] = load_wa(0, 1)
         load_plane(nc.sync, wb_plane, wb4_scales)
@@ -177,10 +185,8 @@ def tile_list_speaker_affine_flow_kernel(
                 scaled = products[n % len(products)][:, 0:width]
             elif n == wide:
                 scaled = kept([P, width], F32, "product_wide")[:]
-            elif n < wide + PACK:
-                scaled = products[(wide - 1) % len(products)][:, half : half + width]
             else:
-                scaled = last_products[0][:, half : half + width]
+                scaled = products[(wide - 1) % len(products)][:, half : half + width]
             nc.vector.tensor_tensor(scaled, scale[n], a_sum[:], ALU.mult)
             return scaled
 
@@ -190,13 +196,8 @@ def tile_list_speaker_affine_flow_kernel(
             )
 
         def round_h(a, j0, width):
-            if (a, j0) == (1, 0):
-                h = kept([P, width * PACK], BF16, "late")
-                last_products.append(kept([P, BANK], F32, "late"))
-            else:
-                h = stage.tile([P, width * PACK], BF16, name="h", align_bytes=64)
-            copy = nc.vector.tensor_copy if (a, j0 + width) == (1, S) else nc.scalar.copy
-            copy(
+            h = stage.tile([P, width * PACK], BF16, name="h", align_bytes=64, bufs=3)
+            nc.scalar.copy(
                 h[:].rearrange("p (c i t) -> p c t i", i=4, t=PACK),
                 h_wide[a, j0][:].rearrange("p t (c i) -> p c t i", i=4),
             )
@@ -211,9 +212,9 @@ def tile_list_speaker_affine_flow_kernel(
         def features(j0, width):
             cols = slice(j0, j0 + width)
             y = kept([P, N // P, width], F32, "y%d" % j0)
-            group = 1
+            group = 1 if width == BANK else 2
             for q in range(N // P):
-                if j0 + width == S:
+                if j0 + width + P == S:
                     y_sum = psum_a.tile([P, width], F32, name="a_sum")
                 else:
                     y_sum = psum_y.tile([P, width], F32, name="y_sum")
@@ -229,7 +230,7 @@ def tile_list_speaker_affine_flow_kernel(
                         start=(a == 0),
                         stop=(a == H // PASS - 1),
                     )
-                if j0 + width == S and q % 2 == 1:
+                if width == P and q % 2 == 1:
                     nc.vector.tensor_scalar_add(y[:, q], y_sum[:], bias_sb[:, q : q + 1])
                 else:
                     nc.scalar.activation(y[:, q], y_sum[:], ACT.Identity, bias=bias_sb[:, q : q + 1])
@@ -246,7 +247,7 @@ def tile_list_speaker_affine_flow_kernel(
             h_wide[1, j0] = kept([P, PACK, width], F32, "h_wide1_%d" % j0)
 
         products = [kept([P, BANK], F32, "product%d" % n) for n in range(3)]
-        last_products, second_scales = [], []
+        second_scales = []
         wa_q = {}
         nc.vector.tensor_copy(v2_scales[:], tab2_plane[:].indirect(idx2[:]))
         nc.vector.tensor_copy(v2_codes[:], tab2_window[:].indirect(idx2[:]))
@@ -302,7 +303,7 @@ def tile_list_speaker_affine_flow_kernel(
             scaled = ahead
             if (a, j0) == (0, BANK) and t in (1, 2):
                 wa_q[1, t - 1] = quantise_wa(1, t - 1)
-            if (a, j0) not in [(u[0], u[2]) for u in units[n + 1 :]]:
+            if n + 1 < len(units) and (a, j0) not in [(u[0], u[2]) for u in units[n + 1 :]]:
                 h = round_h(a, j0, width)
                 if (a, j0) in after:
                     waiting[a, j0] = (h, width)
@@ -310,3 +311,17 @@ def tile_list_speaker_affine_flow_kernel(
                     quantise_h(a, h, j0, width)
                     if a == 1:
                         features(j0, width)
+
+        j0 = last_starts[2]
+        pieces = []
+        for c0 in range(0, LAST_CHUNKS[2], P):
+            h = kept([P, P * PACK], BF16, "h_last%d" % c0)
+            nc.vector.tensor_copy(
+                h[:].rearrange("p (c i t) -> p c t i", i=4, t=PACK),
+                h_wide[1, j0][:, :, c0 : c0 + P].rearrange("p t (c i) -> p c t i", i=4),
+            )
+            pieces.append(h)
+        for n, h in enumerate(pieces):
+            quantise_h(1, h, j0 + n * P, P)
+        for n in range(len(pieces)):
+            features(j0 + n * P, P)

@@ -20,8 +20,9 @@ P = 128
 PACK = 4
 PASS = P * PACK
 BANK = 512
-RING = 10
+RING = 9
 LAST_CHUNKS = (512, 256, 256)
+SHARED = (2, 4, 6, 10)
 
 
 def tile_list_speaker_affine_flow_kernel(
@@ -164,11 +165,10 @@ def tile_list_speaker_affine_flow_kernel(
             else:
                 scale[n] = kept([P, width], F32, "scale%d" % n)[:]
             nc.scalar.activation(scale[n], b_sum[:], ACT.Exp)
+            if n in SHARED:
+                mix_aside(n)
 
-        def scaled_frames(n):
-            a, t, j0, width = units[n]
-            cols = slice(j0, j0 + width)
-            a_sum = psum_a.tile([P, width], F32, name="a_sum")
+        def mix(a, t, j0, width, a_sum):
             for c in range(K // PASS):
                 codes, scales = wa_q[a, c]
                 nc.tensor.matmul_mx(
@@ -176,10 +176,20 @@ def tile_list_speaker_affine_flow_kernel(
                     lhsT=codes[:, t * P : (t + 1) * P].bitcast(FP8X4),
                     lhsT_scale=scales[:, t * P : (t + 1) * P],
                     rhs=v_codes[c][j0 // BANK][:, j0 % BANK : j0 % BANK + width].bitcast(FP8X4),
-                    rhs_scale=v_scales[4 * c :, cols],
+                    rhs_scale=v_scales[4 * c :, j0 : j0 + width],
                     start=(c == 0),
                     stop=(c == K // PASS - 1),
                 )
+
+        def mix_aside(n):
+            a, t, j0, width = units[n]
+            a_sum = psum_y.tile([P, width // 2], F32, name="y_sum")
+            mix(a, t, j0 + width // 2, width // 2, a_sum)
+            mixed[n] = kept([P, width // 2], F32, "mixed%d" % n)
+            nc.scalar.copy(mixed[n][:], a_sum[:])
+
+        def scaled_frames(n):
+            a, t, j0, width = units[n]
             half = (n - wide - 1) % 2 * (BANK // 2)
             if n < wide:
                 scaled = products[n % len(products)][:, 0:width]
@@ -187,7 +197,12 @@ def tile_list_speaker_affine_flow_kernel(
                 scaled = kept([P, width], F32, "product_wide")[:]
             else:
                 scaled = products[(wide - 1) % len(products)][:, half : half + width]
-            nc.vector.tensor_tensor(scaled, scale[n], a_sum[:], ALU.mult)
+            own = width // 2 if n in SHARED else width
+            a_sum = psum_a.tile([P, own], F32, name="a_sum")
+            mix(a, t, j0, own, a_sum)
+            nc.vector.tensor_tensor(scaled[:, 0:own], scale[n][:, 0:own], a_sum[:], ALU.mult)
+            if own < width:
+                nc.gpsimd.tensor_tensor(scaled[:, own:], scale[n][:, own:], mixed[n][:], ALU.mult)
             return scaled
 
         def shift(a, t, j0, width, scaled):
@@ -238,7 +253,7 @@ def tile_list_speaker_affine_flow_kernel(
                     rows = slice(q + 1 - group, q + 1)
                     nc.sync.dma_start(out=out.rearrange("(q p) j -> p q j", p=P)[:, rows, cols], in_=y[:, rows])
 
-        scale = {}
+        scale, mixed = {}, {}
         last_starts = [sum(LAST_CHUNKS[:n]) for n in range(len(LAST_CHUNKS))]
         h_wide = {}
         for j0 in range(0, S, BANK):
@@ -281,13 +296,17 @@ def tile_list_speaker_affine_flow_kernel(
         for n in range(len(first) // 2):
             speaker_scale(n)
 
-        scaled = scaled_frames(0)
+        scaled = {n: scaled_frames(n) for n in (0, 2, 1)}
         for n, (a, t, j0, width) in enumerate(units):
-            if n + 1 == len(first):
+            if n + 2 == len(first):
                 second_scales.append(kept([P, PACK, BANK], F32, "last_wa"))
-                for m in range(len(first), len(units)):
+                for m in range(len(first), len(first) + 3):
                     speaker_scale(m)
-            ahead = scaled_frames(n + 1) if n + 1 < len(units) else None
+            if n + 1 == len(first):
+                for m in range(len(first) + 3, len(units)):
+                    speaker_scale(m)
+            if n + 1 not in scaled and n + 1 < len(units):
+                scaled[n + 1] = scaled_frames(n + 1)
             if n == 0:
                 rest = kept([P, 2, P], U8, "scale0")
                 nc.vector.tensor_copy(rest[:], slots[:, 0, 2:4])
@@ -297,10 +316,9 @@ def tile_list_speaker_affine_flow_kernel(
             if after[1, BANK] == n + 1:
                 quantise_h(1, waiting[1, BANK][0], BANK, waiting[1, BANK][1])
                 features(BANK, waiting[1, BANK][1])
-            shift(a, t, j0, width, scaled)
+            shift(a, t, j0, width, scaled[n])
             if after[0, BANK] == n:
                 quantise_h(0, waiting[0, BANK][0], BANK, BANK)
-            scaled = ahead
             if (a, j0) == (0, BANK) and t in (1, 2):
                 wa_q[1, t - 1] = quantise_wa(1, t - 1)
             if n + 1 < len(units) and (a, j0) not in [(u[0], u[2]) for u in units[n + 1 :]]:

@@ -20,9 +20,20 @@ P = 128
 PACK = 4
 PASS = P * PACK
 BANK = 512
+NARROW = BANK // 2
+HALVES = H // PASS
 RING = 9
-LAST_CHUNKS = (512, 256, 256)
-SHARED = (2, 4, 6, 10)
+
+FIRST = [(0, t, j0, BANK) for t in range(PACK) for j0 in range(0, S, BANK)]
+SECOND_WIDE = [(1, t, 0, BANK) for t in range(PACK)]
+SECOND_NARROW = [(1, (t - 1) % PACK, j0, NARROW) for j0 in range(BANK, S, NARROW) for t in range(PACK)]
+UNITS = FIRST + SECOND_WIDE + SECOND_NARROW
+N_FIRST = len(FIRST)
+N_WIDE = N_FIRST + len(SECOND_WIDE)
+
+SHARED = {2: NARROW, 4: NARROW, 6: NARROW, 10: BANK}
+
+QUANTISE_BEHIND = {(0, BANK): N_WIDE + 2, (1, BANK): N_WIDE + PACK + 2}
 
 
 def tile_list_speaker_affine_flow_kernel(
@@ -46,27 +57,26 @@ def tile_list_speaker_affine_flow_kernel(
         tab2_plane = kept([P, T], U8, "tab2_plane")
         wb_plane = kept([P, H], U8, "wb_plane")
         w8_plane = kept([P, N], U8, "w8_plane")
-        w8_codes = kept([P, H // PASS, N], U32, "w8_codes")
+        w8_codes = kept([P, HALVES, N], U32, "w8_codes")
         bias_sb = kept([P, N // P], F32, "bias_sb")
 
-        nc.gpsimd.memset(tab2_plane[:].bitcast(I32), 0)
-        nc.gpsimd.memset(tab_plane[:].bitcast(I32), 0)
-        nc.gpsimd.memset(wb_plane[:].bitcast(I32), 0)
-        nc.gpsimd.memset(w8_plane[:].bitcast(I32), 0)
+        for plane in (tab2_plane, tab_plane, wb_plane, w8_plane):
+            nc.gpsimd.memset(plane[:].bitcast(I32), 0)
 
-        def load_plane(queue, plane, scales):
+
+        def load_plane_by_quadrant(plane, scales):
             rows = 4 * scales.shape[0]
             for q in range(4):
-                queue.dma_start(
+                nc.sync.dma_start(
                     out=plane[32 * q : 32 * q + rows, :].bitcast(I32),
                     in_=scales[:, 4 * q : 4 * q + 4, :].bitcast(I32),
                 )
 
-        def load_scale_rows(plane, scales, rows):
+        def load_plane_by_row(plane, scales, rows):
             for r in rows:
-                for a in range(scales.shape[0]):
+                for g in range(scales.shape[0]):
                     nc.sync.dma_start(
-                        out=plane[4 * a + r : P : 32, :].bitcast(I32), in_=scales[a, r : 16 : 4, :].bitcast(I32)
+                        out=plane[4 * g + r : P : 32, :].bitcast(I32), in_=scales[g, r : 16 : 4, :].bitcast(I32)
                     )
 
         def load_words(words):
@@ -74,20 +84,20 @@ def tile_list_speaker_affine_flow_kernel(
             nc.sync.dma_start(out=window[:].bitcast(I32), in_=words.rearrange("p t i -> p (t i)").bitcast(I32))
             return window
 
-        def load_wa(a, c, pool=ring, name="ring"):
-            pieces = 2 if a == 0 else 1
+        def load_wa(half, g, pool=ring, name="ring"):
+            pieces = 2 if half == 0 else 1
             raw = pool.tile([P, pieces, PACK, PASS // pieces], F32, name=name, align_bytes=64)
-            rows = wa[c * PASS : (c + 1) * PASS, a * PASS : (a + 1) * PASS]
+            rows = wa[g * PASS : (g + 1) * PASS, half * PASS : (half + 1) * PASS]
             rows = rows.rearrange("(p i) (u r) -> u p i r", i=PACK, u=pieces)
             for u in range(pieces):
                 nc.sync.dma_start(out=raw[:, u], in_=rows[u])
             return raw
 
-        g_planes = gT.rearrange("(a p t) c -> a t p c", p=P, t=PACK)
+        g_slots = gT.rearrange("(a p t) c -> a t p c", p=P, t=PACK)
 
-        def load_g(a, t):
+        def load_g(half, t):
             window = ring.tile([P, T], F32, name="ring", align_bytes=64)
-            nc.sync.dma_start(out=window[:], in_=g_planes[a, t])
+            nc.sync.dma_start(out=window[:], in_=g_slots[half, t])
             return window
 
         tab_window, wa_raw, g_window = {}, {}, {}
@@ -95,14 +105,14 @@ def tile_list_speaker_affine_flow_kernel(
         nc.sync.dma_start(idx2[:], offs2)
         nc.sync.dma_start(idx[:], offs)
         nc.sync.dma_start(out=wb_words[:].bitcast(I32), in_=wb4_words[0].bitcast(I32))
-        load_scale_rows(tab2_plane, tab2_scales, range(4))
+        load_plane_by_row(tab2_plane, tab2_scales, range(4))
         tab2_window = load_words(tab2_words[0])
-        load_scale_rows(tab_plane, tab_scales, (0, 1))
+        load_plane_by_row(tab_plane, tab_scales, (0, 1))
         wa_raw[0, 0] = load_wa(0, 0)
-        load_scale_rows(tab_plane, tab_scales, (2, 3))
+        load_plane_by_row(tab_plane, tab_scales, (2, 3))
         tab_window[0] = load_words(tab_words[0])
         wa_raw[0, 1] = load_wa(0, 1)
-        load_plane(nc.sync, wb_plane, wb4_scales)
+        load_plane_by_quadrant(wb_plane, wb4_scales)
         tab_window[1] = load_words(tab_words[1])
         g_window[0, 0] = load_g(0, 0)
         g_window[0, 1] = load_g(0, 1)
@@ -116,134 +126,134 @@ def tile_list_speaker_affine_flow_kernel(
             out=w8_codes[:].bitcast(I32),
             in_=w8_words.rearrange("a p n i -> p a (n i)").bitcast(I32),
         )
-        load_plane(nc.sync, w8_plane, w8_scales)
+        load_plane_by_quadrant(w8_plane, w8_scales)
         with nc.allow_non_contiguous_dma(reason="one bias value for each partition and tile of rows"):
             nc.sync.dma_start(out=bias_sb[:], in_=bias.rearrange("(q p) -> p q", p=P))
+
 
         v2_scales = kept([P, S], U8, "v2_scales")
         v2_codes = kept([P, S], U32, "v2_codes")
         v_scales = kept([P, S], U8, "v_scales")
-        v_codes = [[kept([P, BANK], U32, "v_codes%d%d" % (c, b)) for b in range(S // BANK)] for c in range(K // PASS)]
-        wb_scales = {}
+        v_codes = [[kept([P, BANK], U32, "v_codes%d%d" % (g, b)) for b in range(S // BANK)] for g in range(K // PASS)]
         wb_codes = kept([P, 2 * H], U8, "wb_codes")
+        h_scales = [kept([P, S], U8, "h_scales%d" % half) for half in range(HALVES)]
+        h_wide = {}
+        for half, t, j0, width in UNITS:
+            if t == 0:
+                h_wide[half, j0] = kept([P, PACK, width], F32, "h_wide%d_%d" % (half, j0))
+        products = [kept([P, BANK], F32, "product%d" % n) for n in range(PACK)]
+        wa_q, wb_scales, exp_b, a_aside, product, h_round, h_codes = {}, {}, {}, {}, {}, {}, {}
 
-        def offsets(tile, j0, width):
-            return tile[:, j0 // 16 : (j0 + width) // 16]
+        def offsets(j0, width):
+            return idx[:, j0 // 16 : (j0 + width) // 16]
 
-        h_codes = {}
-        h_scales = [kept([P, S], U8, "h_scales%d" % a) for a in range(H // PASS)]
+        def gather_words(g):
+            for b in range(S // BANK):
+                nc.vector.tensor_copy(v_codes[g][b][:], tab_window[g][:].indirect(offsets(b * BANK, BANK)))
 
-        def quantise_wa(a, c):
+        def quantise_wa(half, g):
             grouped = stage.tile([P, PASS * PACK], BF16, name="wa_grouped", align_bytes=64)
-            pieces = wa_raw[a, c].shape[1]
+            pieces = wa_raw[half, g].shape[1]
             for u in range(pieces):
                 nc.scalar.copy(
                     grouped[:].rearrange("p (t u m i) -> p u m i t", t=PACK, u=pieces, i=PACK)[:, u],
-                    wa_raw[a, c][:, u].rearrange("p i (m t) -> p m i t", t=PACK),
+                    wa_raw[half, g][:, u].rearrange("p i (m t) -> p m i t", t=PACK),
                 )
-            codes = kept([P, PASS], U32, "wa_codes%d%d" % (a, c))
-            scales = kept([P, PASS], U8, "wa_scales%d%d" % (a, c))
+            codes = kept([P, PASS], U32, "wa_codes%d%d" % (half, g))
+            scales = kept([P, PASS], U8, "wa_scales%d%d" % (half, g))
             nc.vector.quantize_mx(out=codes[:].bitcast(FP8X4), scales=scales[:], in_=grouped[:])
-            return codes, scales
+            wa_q[half, g] = codes, scales
 
-        def speaker_scale(n):
-            a, t, j0, width = units[n]
+        def mix_frames(half, t, j0, width, a_sum):
+            for g in range(K // PASS):
+                codes, scales = wa_q[half, g]
+                nc.tensor.matmul_mx(
+                    out=a_sum[:],
+                    lhsT=codes[:, t * P : (t + 1) * P].bitcast(FP8X4),
+                    lhsT_scale=scales[:, t * P : (t + 1) * P],
+                    rhs=v_codes[g][j0 // BANK][:, j0 % BANK : j0 % BANK + width].bitcast(FP8X4),
+                    rhs_scale=v_scales[4 * g :, j0 : j0 + width],
+                    start=(g == 0),
+                    stop=(g == K // PASS - 1),
+                )
+
+        def speaker_scale(n, dest=None):
+            half, t, j0, width = UNITS[n]
             cols = slice(j0, j0 + width)
-            r0 = a * PASS + t * P
+            r0 = half * PASS + t * P
             b_sum = psum_y.tile([P, width], F32, name="y_sum")
             nc.tensor.matmul_mx(
                 out=b_sum[:],
                 lhsT=wb_codes[:, 2 * r0 : 2 * (r0 + P)].bitcast(FP4X4),
-                lhsT_scale=wb_scales[a, t],
+                lhsT_scale=wb_scales[half, t],
                 rhs=v2_codes[:, cols].bitcast(FP8X4),
                 rhs_scale=v2_scales[:, cols],
                 start=True,
                 stop=True,
             )
-            if len(first) <= n < wide:
-                scale[n] = second_scales[0][:, t]
-            else:
-                scale[n] = kept([P, width], F32, "scale%d" % n)[:]
-            nc.scalar.activation(scale[n], b_sum[:], ACT.Exp)
+            exp_b[n] = kept([P, width], F32, "exp_b%d" % n)[:] if dest is None else dest
+            nc.scalar.activation(exp_b[n], b_sum[:], ACT.Exp)
             if n in SHARED:
-                mix_aside(n)
+                a_sum = psum_y.tile([P, SHARED[n]], F32, name="y_sum")
+                mix_frames(half, t, j0 + width - SHARED[n], SHARED[n], a_sum)
+                a_aside[n] = kept([P, SHARED[n]], F32, "a_aside%d" % n)
+                nc.scalar.copy(a_aside[n][:], a_sum[:])
 
-        def mix(a, t, j0, width, a_sum):
-            for c in range(K // PASS):
-                codes, scales = wa_q[a, c]
-                nc.tensor.matmul_mx(
-                    out=a_sum[:],
-                    lhsT=codes[:, t * P : (t + 1) * P].bitcast(FP8X4),
-                    lhsT_scale=scales[:, t * P : (t + 1) * P],
-                    rhs=v_codes[c][j0 // BANK][:, j0 % BANK : j0 % BANK + width].bitcast(FP8X4),
-                    rhs_scale=v_scales[4 * c :, j0 : j0 + width],
-                    start=(c == 0),
-                    stop=(c == K // PASS - 1),
-                )
-
-        def mix_aside(n):
-            a, t, j0, width = units[n]
-            a_sum = psum_y.tile([P, width // 2], F32, name="y_sum")
-            mix(a, t, j0 + width // 2, width // 2, a_sum)
-            mixed[n] = kept([P, width // 2], F32, "mixed%d" % n)
-            nc.scalar.copy(mixed[n][:], a_sum[:])
-
-        def scaled_frames(n):
-            a, t, j0, width = units[n]
-            half = (n - wide - 1) % 2 * (BANK // 2)
-            if n < wide:
-                scaled = products[n % len(products)][:, 0:width]
-            elif n == wide:
-                scaled = kept([P, width], F32, "product_wide")[:]
+        def multiply(n):
+            half, t, j0, width = UNITS[n]
+            if n < N_WIDE:
+                dest = products[n % PACK][:]
+            elif n == N_WIDE:
+                dest = kept([P, NARROW], F32, "product_narrow")[:]
             else:
-                scaled = products[(wide - 1) % len(products)][:, half : half + width]
-            own = width // 2 if n in SHARED else width
-            a_sum = psum_a.tile([P, own], F32, name="a_sum")
-            mix(a, t, j0, own, a_sum)
-            nc.vector.tensor_tensor(scaled[:, 0:own], scale[n][:, 0:own], a_sum[:], ALU.mult)
+                c0 = (n - N_WIDE - 1) % 2 * NARROW
+                dest = products[(N_WIDE - 1) % PACK][:, c0 : c0 + NARROW]
+            own = width - SHARED.get(n, 0)
+            if own > 0:
+                a_sum = psum_a.tile([P, own], F32, name="a_sum")
+                mix_frames(half, t, j0, own, a_sum)
+                nc.vector.tensor_tensor(dest[:, 0:own], exp_b[n][:, 0:own], a_sum[:], ALU.mult)
             if own < width:
-                nc.gpsimd.tensor_tensor(scaled[:, own:], scale[n][:, own:], mixed[n][:], ALU.mult)
-            return scaled
+                nc.gpsimd.tensor_tensor(dest[:, own:], exp_b[n][:, own:], a_aside[n][:], ALU.mult)
+            product[n] = dest
 
-        def shift(a, t, j0, width, scaled):
+        def shift(n):
+            half, t, j0, width = UNITS[n]
             nc.vector.tensor_tensor(
-                h_wide[a, j0][:, t, :], g_window[a, t][:].indirect(offsets(idx, j0, width)), scaled, ALU.add
+                h_wide[half, j0][:, t, :], g_window[half, t][:].indirect(offsets(j0, width)), product[n], ALU.add
             )
 
-        def round_h(a, j0, width):
-            h = stage.tile([P, width * PACK], BF16, name="h", align_bytes=64, bufs=3)
-            nc.scalar.copy(
-                h[:].rearrange("p (c i t) -> p c t i", i=4, t=PACK),
-                h_wide[a, j0][:].rearrange("p t (c i) -> p c t i", i=4),
+        def round_h(copy, h, slots):
+            copy(h[:].rearrange("p (c i t) -> p c t i", i=4, t=PACK), slots.rearrange("p t (c i) -> p c t i", i=4))
+
+        def quantise_h(half, j0, width):
+            if (half, j0) in QUANTISE_BEHIND:
+                name = "exp_b%d" % QUANTISE_BEHIND[half, j0]
+            else:
+                name = "h_codes%d_%d" % (half, j0)
+            h_codes[half, j0] = kept([P, width], U32, name)
+            nc.vector.quantize_mx(
+                out=h_codes[half, j0][:].bitcast(FP8X4),
+                scales=h_scales[half][:, j0 : j0 + width],
+                in_=h_round[half, j0][:],
             )
-            return h
 
-        def quantise_h(a, h, j0, width):
-            cols = slice(j0, j0 + width)
-            name = "scale%d" % after[a, j0] if (a, j0) in after else "h_codes%d_%d" % (a, j0)
-            h_codes[a, j0] = kept([P, width], U32, name)
-            nc.vector.quantize_mx(out=h_codes[a, j0][:].bitcast(FP8X4), scales=h_scales[a][:, cols], in_=h[:])
-
-        def features(j0, width):
+        def features(j0, width, pool, name):
             cols = slice(j0, j0 + width)
             y = kept([P, N // P, width], F32, "y%d" % j0)
             group = 1 if width == BANK else 2
             for q in range(N // P):
-                if j0 + width + P == S:
-                    y_sum = psum_a.tile([P, width], F32, name="a_sum")
-                else:
-                    y_sum = psum_y.tile([P, width], F32, name="y_sum")
-                for a in range(H // PASS):
-                    base = j0 if a == 1 else j0 // BANK * BANK
-                    codes = h_codes[a, base][:, j0 - base : j0 - base + width]
+                y_sum = pool.tile([P, width], F32, name=name)
+                for half in range(HALVES):
+                    base = j0 if half == 1 else j0 // BANK * BANK
                     nc.tensor.matmul_mx(
                         out=y_sum[:],
-                        lhsT=w8_codes[:, a, q * P : (q + 1) * P].bitcast(FP8X4),
-                        lhsT_scale=w8_plane[4 * a :, q * P : (q + 1) * P],
-                        rhs=codes.bitcast(FP8X4),
-                        rhs_scale=h_scales[a][:, cols],
-                        start=(a == 0),
-                        stop=(a == H // PASS - 1),
+                        lhsT=w8_codes[:, half, q * P : (q + 1) * P].bitcast(FP8X4),
+                        lhsT_scale=w8_plane[4 * half :, q * P : (q + 1) * P],
+                        rhs=h_codes[half, base][:, j0 - base : j0 - base + width].bitcast(FP8X4),
+                        rhs_scale=h_scales[half][:, cols],
+                        start=(half == 0),
+                        stop=(half == HALVES - 1),
                     )
                 if width == P and q % 2 == 1:
                     nc.vector.tensor_scalar_add(y[:, q], y_sum[:], bias_sb[:, q : q + 1])
@@ -253,93 +263,70 @@ def tile_list_speaker_affine_flow_kernel(
                     rows = slice(q + 1 - group, q + 1)
                     nc.sync.dma_start(out=out.rearrange("(q p) j -> p q j", p=P)[:, rows, cols], in_=y[:, rows])
 
-        scale, mixed = {}, {}
-        last_starts = [sum(LAST_CHUNKS[:n]) for n in range(len(LAST_CHUNKS))]
-        h_wide = {}
-        for j0 in range(0, S, BANK):
-            h_wide[0, j0] = kept([P, PACK, BANK], F32, "h_wide0_%d" % j0)
-        for j0, width in zip(last_starts, LAST_CHUNKS):
-            h_wide[1, j0] = kept([P, PACK, width], F32, "h_wide1_%d" % j0)
 
-        products = [kept([P, BANK], F32, "product%d" % n) for n in range(3)]
-        second_scales = []
-        wa_q = {}
         nc.vector.tensor_copy(v2_scales[:], tab2_plane[:].indirect(idx2[:]))
         nc.vector.tensor_copy(v2_codes[:], tab2_window[:].indirect(idx2[:]))
         nc.vector.tensor_copy(v_scales[:], tab_plane[:].indirect(idx[:]))
-        wa_q[0, 0] = quantise_wa(0, 0)
+        quantise_wa(0, 0)
         nc.vector.tensor_copy(
             wb_codes[:].bitcast(U16).rearrange("p (a t m) -> p a t m", t=PACK, m=P),
             wb_words[:].bitcast(U16).rearrange("p (a m t) -> p a t m", t=PACK, m=P),
         )
-        for b in range(S // BANK):
-            nc.vector.tensor_copy(v_codes[0][b][:], tab_window[0][:].indirect(offsets(idx, b * BANK, BANK)))
-        slots = wb_plane[:].rearrange("p (a m t) -> p a t m", t=PACK, m=P)
-        early = kept([P, 2, PACK, P], U8, "wb_scales")
-        nc.vector.tensor_copy(early[:, 0, 0:2], slots[:, 0, 0:2])
-        nc.vector.tensor_copy(early[:, 1], slots[:, 1])
-        wa_q[0, 1] = quantise_wa(0, 1)
-        for b in range(S // BANK):
-            nc.vector.tensor_copy(v_codes[1][b][:], tab_window[1][:].indirect(offsets(idx, b * BANK, BANK)))
-        for a in range(H // PASS):
-            for t in range(PACK):
-                wb_scales[a, t] = early[:, a, t]
+        gather_words(0)
+        wb_slots = wb_plane[:].rearrange("p (a m t) -> p a t m", t=PACK, m=P)
+        early_scales = kept([P, HALVES, PACK, P], U8, "early_scales")
+        nc.vector.tensor_copy(early_scales[:, 0, 0:2], wb_slots[:, 0, 0:2])
+        nc.vector.tensor_copy(early_scales[:, 1], wb_slots[:, 1])
+        for half, t in [(0, 0), (0, 1)] + [(1, t) for t in range(PACK)]:
+            wb_scales[half, t] = early_scales[:, half, t]
+        quantise_wa(0, 1)
+        gather_words(1)
 
-        first = [(0, t, j0, BANK) for t in range(PACK) for j0 in range(0, S, BANK)]
-        later = list(zip(last_starts, LAST_CHUNKS))[1:]
-        second = [(1, t, 0, LAST_CHUNKS[0]) for t in range(PACK)]
-        second += [(1, (t - 1) % PACK, j0, width) for j0, width in later for t in range(PACK)]
-        units = first + second
-        wide = len(first) + PACK
-        after = {(0, BANK): wide + 2, (1, BANK): wide + PACK + 2}
-        waiting = {}
-        for n in range(len(first) // 2):
+
+        for n in range(PACK):
             speaker_scale(n)
+        for n in (0, 2, 1, 3):
+            multiply(n)
 
-        scaled = {n: scaled_frames(n) for n in (0, 2, 1)}
-        for n, (a, t, j0, width) in enumerate(units):
-            if n + 2 == len(first):
-                second_scales.append(kept([P, PACK, BANK], F32, "last_wa"))
-                for m in range(len(first), len(first) + 3):
+        for n, (half, t, j0, width) in enumerate(UNITS):
+            if n == N_FIRST - 2:
+                second_exp_b = kept([P, PACK, BANK], F32, "last_wa")
+                for m in range(N_FIRST, N_WIDE):
+                    speaker_scale(m, second_exp_b[:, m - N_FIRST])
+            if n == N_FIRST - 1:
+                for m in range(N_WIDE, len(UNITS)):
                     speaker_scale(m)
-            if n + 1 == len(first):
-                for m in range(len(first) + 3, len(units)):
-                    speaker_scale(m)
-            if n + 1 not in scaled and n + 1 < len(units):
-                scaled[n + 1] = scaled_frames(n + 1)
+            if PACK <= n + 1 < len(UNITS):
+                multiply(n + 1)
             if n == 0:
-                rest = kept([P, 2, P], U8, "scale0")
-                nc.vector.tensor_copy(rest[:], slots[:, 0, 2:4])
-                wb_scales[0, 2], wb_scales[0, 3] = rest[:, 0], rest[:, 1]
-                for m in range(len(first) // 2, len(first)):
+                late_scales = kept([P, 2, P], U8, "exp_b0")
+                nc.vector.tensor_copy(late_scales[:], wb_slots[:, 0, 2:4])
+                wb_scales[0, 2], wb_scales[0, 3] = late_scales[:, 0], late_scales[:, 1]
+                for m in range(PACK, N_FIRST):
                     speaker_scale(m)
-            if after[1, BANK] == n + 1:
-                quantise_h(1, waiting[1, BANK][0], BANK, waiting[1, BANK][1])
-                features(BANK, waiting[1, BANK][1])
-            shift(a, t, j0, width, scaled[n])
-            if after[0, BANK] == n:
-                quantise_h(0, waiting[0, BANK][0], BANK, BANK)
-            if (a, j0) == (0, BANK) and t in (1, 2):
-                wa_q[1, t - 1] = quantise_wa(1, t - 1)
-            if n + 1 < len(units) and (a, j0) not in [(u[0], u[2]) for u in units[n + 1 :]]:
-                h = round_h(a, j0, width)
-                if (a, j0) in after:
-                    waiting[a, j0] = (h, width)
-                else:
-                    quantise_h(a, h, j0, width)
-                    if a == 1:
-                        features(j0, width)
+            if n + 1 == QUANTISE_BEHIND[1, BANK]:
+                quantise_h(1, BANK, NARROW)
+                features(BANK, NARROW, psum_y, "y_sum")
+            shift(n)
+            if n == QUANTISE_BEHIND[0, BANK]:
+                quantise_h(0, BANK, BANK)
+            if (half, j0) == (0, BANK) and t in (1, 2):
+                quantise_wa(1, t - 1)
+            range_done = (half, j0) not in [(u[0], u[2]) for u in UNITS[n + 1 :]]
+            if range_done and n + 1 < len(UNITS):
+                h_round[half, j0] = stage.tile([P, width * PACK], BF16, name="h", align_bytes=64, bufs=3)
+                round_h(nc.scalar.copy, h_round[half, j0], h_wide[half, j0][:])
+                if (half, j0) not in QUANTISE_BEHIND:
+                    quantise_h(half, j0, width)
+                    if half == 1:
+                        features(j0, width, psum_y, "y_sum")
 
-        j0 = last_starts[2]
-        pieces = []
-        for c0 in range(0, LAST_CHUNKS[2], P):
-            h = kept([P, P * PACK], BF16, "h_last%d" % c0)
-            nc.vector.tensor_copy(
-                h[:].rearrange("p (c i t) -> p c t i", i=4, t=PACK),
-                h_wide[1, j0][:, :, c0 : c0 + P].rearrange("p t (c i) -> p c t i", i=4),
-            )
-            pieces.append(h)
-        for n, h in enumerate(pieces):
-            quantise_h(1, h, j0 + n * P, P)
-        for n in range(len(pieces)):
-            features(j0 + n * P, P)
+
+        last = S - NARROW
+        for j0 in range(last, S, P):
+            h_round[1, j0] = kept([P, P * PACK], BF16, "h_last%d" % j0)
+            round_h(nc.vector.tensor_copy, h_round[1, j0], h_wide[1, last][:, :, j0 - last : j0 - last + P])
+        for j0 in range(last, S, P):
+            quantise_h(1, j0, P)
+        features(last, P, psum_a, "a_sum")
+        features(last + P, P, psum_y, "y_sum")

@@ -22,18 +22,14 @@ PASS = P * PACK
 BANK = 512
 NARROW = BANK // 2
 HALVES = H // PASS
-RING = 9
+Q_AT = 2
+RING = 8
+TAB_ROW = 4
 
-FIRST = [(0, t, j0, BANK) for t in range(PACK) for j0 in range(0, S, BANK)]
-SECOND_WIDE = [(1, t, 0, BANK) for t in range(PACK)]
-SECOND_NARROW = [(1, (t - 1) % PACK, j0, NARROW) for j0 in range(BANK, S, NARROW) for t in range(PACK)]
-UNITS = FIRST + SECOND_WIDE + SECOND_NARROW
-N_FIRST = len(FIRST)
-N_WIDE = N_FIRST + len(SECOND_WIDE)
+FIRST_SHARE = BANK
+SECOND_SHARE = (BANK, BANK, NARROW, 0)
 
-SHARED = {2: NARROW, 4: NARROW, 6: NARROW, 10: BANK}
-
-QUANTISE_BEHIND = {(0, BANK): N_WIDE + 2, (1, BANK): N_WIDE + PACK + 2}
+RANGES = [(j0, NARROW) for j0 in range(0, S, NARROW)]
 
 
 def tile_list_speaker_affine_flow_kernel(
@@ -57,7 +53,6 @@ def tile_list_speaker_affine_flow_kernel(
         tab2_plane = kept([P, T], U8, "tab2_plane")
         wb_plane = kept([P, H], U8, "wb_plane")
         w8_plane = kept([P, N], U8, "w8_plane")
-        w8_codes = kept([P, HALVES, N], U32, "w8_codes")
         bias_sb = kept([P, N // P], F32, "bias_sb")
 
         for plane in (tab2_plane, tab_plane, wb_plane, w8_plane):
@@ -72,11 +67,11 @@ def tile_list_speaker_affine_flow_kernel(
                     in_=scales[:, 4 * q : 4 * q + 4, :].bitcast(I32),
                 )
 
-        def load_plane_by_row(plane, scales, rows):
+        def load_plane_by_row(plane, scales, rows, first=0):
             for r in rows:
                 for g in range(scales.shape[0]):
                     nc.sync.dma_start(
-                        out=plane[4 * g + r : P : 32, :].bitcast(I32), in_=scales[g, r : 16 : 4, :].bitcast(I32)
+                        out=plane[first + 4 * g + r : P : 32, :].bitcast(I32), in_=scales[g, r : 16 : 4, :].bitcast(I32)
                     )
 
         def load_words(words):
@@ -85,7 +80,7 @@ def tile_list_speaker_affine_flow_kernel(
             return window
 
         def load_wa(half, g, pool=ring, name="ring"):
-            pieces = 2 if half == 0 else 1
+            pieces = 2 if (half, g) == (0, 1) else 1
             raw = pool.tile([P, pieces, PACK, PASS // pieces], F32, name=name, align_bytes=64)
             rows = wa[g * PASS : (g + 1) * PASS, half * PASS : (half + 1) * PASS]
             rows = rows.rearrange("(p i) (u r) -> u p i r", i=PACK, u=pieces)
@@ -107,21 +102,22 @@ def tile_list_speaker_affine_flow_kernel(
         nc.sync.dma_start(out=wb_words[:].bitcast(I32), in_=wb4_words[0].bitcast(I32))
         load_plane_by_row(tab2_plane, tab2_scales, range(4))
         tab2_window = load_words(tab2_words[0])
-        load_plane_by_row(tab_plane, tab_scales, (0, 1))
-        wa_raw[0, 0] = load_wa(0, 0)
-        load_plane_by_row(tab_plane, tab_scales, (2, 3))
-        tab_window[0] = load_words(tab_words[0])
-        wa_raw[0, 1] = load_wa(0, 1)
         load_plane_by_quadrant(wb_plane, wb4_scales)
+        load_plane_by_row(tab_plane, tab_scales, (0,), TAB_ROW)
+        wa_raw[0, 0] = load_wa(0, 0, keep, "wa00")
+        load_plane_by_row(tab_plane, tab_scales, (1, 2, 3), TAB_ROW)
+        tab_window[0] = load_words(tab_words[0])
+        wa_raw[0, 1] = load_wa(0, 1, keep, "wa01")
         tab_window[1] = load_words(tab_words[1])
         g_window[0, 0] = load_g(0, 0)
-        g_window[0, 1] = load_g(0, 1)
         wa_raw[1, 0] = load_wa(1, 0)
+        wa_raw[1, 1] = load_wa(1, 1, keep, "wa11")
+        g_window[0, 1] = load_g(0, 1)
         g_window[0, 2] = load_g(0, 2)
-        wa_raw[1, 1] = load_wa(1, 1, keep, "last_wa")
         g_window[0, 3] = load_g(0, 3)
         for t in range(PACK):
             g_window[1, t] = load_g(1, t)
+        w8_codes = ring.tile([P, HALVES, N], U32, name="ring", align_bytes=64)
         nc.sync.dma_start(
             out=w8_codes[:].bitcast(I32),
             in_=w8_words.rearrange("a p n i -> p a (n i)").bitcast(I32),
@@ -137,12 +133,7 @@ def tile_list_speaker_affine_flow_kernel(
         v_codes = [[kept([P, BANK], U32, "v_codes%d%d" % (g, b)) for b in range(S // BANK)] for g in range(K // PASS)]
         wb_codes = kept([P, 2 * H], U8, "wb_codes")
         h_scales = [kept([P, S], U8, "h_scales%d" % half) for half in range(HALVES)]
-        h_wide = {}
-        for half, t, j0, width in UNITS:
-            if t == 0:
-                h_wide[half, j0] = kept([P, PACK, width], F32, "h_wide%d_%d" % (half, j0))
-        products = [kept([P, BANK], F32, "product%d" % n) for n in range(PACK)]
-        wa_q, wb_scales, exp_b, a_aside, product, h_round, h_codes = {}, {}, {}, {}, {}, {}, {}
+        wa_q, h_round, h_codes = {}, {}, {}
 
         def offsets(j0, width):
             return idx[:, j0 // 16 : (j0 + width) // 16]
@@ -151,7 +142,7 @@ def tile_list_speaker_affine_flow_kernel(
             for b in range(S // BANK):
                 nc.vector.tensor_copy(v_codes[g][b][:], tab_window[g][:].indirect(offsets(b * BANK, BANK)))
 
-        def quantise_wa(half, g):
+        def quantise_wa(half, g, name=None):
             grouped = stage.tile([P, PASS * PACK], BF16, name="wa_grouped", align_bytes=64)
             pieces = wa_raw[half, g].shape[1]
             for u in range(pieces):
@@ -159,7 +150,7 @@ def tile_list_speaker_affine_flow_kernel(
                     grouped[:].rearrange("p (t u m i) -> p u m i t", t=PACK, u=pieces, i=PACK)[:, u],
                     wa_raw[half, g][:, u].rearrange("p i (m t) -> p m i t", t=PACK),
                 )
-            codes = kept([P, PASS], U32, "wa_codes%d%d" % (half, g))
+            codes = kept([P, PASS], U32, name or "wa_codes%d%d" % (half, g))
             scales = kept([P, PASS], U8, "wa_scales%d%d" % (half, g))
             nc.vector.quantize_mx(out=codes[:].bitcast(FP8X4), scales=scales[:], in_=grouped[:])
             wa_q[half, g] = codes, scales
@@ -172,66 +163,46 @@ def tile_list_speaker_affine_flow_kernel(
                     lhsT=codes[:, t * P : (t + 1) * P].bitcast(FP8X4),
                     lhsT_scale=scales[:, t * P : (t + 1) * P],
                     rhs=v_codes[g][j0 // BANK][:, j0 % BANK : j0 % BANK + width].bitcast(FP8X4),
-                    rhs_scale=v_scales[4 * g :, j0 : j0 + width],
+                    rhs_scale=v_scales[TAB_ROW + 4 * g :, j0 : j0 + width],
                     start=(g == 0),
                     stop=(g == K // PASS - 1),
                 )
 
-        def speaker_scale(n, dest=None):
-            half, t, j0, width = UNITS[n]
-            cols = slice(j0, j0 + width)
+        def speaker_scale(half, t, j0, dest):
+            cols = slice(j0, j0 + BANK)
             r0 = half * PASS + t * P
-            b_sum = psum_y.tile([P, width], F32, name="y_sum")
+            b_sum = psum_y.tile([P, BANK], F32, name="y_sum")
             nc.tensor.matmul_mx(
                 out=b_sum[:],
                 lhsT=wb_codes[:, 2 * r0 : 2 * (r0 + P)].bitcast(FP4X4),
-                lhsT_scale=wb_scales[half, t],
+                lhsT_scale=wb_scales[:, r0 : r0 + P],
                 rhs=v2_codes[:, cols].bitcast(FP8X4),
                 rhs_scale=v2_scales[:, cols],
                 start=True,
                 stop=True,
             )
-            exp_b[n] = kept([P, width], F32, "exp_b%d" % n)[:] if dest is None else dest
-            nc.scalar.activation(exp_b[n], b_sum[:], ACT.Exp)
-            if n in SHARED:
-                a_sum = psum_y.tile([P, SHARED[n]], F32, name="y_sum")
-                mix_frames(half, t, j0 + width - SHARED[n], SHARED[n], a_sum)
-                a_aside[n] = kept([P, SHARED[n]], F32, "a_aside%d" % n)
-                nc.scalar.copy(a_aside[n][:], a_sum[:])
+            nc.scalar.activation(dest, b_sum[:], ACT.Exp)
 
-        def multiply(n):
-            half, t, j0, width = UNITS[n]
-            if n < N_WIDE:
-                dest = products[n % PACK][:]
-            elif n == N_WIDE:
-                dest = kept([P, NARROW], F32, "product_narrow")[:]
-            else:
-                c0 = (n - N_WIDE - 1) % 2 * NARROW
-                dest = products[(N_WIDE - 1) % PACK][:, c0 : c0 + NARROW]
-            own = width - SHARED.get(n, 0)
-            if own > 0:
-                a_sum = psum_a.tile([P, own], F32, name="a_sum")
-                mix_frames(half, t, j0, own, a_sum)
-                nc.vector.tensor_tensor(dest[:, 0:own], exp_b[n][:, 0:own], a_sum[:], ALU.mult)
-            if own < width:
-                nc.gpsimd.tensor_tensor(dest[:, own:], exp_b[n][:, own:], a_aside[n][:], ALU.mult)
-            product[n] = dest
+        def frames_aside(half, t, j0, width, pool, name):
+            a_sum = pool.tile([P, width], F32, name=name)
+            mix_frames(half, t, j0, width, a_sum)
+            aside = kept([P, width], F32, "aside%d%d" % (half, t))
+            nc.scalar.copy(aside[:], a_sum[:])
+            return aside
 
-        def shift(n):
-            half, t, j0, width = UNITS[n]
-            nc.vector.tensor_tensor(
-                h_wide[half, j0][:, t, :], g_window[half, t][:].indirect(offsets(j0, width)), product[n], ALU.add
-            )
+        def frames(half, t, j0, width, spare=False):
+            a_sum = psum_y.tile([P, width], F32, name="y_sum") if spare else psum_a.tile([P, width], F32, name="a_sum")
+            mix_frames(half, t, j0, width, a_sum)
+            return a_sum
+
+        def shift(half, t, j0, width, dest, product):
+            nc.vector.tensor_tensor(dest, g_window[half, t][:].indirect(offsets(j0, width)), product, ALU.add)
 
         def round_h(copy, h, slots):
-            copy(h[:].rearrange("p (c i t) -> p c t i", i=4, t=PACK), slots.rearrange("p t (c i) -> p c t i", i=4))
+            copy(h.rearrange("p (c i t) -> p c t i", i=4, t=PACK), slots.rearrange("p t (c i) -> p c t i", i=4))
 
         def quantise_h(half, j0, width):
-            if (half, j0) in QUANTISE_BEHIND:
-                name = "exp_b%d" % QUANTISE_BEHIND[half, j0]
-            else:
-                name = "h_codes%d_%d" % (half, j0)
-            h_codes[half, j0] = kept([P, width], U32, name)
+            h_codes[half, j0] = kept([P, width], U32, "h_codes%d_%d" % (half, j0))
             nc.vector.quantize_mx(
                 out=h_codes[half, j0][:].bitcast(FP8X4),
                 scales=h_scales[half][:, j0 : j0 + width],
@@ -266,6 +237,11 @@ def tile_list_speaker_affine_flow_kernel(
 
         nc.vector.tensor_copy(v2_scales[:], tab2_plane[:].indirect(idx2[:]))
         nc.vector.tensor_copy(v2_codes[:], tab2_window[:].indirect(idx2[:]))
+        wb_scales = kept([P, H], U8, "wb_scales")
+        nc.vector.tensor_copy(
+            wb_scales[:].rearrange("p (a t m) -> p a t m", t=PACK, m=P),
+            wb_plane[:].rearrange("p (a m t) -> p a t m", t=PACK, m=P),
+        )
         nc.vector.tensor_copy(v_scales[:], tab_plane[:].indirect(idx[:]))
         quantise_wa(0, 0)
         nc.vector.tensor_copy(
@@ -273,60 +249,121 @@ def tile_list_speaker_affine_flow_kernel(
             wb_words[:].bitcast(U16).rearrange("p (a m t) -> p a t m", t=PACK, m=P),
         )
         gather_words(0)
-        wb_slots = wb_plane[:].rearrange("p (a m t) -> p a t m", t=PACK, m=P)
-        early_scales = kept([P, HALVES, PACK, P], U8, "early_scales")
-        nc.vector.tensor_copy(early_scales[:, 0, 0:2], wb_slots[:, 0, 0:2])
-        nc.vector.tensor_copy(early_scales[:, 1], wb_slots[:, 1])
-        for half, t in [(0, 0), (0, 1)] + [(1, t) for t in range(PACK)]:
-            wb_scales[half, t] = early_scales[:, half, t]
         quantise_wa(0, 1)
         gather_words(1)
 
 
-        for n in range(PACK):
-            speaker_scale(n)
-        for n in (0, 2, 1, 3):
-            multiply(n)
+        first = {(t, b): kept([P, BANK], F32, "first%d%d" % (t, b)) for b in range(S // BANK) for t in range(PACK)}
+        ahead = [(0, 0), (PACK - 1, 0)]
+        behind = [(t, b) for b in range(S // BANK) for t in range(PACK) if (t, b) not in ahead]
+        first_exp = {}
+        for units, name in ((ahead, "wa00"), (behind, "wa01")):
+            cells = kept([P, len(units), BANK], F32, name)
+            for n, (t, b) in enumerate(units):
+                first_exp[t, b] = cells[:, n, :]
+                speaker_scale(0, t, b * BANK, first_exp[t, b])
+        own = BANK - FIRST_SHARE
 
-        for n, (half, t, j0, width) in enumerate(UNITS):
-            if n == N_FIRST - 2:
-                second_exp_b = kept([P, PACK, BANK], F32, "last_wa")
-                for m in range(N_FIRST, N_WIDE):
-                    speaker_scale(m, second_exp_b[:, m - N_FIRST])
-            if n == N_FIRST - 1:
-                for m in range(N_WIDE, len(UNITS)):
-                    speaker_scale(m)
-            if PACK <= n + 1 < len(UNITS):
-                multiply(n + 1)
-            if n == 0:
-                late_scales = kept([P, 2, P], U8, "exp_b0")
-                nc.vector.tensor_copy(late_scales[:], wb_slots[:, 0, 2:4])
-                wb_scales[0, 2], wb_scales[0, 3] = late_scales[:, 0], late_scales[:, 1]
-                for m in range(PACK, N_FIRST):
-                    speaker_scale(m)
-            if n + 1 == QUANTISE_BEHIND[1, BANK]:
-                quantise_h(1, BANK, NARROW)
-                features(BANK, NARROW, psum_y, "y_sum")
-            shift(n)
-            if n == QUANTISE_BEHIND[0, BANK]:
-                quantise_h(0, BANK, BANK)
-            if (half, j0) == (0, BANK) and t in (1, 2):
-                quantise_wa(1, t - 1)
-            range_done = (half, j0) not in [(u[0], u[2]) for u in UNITS[n + 1 :]]
-            if range_done and n + 1 < len(UNITS):
-                h_round[half, j0] = stage.tile([P, width * PACK], BF16, name="h", align_bytes=64, bufs=3)
-                round_h(nc.scalar.copy, h_round[half, j0], h_wide[half, j0][:])
-                if (half, j0) not in QUANTISE_BEHIND:
-                    quantise_h(half, j0, width)
-                    if half == 1:
-                        features(j0, width, psum_y, "y_sum")
+        def multiply_first(t, b):
+            width = own if (t, b) == (PACK - 1, 0) else BANK
+            if width > 0:
+                a_sum = frames(0, t, b * BANK, width, b)
+                nc.vector.tensor_tensor(first[t, b][:, 0:width], first_exp[t, b][:, 0:width], a_sum[:], ALU.mult)
+
+        multiply_first(0, 0)
+        aside = frames_aside(0, PACK - 1, own, FIRST_SHARE, psum_a, "a_sum")
+        nc.gpsimd.tensor_tensor(first[PACK - 1, 0][:, own:], first_exp[PACK - 1, 0][:, own:], aside[:], ALU.mult)
+        for b in range(S // BANK):
+            for t in range(PACK):
+                if (t, b) != (0, 0):
+                    multiply_first(t, b)
+
+        h_first = kept([P, S // BANK, PACK, BANK], F32, "wa00")
+
+        def shift_first(t, b, c0=0, width=BANK):
+            cols = slice(c0, c0 + width)
+            shift(0, t, b * BANK + c0, width, h_first[:, b, t, cols], first[t, b][:, cols])
+
+        def round_first(b):
+            h_round[0, b * BANK] = stage.tile([P, BANK * PACK], BF16, name="h", align_bytes=64, bufs=3)
+            round_h(nc.scalar.copy, h_round[0, b * BANK][:], h_first[:, b])
+
+        shift_first(0, 0)
+        shift_first(0, 1)
+        quantise_wa(1, 0)
+        shift_first(1, 0)
+        shift_first(1, 1, 0, NARROW)
+        quantise_wa(1, 1, "first10")
+        shift_first(1, 1, NARROW, NARROW)
+        second_exp = kept([P, S // BANK, PACK, BANK], F32, "wa11")
+        early_exp, late_exp = second_exp[:, 0], second_exp[:, 1]
+        for t in range(PACK):
+            speaker_scale(1, t, BANK, late_exp[:, t, :])
+        asides = {t: frames_aside(1, t, BANK, share, psum_y, "y_sum") for t, share in enumerate(SECOND_SHARE) if share}
+        for t in range(PACK):
+            speaker_scale(1, t, 0, early_exp[:, t, :])
+        shift_first(2, 0)
+        shift_first(2, 1)
+        shift_first(3, 0)
+        round_first(0)
+        shift_first(3, 1)
 
 
-        last = S - NARROW
+        second = kept([P, PACK * S], F32, "first30")
+        h_second = kept([P, 2 * PACK * NARROW], F32, "first31")
+        corner = h_second[:, P : P + NARROW]
+
+        def product(t, j0, width):
+            return corner if (t, j0) == (PACK - 1, 0) else second[:, t * S + j0 : t * S + j0 + width]
+
+        for t, share in enumerate(SECOND_SHARE):
+            if share > 0:
+                nc.gpsimd.tensor_tensor(product(t, BANK, share), late_exp[:, t, 0:share], asides[t][:], ALU.mult)
+        for t, share in enumerate(SECOND_SHARE):
+            if share < BANK:
+                a_sum = frames(1, t, BANK + share, BANK - share)
+                nc.vector.tensor_tensor(product(t, BANK + share, BANK - share), late_exp[:, t, share:], a_sum[:], ALU.mult)
+        for t in range(PACK):
+            a_sum = frames(1, t, 0, BANK, t >= 2)
+            pieces = [(0, BANK)] if t < PACK - 1 else [(NARROW, NARROW), (0, NARROW)]
+            for j0, width in pieces:
+                cols = slice(j0, j0 + width)
+                nc.vector.tensor_tensor(product(t, j0, width), early_exp[:, t, cols], a_sum[:, cols], ALU.mult)
+        round_first(1)
+
+        def shift_range(n):
+            j0, width = RANGES[n]
+            base = NARROW * (PACK, 0, PACK, PACK // 2)[n]
+            h = h_second[:, base : base + PACK * width]
+            for t in ([PACK - 1] + list(range(PACK - 1)) if n == 1 else range(PACK)):
+                shift(1, t, j0, width, h[:, t * width : (t + 1) * width], product(t, j0, width))
+                if n == 0 and t == Q_AT:
+                    quantise_h(0, BANK, BANK)
+                if n == len(RANGES) - 1 and t == 1:
+                    finish(n - 1)
+            return h.rearrange("p (t c) -> p t c", t=PACK)
+
+        def finish(n):
+            j0, width = RANGES[n]
+            quantise_h(1, j0, width)
+            features(j0, width, psum_y, "y_sum")
+
+        quantise_h(0, 0, BANK)
+        for n, (j0, width) in enumerate(RANGES[:-1]):
+            h = shift_range(n)
+            h_round[1, j0] = stage.tile([P, width * PACK], BF16, name="h", align_bytes=64, bufs=3)
+            round_h(nc.scalar.copy, h_round[1, j0][:], h)
+            if n > 0:
+                finish(n - 1)
+        h = shift_range(len(RANGES) - 1)
+
+
+        last = RANGES[-1][0]
         for j0 in range(last, S, P):
             h_round[1, j0] = kept([P, P * PACK], BF16, "h_last%d" % j0)
-            round_h(nc.vector.tensor_copy, h_round[1, j0], h_wide[1, last][:, :, j0 - last : j0 - last + P])
+            round_h(nc.vector.tensor_copy, h_round[1, j0][:], h[:, :, j0 - last : j0 - last + P])
         for j0 in range(last, S, P):
             quantise_h(1, j0, P)
-        features(last, P, psum_a, "a_sum")
-        features(last + P, P, psum_y, "y_sum")
+        for j0 in range(last, S, P):
+            pool, name = (psum_a, "a_sum") if j0 == last else (psum_y, "y_sum")
+            features(j0, P, pool, name)

@@ -22,12 +22,11 @@ PASS = P * PACK
 BANK = 512
 NARROW = BANK // 2
 HALVES = H // PASS
-Q_AT = 2
 RING = 8
 TAB_ROW = 4
 
-FIRST_SHARE = BANK
-SECOND_SHARE = (BANK, BANK, NARROW, 0)
+FIRST_SHARE = (0, 0, 0, BANK)
+SECOND_SHARE = (BANK, BANK, 0, 0)
 
 RANGES = [(j0, NARROW) for j0 in range(0, S, NARROW)]
 
@@ -201,8 +200,8 @@ def tile_list_speaker_affine_flow_kernel(
         def round_h(copy, h, slots):
             copy(h.rearrange("p (c i t) -> p c t i", i=4, t=PACK), slots.rearrange("p t (c i) -> p c t i", i=4))
 
-        def quantise_h(half, j0, width):
-            h_codes[half, j0] = kept([P, width], U32, "h_codes%d_%d" % (half, j0))
+        def quantise_h(half, j0, width, name=None):
+            h_codes[half, j0] = kept([P, width], U32, name or "h_codes%d_%d" % (half, j0))
             nc.vector.quantize_mx(
                 out=h_codes[half, j0][:].bitcast(FP8X4),
                 scales=h_scales[half][:, j0 : j0 + width],
@@ -257,26 +256,28 @@ def tile_list_speaker_affine_flow_kernel(
         ahead = [(0, 0), (PACK - 1, 0)]
         behind = [(t, b) for b in range(S // BANK) for t in range(PACK) if (t, b) not in ahead]
         first_exp = {}
-        for units, name in ((ahead, "wa00"), (behind, "wa01")):
+
+        def first_exps(units, name):
             cells = kept([P, len(units), BANK], F32, name)
             for n, (t, b) in enumerate(units):
                 first_exp[t, b] = cells[:, n, :]
                 speaker_scale(0, t, b * BANK, first_exp[t, b])
-        own = BANK - FIRST_SHARE
 
-        def multiply_first(t, b):
-            width = own if (t, b) == (PACK - 1, 0) else BANK
-            if width > 0:
-                a_sum = frames(0, t, b * BANK, width, b)
-                nc.vector.tensor_tensor(first[t, b][:, 0:width], first_exp[t, b][:, 0:width], a_sum[:], ALU.mult)
-
-        multiply_first(0, 0)
-        aside = frames_aside(0, PACK - 1, own, FIRST_SHARE, psum_a, "a_sum")
-        nc.gpsimd.tensor_tensor(first[PACK - 1, 0][:, own:], first_exp[PACK - 1, 0][:, own:], aside[:], ALU.mult)
+        first_exps(ahead, "wa00")
+        sums = {(0, 0): frames(0, 0, 0, BANK)}
+        for t, b in ahead[1:]:
+            own = BANK - FIRST_SHARE[t]
+            aside = frames_aside(0, t, own, FIRST_SHARE[t], psum_a, "a_sum")
+            nc.gpsimd.tensor_tensor(first[t, b][:, own:], first_exp[t, b][:, own:], aside[:], ALU.mult)
+        for t in (1, 2):
+            sums[t, 0] = frames(0, t, 0, BANK)
+        first_exps(behind, "wa01")
         for b in range(S // BANK):
             for t in range(PACK):
-                if (t, b) != (0, 0):
-                    multiply_first(t, b)
+                own = BANK - FIRST_SHARE[t] if b == 0 else BANK
+                if own > 0:
+                    a_sum = sums[t, b] if (t, b) in sums else frames(0, t, b * BANK, own, True)
+                    nc.vector.tensor_tensor(first[t, b][:, 0:own], first_exp[t, b][:, 0:own], a_sum[:, 0:own], ALU.mult)
 
         h_first = kept([P, S // BANK, PACK, BANK], F32, "wa00")
 
@@ -285,21 +286,20 @@ def tile_list_speaker_affine_flow_kernel(
             shift(0, t, b * BANK + c0, width, h_first[:, b, t, cols], first[t, b][:, cols])
 
         def round_first(b):
-            h_round[0, b * BANK] = stage.tile([P, BANK * PACK], BF16, name="h", align_bytes=64, bufs=3)
+            h_round[0, b * BANK] = stage.tile([P, BANK * PACK], BF16, name="h", align_bytes=64)
             round_h(nc.scalar.copy, h_round[0, b * BANK][:], h_first[:, b])
 
         shift_first(0, 0)
         shift_first(0, 1)
         quantise_wa(1, 0)
         shift_first(1, 0)
-        shift_first(1, 1, 0, NARROW)
+        shift_first(1, 1)
         quantise_wa(1, 1, "first10")
-        shift_first(1, 1, NARROW, NARROW)
         second_exp = kept([P, S // BANK, PACK, BANK], F32, "wa11")
         early_exp, late_exp = second_exp[:, 0], second_exp[:, 1]
         for t in range(PACK):
             speaker_scale(1, t, BANK, late_exp[:, t, :])
-        asides = {t: frames_aside(1, t, BANK, share, psum_y, "y_sum") for t, share in enumerate(SECOND_SHARE) if share}
+        asides = {t: frames_aside(1, t, BANK, share, psum_a, "a_sum") for t, share in enumerate(SECOND_SHARE) if share}
         for t in range(PACK):
             speaker_scale(1, t, 0, early_exp[:, t, :])
         shift_first(2, 0)
@@ -310,11 +310,16 @@ def tile_list_speaker_affine_flow_kernel(
 
 
         second = kept([P, PACK * S], F32, "first30")
-        h_second = kept([P, 2 * PACK * NARROW], F32, "first31")
+        h_second = kept([P, 2 * PACK * NARROW + sum(SECOND_SHARE)], F32, "first31")
         corner = h_second[:, P : P + NARROW]
 
         def product(t, j0, width):
-            return corner if (t, j0) == (PACK - 1, 0) else second[:, t * S + j0 : t * S + j0 + width]
+            if (t, j0) == (PACK - 1, 0):
+                return corner
+            if BANK <= j0 < BANK + SECOND_SHARE[t]:
+                c0 = 2 * PACK * NARROW + sum(SECOND_SHARE[:t]) + j0 - BANK
+                return h_second[:, c0 : c0 + width]
+            return second[:, t * S + j0 : t * S + j0 + width]
 
         for t, share in enumerate(SECOND_SHARE):
             if share > 0:
@@ -333,13 +338,13 @@ def tile_list_speaker_affine_flow_kernel(
 
         def shift_range(n):
             j0, width = RANGES[n]
-            base = NARROW * (PACK, 0, PACK, PACK // 2)[n]
+            base = NARROW * (PACK, 0, PACK, 1)[n]
             h = h_second[:, base : base + PACK * width]
             for t in ([PACK - 1] + list(range(PACK - 1)) if n == 1 else range(PACK)):
                 shift(1, t, j0, width, h[:, t * width : (t + 1) * width], product(t, j0, width))
-                if n == 0 and t == Q_AT:
-                    quantise_h(0, BANK, BANK)
-                if n == len(RANGES) - 1 and t == 1:
+                if n == 2 and t == 0:
+                    quantise_h(0, BANK, BANK, "h_round_first")
+                if n == len(RANGES) - 1 and t == PACK - 2:
                     finish(n - 1)
             return h.rearrange("p (t c) -> p t c", t=PACK)
 
@@ -350,11 +355,12 @@ def tile_list_speaker_affine_flow_kernel(
 
         quantise_h(0, 0, BANK)
         for n, (j0, width) in enumerate(RANGES[:-1]):
+            if n == 2:
+                finish(0)
             h = shift_range(n)
-            h_round[1, j0] = stage.tile([P, width * PACK], BF16, name="h", align_bytes=64, bufs=3)
+            h_round[1, j0] = kept([P, width * PACK], BF16, ("h_round_first", "h_round1", "h_codes1_0")[n])
             round_h(nc.scalar.copy, h_round[1, j0][:], h)
-            if n > 0:
-                finish(n - 1)
+        finish(1)
         h = shift_range(len(RANGES) - 1)
 
 

@@ -25,8 +25,7 @@ HALVES = H // PASS
 RING = 8
 TAB_ROW = 4
 
-FIRST_SHARE = (0, 0, 0, BANK)
-SECOND_SHARE = (BANK, BANK, 0, 0)
+SECOND_SHARE = (BANK, BANK, P, 0)
 
 RANGES = [(j0, NARROW) for j0 in range(0, S, NARROW)]
 
@@ -138,8 +137,10 @@ def tile_list_speaker_affine_flow_kernel(
             return idx[:, j0 // 16 : (j0 + width) // 16]
 
         def gather_words(g):
-            for b in range(S // BANK):
-                nc.vector.tensor_copy(v_codes[g][b][:], tab_window[g][:].indirect(offsets(b * BANK, BANK)))
+            cuts = (0, BANK, S) if g == 0 else (0, NARROW, BANK, S)
+            for j0, j1 in zip(cuts, cuts[1:]):
+                dest = v_codes[g][j0 // BANK][:, j0 % BANK : j0 % BANK + j1 - j0]
+                nc.vector.tensor_copy(dest, tab_window[g][:].indirect(offsets(j0, j1 - j0)))
 
         def quantise_wa(half, g, name=None):
             grouped = stage.tile([P, PASS * PACK], BF16, name="wa_grouped", align_bytes=64)
@@ -158,7 +159,7 @@ def tile_list_speaker_affine_flow_kernel(
             for g in range(K // PASS):
                 codes, scales = wa_q[half, g]
                 nc.tensor.matmul_mx(
-                    out=a_sum[:],
+                    out=a_sum,
                     lhsT=codes[:, t * P : (t + 1) * P].bitcast(FP8X4),
                     lhsT_scale=scales[:, t * P : (t + 1) * P],
                     rhs=v_codes[g][j0 // BANK][:, j0 % BANK : j0 % BANK + width].bitcast(FP8X4),
@@ -167,10 +168,10 @@ def tile_list_speaker_affine_flow_kernel(
                     stop=(g == K // PASS - 1),
                 )
 
-        def speaker_scale(half, t, j0, dest):
+        def speaker_scale(half, t, j0, dest, spare=False):
             cols = slice(j0, j0 + BANK)
             r0 = half * PASS + t * P
-            b_sum = psum_y.tile([P, BANK], F32, name="y_sum")
+            b_sum = psum_a.tile([P, BANK], F32, name="a_sum") if spare else psum_y.tile([P, BANK], F32, name="y_sum")
             nc.tensor.matmul_mx(
                 out=b_sum[:],
                 lhsT=wb_codes[:, 2 * r0 : 2 * (r0 + P)].bitcast(FP4X4),
@@ -182,16 +183,9 @@ def tile_list_speaker_affine_flow_kernel(
             )
             nc.scalar.activation(dest, b_sum[:], ACT.Exp)
 
-        def frames_aside(half, t, j0, width, pool, name):
-            a_sum = pool.tile([P, width], F32, name=name)
-            mix_frames(half, t, j0, width, a_sum)
-            aside = kept([P, width], F32, "aside%d%d" % (half, t))
-            nc.scalar.copy(aside[:], a_sum[:])
-            return aside
-
         def frames(half, t, j0, width, spare=False):
             a_sum = psum_y.tile([P, width], F32, name="y_sum") if spare else psum_a.tile([P, width], F32, name="a_sum")
-            mix_frames(half, t, j0, width, a_sum)
+            mix_frames(half, t, j0, width, a_sum[:])
             return a_sum
 
         def shift(half, t, j0, width, dest, product):
@@ -252,8 +246,12 @@ def tile_list_speaker_affine_flow_kernel(
         gather_words(1)
 
 
-        first = {(t, b): kept([P, BANK], F32, "first%d%d" % (t, b)) for b in range(S // BANK) for t in range(PACK)}
-        ahead = [(0, 0), (PACK - 1, 0)]
+        even = kept([P, 2, S], F32, "first_even")
+        first = {(2 * n, b): even[:, n, b * BANK : (b + 1) * BANK] for n in range(2) for b in range(S // BANK)}
+        for t in range(1, PACK, 2):
+            for b in range(S // BANK):
+                first[t, b] = kept([P, BANK], F32, "first%d%d" % (t, b))[:]
+        ahead = [(0, 0), (2, 0), (1, 0)]
         behind = [(t, b) for b in range(S // BANK) for t in range(PACK) if (t, b) not in ahead]
         first_exp = {}
 
@@ -261,36 +259,35 @@ def tile_list_speaker_affine_flow_kernel(
             cells = kept([P, len(units), BANK], F32, name)
             for n, (t, b) in enumerate(units):
                 first_exp[t, b] = cells[:, n, :]
-                speaker_scale(0, t, b * BANK, first_exp[t, b])
+                speaker_scale(0, t, b * BANK, first_exp[t, b], (t, b) in behind[-1:])
+            return cells
 
-        first_exps(ahead, "wa00")
-        sums = {(0, 0): frames(0, 0, 0, BANK)}
-        for t, b in ahead[1:]:
-            own = BANK - FIRST_SHARE[t]
-            aside = frames_aside(0, t, own, FIRST_SHARE[t], psum_a, "a_sum")
-            nc.gpsimd.tensor_tensor(first[t, b][:, own:], first_exp[t, b][:, own:], aside[:], ALU.mult)
-        for t in (1, 2):
-            sums[t, 0] = frames(0, t, 0, BANK)
+        ahead_exp = first_exps(ahead, "wa00")
+        sums = {}
+        for n, j0 in enumerate(range(0, BANK, NARROW)):
+            a_sum = psum_a.tile([P, 2, NARROW], F32, name="a_sum")
+            for m in range(2):
+                mix_frames(0, 2 * m, j0, NARROW, a_sum[:, m])
+            aside = kept([P, 2, NARROW], F32, "first_aside%d" % n)
+            nc.scalar.copy(aside[:], a_sum[:])
+            cols = slice(j0, j0 + NARROW)
+            nc.gpsimd.tensor_tensor(even[:, :, cols], ahead_exp[:, 0:2, cols], aside[:], ALU.mult)
+            sums[2 * n + 1, 0] = frames(0, 2 * n + 1, 0, BANK)
         first_exps(behind, "wa01")
-        for b in range(S // BANK):
-            for t in range(PACK):
-                own = BANK - FIRST_SHARE[t] if b == 0 else BANK
-                if own > 0:
-                    a_sum = sums[t, b] if (t, b) in sums else frames(0, t, b * BANK, own, True)
-                    nc.vector.tensor_tensor(first[t, b][:, 0:own], first_exp[t, b][:, 0:own], a_sum[:, 0:own], ALU.mult)
+        for t, b in list(sums) + [(t, 1) for t in range(PACK)]:
+            a_sum = sums[t, b] if b == 0 else frames(0, t, BANK, BANK, True)
+            nc.vector.tensor_tensor(first[t, b], first_exp[t, b], a_sum[:], ALU.mult)
 
-        h_first = kept([P, S // BANK, PACK, BANK], F32, "wa00")
+        h_first = kept([P, PACK, S], F32, "wa00")
 
-        def shift_first(t, b, c0=0, width=BANK):
-            cols = slice(c0, c0 + width)
-            shift(0, t, b * BANK + c0, width, h_first[:, b, t, cols], first[t, b][:, cols])
+        def shift_first(t, b):
+            shift(0, t, b * BANK, BANK, h_first[:, t, b * BANK : (b + 1) * BANK], first[t, b])
 
         def round_first(b):
             h_round[0, b * BANK] = stage.tile([P, BANK * PACK], BF16, name="h", align_bytes=64)
-            round_h(nc.scalar.copy, h_round[0, b * BANK][:], h_first[:, b])
+            round_h(nc.scalar.copy, h_round[0, b * BANK][:], h_first[:, :, b * BANK : (b + 1) * BANK])
 
-        shift_first(0, 0)
-        shift_first(0, 1)
+        shift(0, 0, 0, S, h_first[:, 0, :], even[:, 0, :])
         quantise_wa(1, 0)
         shift_first(1, 0)
         shift_first(1, 1)
@@ -299,41 +296,43 @@ def tile_list_speaker_affine_flow_kernel(
         early_exp, late_exp = second_exp[:, 0], second_exp[:, 1]
         for t in range(PACK):
             speaker_scale(1, t, BANK, late_exp[:, t, :])
-        asides = {t: frames_aside(1, t, BANK, share, psum_a, "a_sum") for t, share in enumerate(SECOND_SHARE) if share}
+        late_sums = [frames(1, t, BANK, BANK) for t in range(PACK)]
+        shared = sum(SECOND_SHARE)
+        aside = kept([P, shared], F32, "second_aside")
+        for t, share in enumerate(SECOND_SHARE):
+            if share > 0:
+                nc.scalar.copy(aside[:, t * BANK : t * BANK + share], late_sums[t][:, 0:share])
         for t in range(PACK):
             speaker_scale(1, t, 0, early_exp[:, t, :])
-        shift_first(2, 0)
-        shift_first(2, 1)
+        shift(0, 2, 0, S, h_first[:, 2, :], even[:, 1, :])
         shift_first(3, 0)
         round_first(0)
         shift_first(3, 1)
 
 
-        second = kept([P, PACK * S], F32, "first30")
-        h_second = kept([P, 2 * PACK * NARROW + sum(SECOND_SHARE)], F32, "first31")
+        early = kept([P, PACK * BANK], F32, "first30")
+        h_second = kept([P, 2 * PACK * NARROW + PACK * BANK], F32, "first31")
         corner = h_second[:, P : P + NARROW]
+        late = h_second[:, 2 * PACK * NARROW :]
 
         def product(t, j0, width):
             if (t, j0) == (PACK - 1, 0):
                 return corner
-            if BANK <= j0 < BANK + SECOND_SHARE[t]:
-                c0 = 2 * PACK * NARROW + sum(SECOND_SHARE[:t]) + j0 - BANK
-                return h_second[:, c0 : c0 + width]
-            return second[:, t * S + j0 : t * S + j0 + width]
+            c0 = t * BANK + j0 % BANK
+            return (early if j0 < BANK else late)[:, c0 : c0 + width]
 
-        for t, share in enumerate(SECOND_SHARE):
-            if share > 0:
-                nc.gpsimd.tensor_tensor(product(t, BANK, share), late_exp[:, t, 0:share], asides[t][:], ALU.mult)
-        for t, share in enumerate(SECOND_SHARE):
-            if share < BANK:
-                a_sum = frames(1, t, BANK + share, BANK - share)
-                nc.vector.tensor_tensor(product(t, BANK + share, BANK - share), late_exp[:, t, share:], a_sum[:], ALU.mult)
+        nc.gpsimd.tensor_tensor(late[:, 0:shared], late_exp.rearrange("p t c -> p (t c)")[:, 0:shared], aside[:], ALU.mult)
         for t in range(PACK):
             a_sum = frames(1, t, 0, BANK, t >= 2)
             pieces = [(0, BANK)] if t < PACK - 1 else [(NARROW, NARROW), (0, NARROW)]
             for j0, width in pieces:
                 cols = slice(j0, j0 + width)
                 nc.vector.tensor_tensor(product(t, j0, width), early_exp[:, t, cols], a_sum[:, cols], ALU.mult)
+        for t, share in enumerate(SECOND_SHARE):
+            if share < BANK:
+                nc.vector.tensor_tensor(
+                    product(t, BANK + share, BANK - share), late_exp[:, t, share:], late_sums[t][:, share:], ALU.mult
+                )
         round_first(1)
 
         def shift_range(n):
@@ -341,7 +340,9 @@ def tile_list_speaker_affine_flow_kernel(
             base = NARROW * (PACK, 0, PACK, 1)[n]
             h = h_second[:, base : base + PACK * width]
             for t in ([PACK - 1] + list(range(PACK - 1)) if n == 1 else range(PACK)):
-                shift(1, t, j0, width, h[:, t * width : (t + 1) * width], product(t, j0, width))
+                step = P if (n, t) == (len(RANGES) - 1, PACK - 1) else width
+                for c0 in range(0, width, step):
+                    shift(1, t, j0 + c0, step, h[:, t * width + c0 : t * width + c0 + step], product(t, j0 + c0, step))
                 if n == 2 and t == 0:
                     quantise_h(0, BANK, BANK, "h_round_first")
                 if n == len(RANGES) - 1 and t == PACK - 2:

@@ -1,6 +1,7 @@
 from contextlib import ExitStack
 
 import concourse.mybir as mybir
+from concourse.masks import make_identity
 
 K, C, H, N, T, S = 1024, 512, 1024, 512, 2048, 1024
 FLOPS = 2 * S * (K * H + C * H + H * N)
@@ -22,12 +23,8 @@ PASS = P * PACK
 BANK = 512
 NARROW = BANK // 2
 HALVES = H // PASS
-RING = 8
+RING = 7
 TAB_ROW = 4
-
-SECOND_SHARE = (BANK, BANK, P, 0)
-
-RANGES = [(j0, NARROW) for j0 in range(0, S, NARROW)]
 
 
 def tile_list_speaker_affine_flow_kernel(
@@ -38,12 +35,17 @@ def tile_list_speaker_affine_flow_kernel(
     with ExitStack() as ctx:
         keep = ctx.enter_context(tc.tile_pool(name="keep", bufs=1))
         ring = ctx.enter_context(tc.tile_pool(name="ring", bufs=RING))
-        stage = ctx.enter_context(tc.tile_pool(name="stage", bufs=2))
         psum_a = ctx.enter_context(tc.psum_pool(name="psum_a", bufs=4))
         psum_y = ctx.enter_context(tc.psum_pool(name="psum_y", bufs=4))
 
         def kept(shape, dtype, name):
             return keep.tile(shape, dtype, name=name, align_bytes=64)
+
+        def bank_a(shape):
+            return psum_a.tile(shape, F32, name="a_sum")
+
+        def bank_y(shape):
+            return psum_y.tile(shape, F32, name="y_sum")
 
         idx = keep.tile([P, S // 16], U16, name="idx")
         idx2 = keep.tile([P, S // 16], U16, name="idx2")
@@ -52,10 +54,11 @@ def tile_list_speaker_affine_flow_kernel(
         wb_plane = kept([P, H], U8, "wb_plane")
         w8_plane = kept([P, N], U8, "w8_plane")
         bias_sb = kept([P, N // P], F32, "bias_sb")
+        identity = kept([P, P], F32, "identity")
 
         for plane in (tab2_plane, tab_plane, wb_plane, w8_plane):
             nc.gpsimd.memset(plane[:].bitcast(I32), 0)
-
+        make_identity(nc, identity[:])
 
         def load_plane_by_quadrant(plane, scales):
             rows = 4 * scales.shape[0]
@@ -72,25 +75,26 @@ def tile_list_speaker_affine_flow_kernel(
                         out=plane[first + 4 * g + r : P : 32, :].bitcast(I32), in_=scales[g, r : 16 : 4, :].bitcast(I32)
                     )
 
-        def load_words(words):
-            window = ring.tile([P, T], U32, name="ring", align_bytes=64)
+        def load_words(words, pool, name):
+            window = pool.tile([P, T], U32, name=name, align_bytes=64)
             nc.sync.dma_start(out=window[:].bitcast(I32), in_=words.rearrange("p t i -> p (t i)").bitcast(I32))
             return window
 
-        def load_wa(half, g, pool=ring, name="ring"):
-            pieces = 2 if (half, g) == (0, 1) else 1
-            raw = pool.tile([P, pieces, PACK, PASS // pieces], F32, name=name, align_bytes=64)
-            rows = wa[g * PASS : (g + 1) * PASS, half * PASS : (half + 1) * PASS]
-            rows = rows.rearrange("(p i) (u r) -> u p i r", i=PACK, u=pieces)
-            for u in range(pieces):
-                nc.sync.dma_start(out=raw[:, u], in_=rows[u])
+        def load_wa(g, r0, width):
+            raw = kept([P, PACK, width], F32, "wa%d_%d" % (g, r0))
+            rows = wa[g * PASS : (g + 1) * PASS, r0 : r0 + width]
+            nc.sync.dma_start(out=raw[:], in_=rows.rearrange("(p i) r -> p i r", i=PACK))
             return raw
 
-        g_slots = gT.rearrange("(a p t) c -> a t p c", p=P, t=PACK)
+        g_rows = [
+            gT[0:PASS].rearrange("(t p) c -> t p c", p=P),
+            gT[PASS:H].rearrange("(p t) c -> t p c", t=PACK),
+        ]
 
         def load_g(half, t):
-            window = ring.tile([P, T], F32, name="ring", align_bytes=64)
-            nc.sync.dma_start(out=window[:], in_=g_slots[half, t])
+            pool, name = (keep, "g_first") if (half, t) == (0, 0) else (ring, "ring")
+            window = pool.tile([P, T], F32, name=name, align_bytes=64)
+            nc.sync.dma_start(out=window[:], in_=g_rows[half][t])
             return window
 
         tab_window, wa_raw, g_window = {}, {}, {}
@@ -99,22 +103,20 @@ def tile_list_speaker_affine_flow_kernel(
         nc.sync.dma_start(idx[:], offs)
         nc.sync.dma_start(out=wb_words[:].bitcast(I32), in_=wb4_words[0].bitcast(I32))
         load_plane_by_row(tab2_plane, tab2_scales, range(4))
-        tab2_window = load_words(tab2_words[0])
+        tab2_window = load_words(tab2_words[0], keep, "tab2")
         load_plane_by_quadrant(wb_plane, wb4_scales)
         load_plane_by_row(tab_plane, tab_scales, (0,), TAB_ROW)
-        wa_raw[0, 0] = load_wa(0, 0, keep, "wa00")
+        wa_raw[0, 0] = load_wa(0, 0, PASS)
         load_plane_by_row(tab_plane, tab_scales, (1, 2, 3), TAB_ROW)
-        tab_window[0] = load_words(tab_words[0])
-        wa_raw[0, 1] = load_wa(0, 1, keep, "wa01")
-        tab_window[1] = load_words(tab_words[1])
-        g_window[0, 0] = load_g(0, 0)
-        wa_raw[1, 0] = load_wa(1, 0)
-        wa_raw[1, 1] = load_wa(1, 1, keep, "wa11")
-        g_window[0, 1] = load_g(0, 1)
-        g_window[0, 2] = load_g(0, 2)
-        g_window[0, 3] = load_g(0, 3)
-        for t in range(PACK):
-            g_window[1, t] = load_g(1, t)
+        tab_window[0] = load_words(tab_words[0], ring, "ring")
+        wa_piece = [load_wa(1, 0, NARROW)]
+        tab_window[1] = load_words(tab_words[1], ring, "ring")
+        wa_piece.append(load_wa(1, NARROW, NARROW))
+        wa_raw[1, 0] = load_wa(0, PASS, PASS)
+        wa_raw[1, 1] = load_wa(1, PASS, PASS)
+        for half in range(HALVES):
+            for t in range(PACK):
+                g_window[half, t] = load_g(half, t)
         w8_codes = ring.tile([P, HALVES, N], U32, name="ring", align_bytes=64)
         nc.sync.dma_start(
             out=w8_codes[:].bitcast(I32),
@@ -124,58 +126,68 @@ def tile_list_speaker_affine_flow_kernel(
         with nc.allow_non_contiguous_dma(reason="one bias value for each partition and tile of rows"):
             nc.sync.dma_start(out=bias_sb[:], in_=bias.rearrange("(q p) -> p q", p=P))
 
-
         v2_scales = kept([P, S], U8, "v2_scales")
         v2_codes = kept([P, S], U32, "v2_codes")
         v_scales = kept([P, S], U8, "v_scales")
         v_codes = [[kept([P, BANK], U32, "v_codes%d%d" % (g, b)) for b in range(S // BANK)] for g in range(K // PASS)]
-        wb_codes = kept([P, 2 * H], U8, "wb_codes")
+        wb_codes = kept([P, 2 * PASS], U8, "wb_codes")
         h_scales = [kept([P, S], U8, "h_scales%d" % half) for half in range(HALVES)]
-        wa_q, h_round, h_codes = {}, {}, {}
+        wa_q = {
+            (half, g): (
+                kept([P, PASS], U32, "wa_codes%d%d" % (half, g) if half + g else "tab_plane"),
+                kept([P, PASS], U8, "wa_scales%d%d" % (half, g)),
+            )
+            for half in range(HALVES)
+            for g in range(K // PASS)
+        }
+        wa_grouped, h_round, h_codes = {}, {}, {}
 
         def offsets(j0, width):
             return idx[:, j0 // 16 : (j0 + width) // 16]
 
-        def gather_words(g):
-            cuts = (0, BANK, S) if g == 0 else (0, NARROW, BANK, S)
+        def gather_words(g, cuts):
             for j0, j1 in zip(cuts, cuts[1:]):
                 dest = v_codes[g][j0 // BANK][:, j0 % BANK : j0 % BANK + j1 - j0]
                 nc.vector.tensor_copy(dest, tab_window[g][:].indirect(offsets(j0, j1 - j0)))
 
-        def quantise_wa(half, g, name=None):
-            grouped = stage.tile([P, PASS * PACK], BF16, name="wa_grouped", align_bytes=64)
-            pieces = wa_raw[half, g].shape[1]
-            for u in range(pieces):
-                nc.scalar.copy(
-                    grouped[:].rearrange("p (t u m i) -> p u m i t", t=PACK, u=pieces, i=PACK)[:, u],
-                    wa_raw[half, g][:, u].rearrange("p i (m t) -> p m i t", t=PACK),
-                )
-            codes = kept([P, PASS], U32, name or "wa_codes%d%d" % (half, g))
-            scales = kept([P, PASS], U8, "wa_scales%d%d" % (half, g))
-            nc.vector.quantize_mx(out=codes[:].bitcast(FP8X4), scales=scales[:], in_=grouped[:])
-            wa_q[half, g] = codes, scales
+        def interleave(copy, grouped, rows):
+            copy(grouped.rearrange("p (c i t) -> p c t i", i=4, t=PACK), rows.rearrange("p t (c i) -> p c t i", i=4))
 
-        def mix_frames(half, t, j0, width, a_sum):
+        def round_on_gpsimd(grouped, rows):
+            nc.gpsimd.tensor_scalar(grouped, rows, 1.0, 0.0, ALU.mult, ALU.add)
+
+        def quantise_wa(half, g, r0, grouped):
+            codes, scales = wa_q[half, g]
+            width = grouped.shape[1] // PACK
+            nc.vector.quantize_mx(
+                out=codes[:, r0 : r0 + width].bitcast(FP8X4),
+                scales=scales[:, r0 : r0 + width],
+                in_=grouped[:],
+            )
+
+        def frames(half, t, j0, bank):
+            a_sum = bank([P, BANK])
             for g in range(K // PASS):
                 codes, scales = wa_q[half, g]
                 nc.tensor.matmul_mx(
-                    out=a_sum,
+                    out=a_sum[:],
                     lhsT=codes[:, t * P : (t + 1) * P].bitcast(FP8X4),
                     lhsT_scale=scales[:, t * P : (t + 1) * P],
-                    rhs=v_codes[g][j0 // BANK][:, j0 % BANK : j0 % BANK + width].bitcast(FP8X4),
-                    rhs_scale=v_scales[TAB_ROW + 4 * g :, j0 : j0 + width],
+                    rhs=v_codes[g][j0 // BANK][:].bitcast(FP8X4),
+                    rhs_scale=v_scales[TAB_ROW + 4 * g :, j0 : j0 + BANK],
                     start=(g == 0),
                     stop=(g == K // PASS - 1),
                 )
+            return a_sum
 
-        def speaker_scale(half, t, j0, dest, spare=False):
+        def speaker_scale(half, t, j0, dest):
             cols = slice(j0, j0 + BANK)
-            r0 = half * PASS + t * P
-            b_sum = psum_a.tile([P, BANK], F32, name="a_sum") if spare else psum_y.tile([P, BANK], F32, name="y_sum")
+            codes, scales = (wb_words, wb_plane) if half == 0 else (wb_codes, wb_scales)
+            b_sum = bank_y([P, BANK])
             nc.tensor.matmul_mx(
                 out=b_sum[:],
-                lhsT=wb_codes[:, 2 * r0 : 2 * (r0 + P)].bitcast(FP4X4),
-                lhsT_scale=wb_scales[:, r0 : r0 + P],
+                lhsT=codes[:, 2 * t * P : 2 * (t + 1) * P].bitcast(FP4X4),
+                lhsT_scale=scales[:, t * P : (t + 1) * P],
                 rhs=v2_codes[:, cols].bitcast(FP8X4),
                 rhs_scale=v2_scales[:, cols],
                 start=True,
@@ -183,31 +195,29 @@ def tile_list_speaker_affine_flow_kernel(
             )
             nc.scalar.activation(dest, b_sum[:], ACT.Exp)
 
-        def frames(half, t, j0, width, spare=False):
-            a_sum = psum_y.tile([P, width], F32, name="y_sum") if spare else psum_a.tile([P, width], F32, name="a_sum")
-            mix_frames(half, t, j0, width, a_sum[:])
-            return a_sum
+        def exponentials(units, name, spare=0):
+            cells = kept([P, (len(units) + spare) * BANK], F32, name)
+            for n, (half, t, b) in enumerate(units):
+                scale[half, t, b] = cells[:, n * BANK : (n + 1) * BANK]
+                speaker_scale(half, t, b * BANK, scale[half, t, b])
+            return cells
 
-        def shift(half, t, j0, width, dest, product):
-            nc.vector.tensor_tensor(dest, g_window[half, t][:].indirect(offsets(j0, width)), product, ALU.add)
+        def shift(t, j0, width, dest, product):
+            nc.vector.tensor_tensor(dest, g_window[1, t][:].indirect(offsets(j0, width)), product, ALU.add)
 
-        def round_h(copy, h, slots):
-            copy(h.rearrange("p (c i t) -> p c t i", i=4, t=PACK), slots.rearrange("p t (c i) -> p c t i", i=4))
-
-        def quantise_h(half, j0, width, name=None):
-            h_codes[half, j0] = kept([P, width], U32, name or "h_codes%d_%d" % (half, j0))
+        def quantise_h(half, j0, width, name):
+            h_codes[half, j0] = kept([P, width], U32, name)
             nc.vector.quantize_mx(
                 out=h_codes[half, j0][:].bitcast(FP8X4),
                 scales=h_scales[half][:, j0 : j0 + width],
                 in_=h_round[half, j0][:],
             )
 
-        def features(j0, width, pool, name):
+        def features(j0, width, bank, name):
             cols = slice(j0, j0 + width)
-            y = kept([P, N // P, width], F32, "y%d" % j0)
-            group = 1 if width == BANK else 2
+            y = kept([P, N // P, width], F32, name)
             for q in range(N // P):
-                y_sum = pool.tile([P, width], F32, name=name)
+                y_sum = bank([P, width])
                 for half in range(HALVES):
                     base = j0 if half == 1 else j0 // BANK * BANK
                     nc.tensor.matmul_mx(
@@ -223,154 +233,194 @@ def tile_list_speaker_affine_flow_kernel(
                     nc.vector.tensor_scalar_add(y[:, q], y_sum[:], bias_sb[:, q : q + 1])
                 else:
                     nc.scalar.activation(y[:, q], y_sum[:], ACT.Identity, bias=bias_sb[:, q : q + 1])
-                if (q + 1) % group == 0:
-                    rows = slice(q + 1 - group, q + 1)
+                if q % 2 == 1:
+                    rows = slice(q - 1, q + 1)
                     nc.sync.dma_start(out=out.rearrange("(q p) j -> p q j", p=P)[:, rows, cols], in_=y[:, rows])
 
-
-        nc.vector.tensor_copy(v2_scales[:], tab2_plane[:].indirect(idx2[:]))
-        nc.vector.tensor_copy(v2_codes[:], tab2_window[:].indirect(idx2[:]))
-        wb_scales = kept([P, H], U8, "wb_scales")
+        scale = {}
         nc.vector.tensor_copy(
-            wb_scales[:].rearrange("p (a t m) -> p a t m", t=PACK, m=P),
-            wb_plane[:].rearrange("p (a m t) -> p a t m", t=PACK, m=P),
+            wb_codes[:].bitcast(U16).rearrange("p (t m) -> p t m", t=PACK),
+            wb_words[:, 2 * PASS :].bitcast(U16).rearrange("p (m t) -> p t m", t=PACK),
+        )
+        nc.vector.tensor_copy(v2_scales[:], tab2_plane[:].indirect(idx2[:]))
+        for j0 in range(0, S, BANK):
+            nc.vector.tensor_copy(
+                v2_codes[:, j0 : j0 + BANK], tab2_window[:].indirect(idx2[:, j0 // 16 : (j0 + BANK) // 16])
+            )
+        wb_scales = kept([P, PASS], U8, "wb_scales")
+        nc.vector.tensor_copy(
+            wb_scales[:].rearrange("p (t m) -> p t m", t=PACK),
+            wb_plane[:, PASS:].rearrange("p (m t) -> p t m", t=PACK),
         )
         nc.vector.tensor_copy(v_scales[:], tab_plane[:].indirect(idx[:]))
-        quantise_wa(0, 0)
-        nc.vector.tensor_copy(
-            wb_codes[:].bitcast(U16).rearrange("p (a t m) -> p a t m", t=PACK, m=P),
-            wb_words[:].bitcast(U16).rearrange("p (a m t) -> p a t m", t=PACK, m=P),
+        wa_grouped[0, 0] = kept([P, PASS * PACK], BF16, "tab2")
+        round_on_gpsimd(
+            wa_grouped[0, 0][:].rearrange("p (r i) -> p r i", i=PACK), wa_raw[0, 0][:].rearrange("p i r -> p r i")
         )
-        gather_words(0)
-        quantise_wa(0, 1)
-        gather_words(1)
+        gather_words(0, (0, BANK, S))
+        quantise_wa(0, 0, 0, wa_grouped[0, 0])
+        grouped_piece = [kept([P, NARROW * PACK], BF16, "grouped_piece%d" % u) for u in range(2)]
+        for u in range(2):
+            interleave(nc.scalar.copy, grouped_piece[u][:], wa_piece[u][:])
+        quantise_wa(0, 1, 0, grouped_piece[0])
+        gather_words(1, (0, BANK, S))
 
-
-        even = kept([P, 2, S], F32, "first_even")
-        first = {(2 * n, b): even[:, n, b * BANK : (b + 1) * BANK] for n in range(2) for b in range(S // BANK)}
-        for t in range(1, PACK, 2):
-            for b in range(S // BANK):
-                first[t, b] = kept([P, BANK], F32, "first%d%d" % (t, b))[:]
-        ahead = [(0, 0), (2, 0), (1, 0)]
-        behind = [(t, b) for b in range(S // BANK) for t in range(PACK) if (t, b) not in ahead]
-        first_exp = {}
-
-        def first_exps(units, name):
-            cells = kept([P, len(units), BANK], F32, name)
+        first_units = [(0, 0), (1, 0), (0, 1), (1, 1), (2, 0), (3, 0), (2, 1), (3, 1)]
+        exponentials([(0, t, b) for t, b in first_units[:-1]], "first_early")
+        early = exponentials([(0, 3, 1), (1, 0, 0), (1, 0, 1), (1, 3, 1)], "wa1_0")
+        middle = exponentials([(1, 1, 0), (1, 2, 0)], "wa1_256", 2)
+        def first_products(units, held=None):
             for n, (t, b) in enumerate(units):
-                first_exp[t, b] = cells[:, n, :]
-                speaker_scale(0, t, b * BANK, first_exp[t, b], (t, b) in behind[-1:])
-            return cells
+                a_sum = frames(0, t, b * BANK, bank_a)
+                product = scale[0, t, b] if held is None else held[:, n * BANK : (n + 1) * BANK]
+                nc.vector.tensor_tensor(product, scale[0, t, b], a_sum[:], ALU.mult)
+                scale[0, t, b] = product
 
-        ahead_exp = first_exps(ahead, "wa00")
-        sums = {}
-        for n, j0 in enumerate(range(0, BANK, NARROW)):
-            a_sum = psum_a.tile([P, 2, NARROW], F32, name="a_sum")
-            for m in range(2):
-                mix_frames(0, 2 * m, j0, NARROW, a_sum[:, m])
-            aside = kept([P, 2, NARROW], F32, "first_aside%d" % n)
-            nc.scalar.copy(aside[:], a_sum[:])
-            cols = slice(j0, j0 + NARROW)
-            nc.gpsimd.tensor_tensor(even[:, :, cols], ahead_exp[:, 0:2, cols], aside[:], ALU.mult)
-            sums[2 * n + 1, 0] = frames(0, 2 * n + 1, 0, BANK)
-        first_exps(behind, "wa01")
-        for t, b in list(sums) + [(t, 1) for t in range(PACK)]:
-            a_sum = sums[t, b] if b == 0 else frames(0, t, BANK, BANK, True)
-            nc.vector.tensor_tensor(first[t, b], first_exp[t, b], a_sum[:], ALU.mult)
+        def round_shared(g):
+            wa_grouped[1, g] = kept([P, PASS * PACK], BF16, "grouped_piece1")
+            nc.scalar.copy(
+                wa_grouped[1, g][:].rearrange("p (t m i) -> p m i t", t=PACK, i=PACK)[:, :, :, 0:2],
+                wa_raw[1, g][:].rearrange("p i (m t) -> p m i t", t=PACK)[:, :, :, 0:2],
+            )
+            round_on_gpsimd(
+                wa_grouped[1, g][:].rearrange("p (t m i) -> p t m i", t=PACK, i=PACK)[:, 2:],
+                wa_raw[1, g][:].rearrange("p i (m t) -> p t m i", t=PACK)[:, 2:],
+            )
 
-        h_first = kept([P, PACK, S], F32, "wa00")
+        first_products(first_units[0:2])
+        quantise_wa(0, 1, NARROW, grouped_piece[1])
+        first_products(first_units[2:4], middle[:, S:])
+        first_products(first_units[4:6])
+        round_shared(0)
+        quantise_wa(1, 0, 0, wa_grouped[1, 0])
+        late = exponentials([(1, 1, 1), (1, 2, 1)], "wa0_512", 2)
+        first_products(first_units[6:8], late[:, S:])
+        round_shared(1)
+        quantise_wa(1, 1, 0, wa_grouped[1, 1])
+        exponentials([(1, 3, 0)], "wa1_512")
 
-        def shift_first(t, b):
-            shift(0, t, b * BANK, BANK, h_first[:, t, b * BANK : (b + 1) * BANK], first[t, b])
+        aside = kept([P, 4 * BANK], F32, "aside")
+        aside_late = kept([P, 2 * BANK], F32, "aside_late")
+        for pair, (exps, copies) in enumerate(((early[:, BANK:], aside), (middle, aside[:, S:]), (late, aside_late))):
+            units = (((0, 0), (0, 1)), ((1, 0), (2, 0)), ((1, 1), (2, 1)))[pair]
+            for n, (t, b) in enumerate(units):
+                a_sum = frames(1, t, b * BANK, bank_a)
+                nc.scalar.copy(copies[:, n * BANK : (n + 1) * BANK], a_sum[:])
+            nc.gpsimd.tensor_tensor(exps[:, 0:S], exps[:, 0:S], copies[:, 0:S], ALU.mult)
 
-        def round_first(b):
-            h_round[0, b * BANK] = stage.tile([P, BANK * PACK], BF16, name="h", align_bytes=64)
-            round_h(nc.scalar.copy, h_round[0, b * BANK][:], h_first[:, :, b * BANK : (b + 1) * BANK])
+            if pair == 0:
+                last_sums = [frames(1, PACK - 1, b * BANK, bank_y) for b in range(S // BANK)]
 
-        shift(0, 0, 0, S, h_first[:, 0, :], even[:, 0, :])
-        quantise_wa(1, 0)
-        shift_first(1, 0)
-        shift_first(1, 1)
-        quantise_wa(1, 1, "first10")
-        second_exp = kept([P, S // BANK, PACK, BANK], F32, "wa11")
-        early_exp, late_exp = second_exp[:, 0], second_exp[:, 1]
-        for t in range(PACK):
-            speaker_scale(1, t, BANK, late_exp[:, t, :])
-        late_sums = [frames(1, t, BANK, BANK) for t in range(PACK)]
-        shared = sum(SECOND_SHARE)
-        aside = kept([P, shared], F32, "second_aside")
-        for t, share in enumerate(SECOND_SHARE):
-            if share > 0:
-                nc.scalar.copy(aside[:, t * BANK : t * BANK + share], late_sums[t][:, 0:share])
-        for t in range(PACK):
-            speaker_scale(1, t, 0, early_exp[:, t, :])
-        shift(0, 2, 0, S, h_first[:, 2, :], even[:, 1, :])
-        shift_first(3, 0)
-        round_first(0)
-        shift_first(3, 1)
+        picked = {}
 
+        def pick(t, name, cuts):
+            picked[t] = kept([P, S], F32, name)
+            for j0, j1 in zip(cuts, cuts[1:]):
+                nc.vector.tensor_copy(picked[t][:, j0:j1], g_window[0, t][:].indirect(offsets(j0, j1 - j0)))
 
-        early = kept([P, PACK * BANK], F32, "first30")
-        h_second = kept([P, 2 * PACK * NARROW + PACK * BANK], F32, "first31")
-        corner = h_second[:, P : P + NARROW]
-        late = h_second[:, 2 * PACK * NARROW :]
+        pick(0, "picked0", (0, S))
+        cells = kept([P, 20 * NARROW], F32, "g_first")
 
-        def product(t, j0, width):
-            if (t, j0) == (PACK - 1, 0):
-                return corner
-            c0 = t * BANK + j0 % BANK
-            return (early if j0 < BANK else late)[:, c0 : c0 + width]
+        def cell(n, count=1):
+            return cells[:, n * NARROW : (n + count) * NARROW]
 
-        nc.gpsimd.tensor_tensor(late[:, 0:shared], late_exp.rearrange("p t c -> p (t c)")[:, 0:shared], aside[:], ALU.mult)
-        for t in range(PACK):
-            a_sum = frames(1, t, 0, BANK, t >= 2)
-            pieces = [(0, BANK)] if t < PACK - 1 else [(NARROW, NARROW), (0, NARROW)]
-            for j0, width in pieces:
-                cols = slice(j0, j0 + width)
-                nc.vector.tensor_tensor(product(t, j0, width), early_exp[:, t, cols], a_sum[:, cols], ALU.mult)
-        for t, share in enumerate(SECOND_SHARE):
-            if share < BANK:
-                nc.vector.tensor_tensor(
-                    product(t, BANK + share, BANK - share), late_exp[:, t, share:], late_sums[t][:, share:], ALU.mult
+        nc.vector.tensor_tensor(cell(10, 2), scale[1, 3, 0], last_sums[0][:], ALU.mult)
+        scale[1, 3, 0] = cell(10, 2)
+        nc.vector.tensor_tensor(cell(13), scale[1, 3, 1][:, NARROW:], last_sums[1][:, NARROW:], ALU.mult)
+        last_third = kept([P, NARROW], F32, "wa1_512")
+        nc.vector.tensor_tensor(last_third[:], scale[1, 3, 1][:, 0:NARROW], last_sums[1][:, 0:NARROW], ALU.mult)
+        pick(1, "grouped_piece1", (0, S))
+        pick(2, "picked", (0, S))
+        pick(3, "picked3", (0, BANK, S))
+
+        turned = kept([P, S // P, 2, 2 * P], BF16, "tab2")
+
+        def add_turned(t, b):
+            h_sum = (bank_y if t == PACK - 1 else bank_a)([P, BANK // P, P])
+            for n, source in enumerate((scale[0, t, b], picked[t][:, b * BANK : (b + 1) * BANK])):
+                for c in range(BANK // P):
+                    nc.tensor.matmul(
+                        h_sum[:, c], source[:, c * P : (c + 1) * P], identity[:], is_transpose=True,
+                        start=(n, c) == (0, 0), stop=(n, c) == (1, BANK // P - 1),
+                    )
+            nc.scalar.copy(
+                turned[:, 4 * b : 4 * b + 4, :, 64 * t : 64 * (t + 1)].rearrange("p c u (w e) -> p c u w e", e=2),
+                h_sum[:].rearrange("p c (w u e) -> p c u w e", u=2, e=2),
+            )
+
+        def turn_back(b):
+            h_round[0, b * BANK] = kept([P, BANK * PACK], BF16, "h_first%d" % b)
+            words = h_round[0, b * BANK][:].bitcast(F32)
+            for n in range(2):
+                pairs = bank_y([P, 2, 2, P])
+                for c in range(2):
+                    for u in range(2):
+                        nc.tensor.transpose(pairs[:, c, u], turned[:, 4 * b + 2 * n + c, u].bitcast(F32), identity[:])
+                nc.scalar.copy(
+                    words[:, n * BANK : (n + 1) * BANK].rearrange("p (c j u) -> p c j u", c=2, u=2),
+                    pairs[:].rearrange("p c u j -> p c j u"),
                 )
-        round_first(1)
 
-        def shift_range(n):
-            j0, width = RANGES[n]
-            base = NARROW * (PACK, 0, PACK, 1)[n]
-            h = h_second[:, base : base + PACK * width]
-            for t in ([PACK - 1] + list(range(PACK - 1)) if n == 1 else range(PACK)):
-                step = P if (n, t) == (len(RANGES) - 1, PACK - 1) else width
-                for c0 in range(0, width, step):
-                    shift(1, t, j0 + c0, step, h[:, t * width + c0 : t * width + c0 + step], product(t, j0 + c0, step))
-                if n == 2 and t == 0:
-                    quantise_h(0, BANK, BANK, "h_round_first")
-                if n == len(RANGES) - 1 and t == PACK - 2:
-                    finish(n - 1)
-            return h.rearrange("p (t c) -> p t c", t=PACK)
+        for t in range(PACK - 1):
+            for b in range(S // BANK):
+                add_turned(t, b)
+        for b in range(S // BANK):
+            add_turned(PACK - 1, b)
+        for b in range(S // BANK):
+            turn_back(b)
 
-        def finish(n):
-            j0, width = RANGES[n]
-            quantise_h(1, j0, width)
-            features(j0, width, psum_y, "y_sum")
+        places = ((1, 4, 2), (2, 4, 2), (9, 2, 1), (0, 10, 2))
 
-        quantise_h(0, 0, BANK)
-        for n, (j0, width) in enumerate(RANGES[:-1]):
-            if n == 2:
-                finish(0)
-            h = shift_range(n)
-            h_round[1, j0] = kept([P, width * PACK], BF16, ("h_round_first", "h_round1", "h_codes1_0")[n])
-            round_h(nc.scalar.copy, h_round[1, j0][:], h)
-        finish(1)
-        h = shift_range(len(RANGES) - 1)
+        def place(n, t):
+            base, far, near = places[n]
+            return cell(base + far * (t // 2) + near * (t % 2))
 
+        def slots(n):
+            base, far, near = places[n]
+            return cell(base, 2 * far).rearrange("p (a b c) -> p a b c", a=2, c=NARROW)[:, :, 0 : near + 1 : near, :]
 
-        last = RANGES[-1][0]
+        def round_second(copy, j0, width, name):
+            n = j0 // NARROW
+            h_round[1, j0] = kept([P, width * PACK], BF16, name)
+            c0 = j0 % NARROW
+            copy(
+                h_round[1, j0][:].rearrange("p (c i a b) -> p c a b i", i=4, a=2, b=2),
+                slots(n)[:, :, :, c0 : c0 + width].rearrange("p a b (c i) -> p c a b i", i=4),
+            )
+
+        def shift_narrow(n, t):
+            b, c0 = divmod(n * NARROW, BANK)
+            shift(t, n * NARROW, NARROW, place(n, t), scale[1, t, b][:, c0 : c0 + NARROW])
+
+        shift(0, 0, BANK, cell(1, 2), scale[1, 0, 0])
+        shift_narrow(2, 0)
+        shift_narrow(3, 0)
+        shift(1, 0, BANK, cell(3, 2), scale[1, 1, 0])
+        shift(2, 0, BANK, cell(5, 2), scale[1, 2, 0])
+        for n in range(2):
+            shift_narrow(n, 3)
+            round_second(nc.scalar.copy, n * NARROW, NARROW, "h_round%d" % n)
+        shift(3, BANK, NARROW, place(2, 3), last_third[:])
+        shift_narrow(2, 1)
+        shift_narrow(2, 2)
+        round_second(nc.scalar.copy, BANK, NARROW, "h_round2")
+        quantise_h(0, 0, BANK, "wa1_512")
+        quantise_h(1, 0, NARROW, "h_codes1_0")
+        features(0, NARROW, bank_y, "first_early")
+        quantise_h(1, NARROW, NARROW, "h_codes1_1")
+        features(NARROW, NARROW, bank_a, "wa1_0")
+        shift_narrow(3, 1)
+        quantise_h(0, BANK, BANK, "h_round1")
+        quantise_h(1, BANK, NARROW, "h_codes1_2")
+        features(BANK, NARROW, bank_y, "aside")
+        shift_narrow(3, 2)
+        last = S - NARROW
         for j0 in range(last, S, P):
-            h_round[1, j0] = kept([P, P * PACK], BF16, "h_last%d" % j0)
-            round_h(nc.vector.tensor_copy, h_round[1, j0][:], h[:, :, j0 - last : j0 - last + P])
+            c0 = j0 - last
+            shift(3, j0, P, place(3, 3)[:, c0 : c0 + P], cell(13)[:, c0 : c0 + P])
         for j0 in range(last, S, P):
-            quantise_h(1, j0, P)
+            round_second(nc.vector.tensor_copy, j0, P, "h_last%d" % j0)
         for j0 in range(last, S, P):
-            pool, name = (psum_a, "a_sum") if j0 == last else (psum_y, "y_sum")
-            features(j0, P, pool, name)
+            quantise_h(1, j0, P, "h_codes1_%d" % j0)
+        for j0 in range(last, S, P):
+            features(j0, P, bank_a if j0 == last else bank_y, "y%d" % j0)

@@ -23,7 +23,7 @@ PASS = P * PACK
 BANK = 512
 NARROW = BANK // 2
 HALVES = H // PASS
-RING = 7
+RING = 6
 TAB_ROW = 4
 
 
@@ -108,7 +108,7 @@ def tile_list_speaker_affine_flow_kernel(
         load_plane_by_row(tab_plane, tab_scales, (0,), TAB_ROW)
         wa_raw[0, 0] = load_wa(0, 0, PASS)
         load_plane_by_row(tab_plane, tab_scales, (1, 2, 3), TAB_ROW)
-        tab_window[0] = load_words(tab_words[0], ring, "ring")
+        tab_window[0] = load_words(tab_words[0], keep, "tab0")
         wa_piece = [load_wa(1, 0, NARROW)]
         tab_window[1] = load_words(tab_words[1], ring, "ring")
         wa_piece.append(load_wa(1, NARROW, NARROW))
@@ -134,13 +134,13 @@ def tile_list_speaker_affine_flow_kernel(
         h_scales = [kept([P, S], U8, "h_scales%d" % half) for half in range(HALVES)]
         wa_q = {
             (half, g): (
-                kept([P, PASS], U32, "wa_codes%d%d" % (half, g) if half + g else "tab_plane"),
+                kept([P, PASS], U32, "wa_codes%d%d" % (half, g) if half + g else "tab0"),
                 kept([P, PASS], U8, "wa_scales%d%d" % (half, g)),
             )
             for half in range(HALVES)
             for g in range(K // PASS)
         }
-        wa_grouped, h_round, h_codes = {}, {}, {}
+        wa_grouped, h_round, h_codes, y_sums = {}, {}, {}, {}
 
         def offsets(j0, width):
             return idx[:, j0 // 16 : (j0 + width) // 16]
@@ -213,22 +213,29 @@ def tile_list_speaker_affine_flow_kernel(
                 in_=h_round[half, j0][:],
             )
 
-        def features(j0, width, bank, name):
+        def feature_pass(half, j0, width, y_sum, q):
+            base = j0 if half == 1 else j0 // BANK * BANK
+            nc.tensor.matmul_mx(
+                out=y_sum[:],
+                lhsT=w8_codes[:, half, q * P : (q + 1) * P].bitcast(FP8X4),
+                lhsT_scale=w8_plane[4 * half :, q * P : (q + 1) * P],
+                rhs=h_codes[half, base][:, j0 - base : j0 - base + width].bitcast(FP8X4),
+                rhs_scale=h_scales[half][:, j0 : j0 + width],
+                start=(half == 0),
+                stop=(half == HALVES - 1),
+            )
+
+        def open_features(j0, width, bank):
+            y_sums[j0] = [bank([P, width]) for q in range(N // P)]
+            for q in range(N // P):
+                feature_pass(0, j0, width, y_sums[j0][q], q)
+
+        def features(j0, width, name):
             cols = slice(j0, j0 + width)
             y = kept([P, N // P, width], F32, name)
             for q in range(N // P):
-                y_sum = bank([P, width])
-                for half in range(HALVES):
-                    base = j0 if half == 1 else j0 // BANK * BANK
-                    nc.tensor.matmul_mx(
-                        out=y_sum[:],
-                        lhsT=w8_codes[:, half, q * P : (q + 1) * P].bitcast(FP8X4),
-                        lhsT_scale=w8_plane[4 * half :, q * P : (q + 1) * P],
-                        rhs=h_codes[half, base][:, j0 - base : j0 - base + width].bitcast(FP8X4),
-                        rhs_scale=h_scales[half][:, cols],
-                        start=(half == 0),
-                        stop=(half == HALVES - 1),
-                    )
+                y_sum = y_sums[j0][q]
+                feature_pass(1, j0, width, y_sum, q)
                 if width == P and q % 2 == 1:
                     nc.vector.tensor_scalar_add(y[:, q], y_sum[:], bias_sb[:, q : q + 1])
                 else:
@@ -266,50 +273,46 @@ def tile_list_speaker_affine_flow_kernel(
         gather_words(1, (0, BANK, S))
 
         first_units = [(0, 0), (1, 0), (0, 1), (1, 1), (2, 0), (3, 0), (2, 1), (3, 1)]
-        exponentials([(0, t, b) for t, b in first_units[:-1]], "first_early")
-        early = exponentials([(0, 3, 1), (1, 0, 0), (1, 0, 1), (1, 3, 1)], "wa1_0")
-        middle = exponentials([(1, 1, 0), (1, 2, 0)], "wa1_256", 2)
-        def first_products(units, held=None):
+        exponentials([(0, t, b) for t, b in first_units[:6]], "first_early")
+        early = exponentials([(0, t, b) for t, b in first_units[6:]] + [(1, 0, 0), (1, 0, 1)], "wa1_0")
+
+        def first_products(units, bank, held=None):
             for n, (t, b) in enumerate(units):
-                a_sum = frames(0, t, b * BANK, bank_a)
+                a_sum = frames(0, t, b * BANK, bank)
                 product = scale[0, t, b] if held is None else held[:, n * BANK : (n + 1) * BANK]
                 nc.vector.tensor_tensor(product, scale[0, t, b], a_sum[:], ALU.mult)
                 scale[0, t, b] = product
 
-        def round_shared(g):
-            wa_grouped[1, g] = kept([P, PASS * PACK], BF16, "grouped_piece1")
-            nc.scalar.copy(
-                wa_grouped[1, g][:].rearrange("p (t m i) -> p m i t", t=PACK, i=PACK)[:, :, :, 0:2],
-                wa_raw[1, g][:].rearrange("p i (m t) -> p m i t", t=PACK)[:, :, :, 0:2],
-            )
-            round_on_gpsimd(
-                wa_grouped[1, g][:].rearrange("p (t m i) -> p t m i", t=PACK, i=PACK)[:, 2:],
-                wa_raw[1, g][:].rearrange("p i (m t) -> p t m i", t=PACK)[:, 2:],
-            )
-
-        first_products(first_units[0:2])
+        first_products(first_units[0:2], bank_a)
         quantise_wa(0, 1, NARROW, grouped_piece[1])
-        first_products(first_units[2:4], middle[:, S:])
-        first_products(first_units[4:6])
-        round_shared(0)
+        first_products(first_units[2:4], bank_y, kept([P, S], F32, "wa1_256"))
+        first_products(first_units[4:6], bank_y)
+        for g in range(K // PASS):
+            wa_grouped[1, g] = kept([P, PASS * PACK], BF16, "grouped1%d" % g)
+            nc.scalar.copy(
+                wa_grouped[1, g][:].rearrange("p (t m i) -> p m i t", t=PACK, i=PACK),
+                wa_raw[1, g][:].rearrange("p i (m t) -> p m i t", t=PACK),
+            )
+        first_products(first_units[6:7], bank_y)
         quantise_wa(1, 0, 0, wa_grouped[1, 0])
-        late = exponentials([(1, 1, 1), (1, 2, 1)], "wa0_512", 2)
-        first_products(first_units[6:8], late[:, S:])
-        round_shared(1)
+        first_products(first_units[7:8], bank_y, kept([P, BANK], F32, "wa0_512"))
         quantise_wa(1, 1, 0, wa_grouped[1, 1])
-        exponentials([(1, 3, 0)], "wa1_512")
 
         aside = kept([P, 4 * BANK], F32, "aside")
         aside_late = kept([P, 2 * BANK], F32, "aside_late")
-        for pair, (exps, copies) in enumerate(((early[:, BANK:], aside), (middle, aside[:, S:]), (late, aside_late))):
-            units = (((0, 0), (0, 1)), ((1, 0), (2, 0)), ((1, 1), (2, 1)))[pair]
+
+        def share(exps, copies, units, product=None):
             for n, (t, b) in enumerate(units):
                 a_sum = frames(1, t, b * BANK, bank_a)
                 nc.scalar.copy(copies[:, n * BANK : (n + 1) * BANK], a_sum[:])
-            nc.gpsimd.tensor_tensor(exps[:, 0:S], exps[:, 0:S], copies[:, 0:S], ALU.mult)
+            nc.gpsimd.tensor_tensor(exps if product is None else product, exps, copies, ALU.mult)
 
-            if pair == 0:
-                last_sums = [frames(1, PACK - 1, b * BANK, bank_y) for b in range(S // BANK)]
+        share(early[:, S:], aside[:, 0:S], ((0, 0), (0, 1)))
+        late = exponentials([(1, 3, 0), (1, 3, 1), (1, 1, 0), (1, 2, 0), (1, 1, 1), (1, 2, 1)], "wa1_512")
+        last_sums = [frames(1, PACK - 1, b * BANK, bank_a) for b in range(S // BANK)]
+        middle = kept([P, S], F32, "middle")
+        share(late[:, S : 2 * S], aside[:, S:], ((1, 0), (2, 0)), middle[:])
+        scale[1, 1, 0], scale[1, 2, 0] = middle[:, 0:BANK], middle[:, BANK:]
 
         picked = {}
 
@@ -318,18 +321,16 @@ def tile_list_speaker_affine_flow_kernel(
             for j0, j1 in zip(cuts, cuts[1:]):
                 nc.vector.tensor_copy(picked[t][:, j0:j1], g_window[0, t][:].indirect(offsets(j0, j1 - j0)))
 
-        pick(0, "picked0", (0, S))
-        cells = kept([P, 20 * NARROW], F32, "g_first")
+        pick(0, "grouped10", (0, S))
+        cells = kept([P, 13 * NARROW], F32, "g_first")
 
         def cell(n, count=1):
             return cells[:, n * NARROW : (n + count) * NARROW]
 
-        nc.vector.tensor_tensor(cell(10, 2), scale[1, 3, 0], last_sums[0][:], ALU.mult)
-        scale[1, 3, 0] = cell(10, 2)
-        nc.vector.tensor_tensor(cell(13), scale[1, 3, 1][:, NARROW:], last_sums[1][:, NARROW:], ALU.mult)
-        last_third = kept([P, NARROW], F32, "wa1_512")
-        nc.vector.tensor_tensor(last_third[:], scale[1, 3, 1][:, 0:NARROW], last_sums[1][:, 0:NARROW], ALU.mult)
-        pick(1, "grouped_piece1", (0, S))
+        for b, first in enumerate((1, 11)):
+            nc.vector.tensor_tensor(cell(first, 2), scale[1, 3, b], last_sums[b][:], ALU.mult)
+            scale[1, 3, b] = cell(first, 2)
+        pick(1, "grouped11", (0, S))
         pick(2, "picked", (0, S))
         pick(3, "picked3", (0, BANK, S))
 
@@ -361,15 +362,25 @@ def tile_list_speaker_affine_flow_kernel(
                     pairs[:].rearrange("p c u j -> p c j u"),
                 )
 
-        for t in range(PACK - 1):
-            for b in range(S // BANK):
-                add_turned(t, b)
+        def set_aside(n):
+            a_sum = frames(1, n + 1, BANK, bank_a)
+            nc.scalar.copy(aside_late[:, n * BANK : (n + 1) * BANK], a_sum[:])
+
+        add_turned(0, 0)
+        add_turned(0, 1)
+        set_aside(0)
+        add_turned(1, 0)
+        set_aside(1)
+        nc.gpsimd.tensor_tensor(late[:, 2 * S :], late[:, 2 * S :], aside_late[:], ALU.mult)
+        add_turned(1, 1)
+        add_turned(2, 0)
+        add_turned(2, 1)
         for b in range(S // BANK):
             add_turned(PACK - 1, b)
         for b in range(S // BANK):
             turn_back(b)
 
-        places = ((1, 4, 2), (2, 4, 2), (9, 2, 1), (0, 10, 2))
+        places = ((3, 4, 2), (4, 4, 2), (0, 2, 1), (3, 2, 1))
 
         def place(n, t):
             base, far, near = places[n]
@@ -392,35 +403,39 @@ def tile_list_speaker_affine_flow_kernel(
             b, c0 = divmod(n * NARROW, BANK)
             shift(t, n * NARROW, NARROW, place(n, t), scale[1, t, b][:, c0 : c0 + NARROW])
 
-        shift(0, 0, BANK, cell(1, 2), scale[1, 0, 0])
+        shift(0, 0, BANK, cell(3, 2), scale[1, 0, 0])
         shift_narrow(2, 0)
-        shift_narrow(3, 0)
-        shift(1, 0, BANK, cell(3, 2), scale[1, 1, 0])
-        shift(2, 0, BANK, cell(5, 2), scale[1, 2, 0])
+        shift(1, 0, BANK, cell(5, 2), scale[1, 1, 0])
+        shift(2, 0, BANK, cell(7, 2), scale[1, 2, 0])
+        quantise_h(0, 0, BANK, "middle")
+        open_features(0, NARROW, bank_y)
         for n in range(2):
             shift_narrow(n, 3)
             round_second(nc.scalar.copy, n * NARROW, NARROW, "h_round%d" % n)
-        shift(3, BANK, NARROW, place(2, 3), last_third[:])
         shift_narrow(2, 1)
         shift_narrow(2, 2)
-        round_second(nc.scalar.copy, BANK, NARROW, "h_round2")
-        quantise_h(0, 0, BANK, "wa1_512")
         quantise_h(1, 0, NARROW, "h_codes1_0")
-        features(0, NARROW, bank_y, "first_early")
+        features(0, NARROW, "first_early")
+        open_features(NARROW, NARROW, bank_a)
+        shift_narrow(2, 3)
+        round_second(nc.scalar.copy, BANK, NARROW, "h_codes1_0")
+        quantise_h(0, BANK, BANK, "h_round0")
+        open_features(BANK, NARROW, bank_y)
         quantise_h(1, NARROW, NARROW, "h_codes1_1")
-        features(NARROW, NARROW, bank_a, "wa1_0")
-        shift_narrow(3, 1)
-        quantise_h(0, BANK, BANK, "h_round1")
+        features(NARROW, NARROW, "wa0_0")
+        open_features(S - NARROW, P, bank_a)
+        for t in range(1, PACK):
+            shift_narrow(3, t)
         quantise_h(1, BANK, NARROW, "h_codes1_2")
-        features(BANK, NARROW, bank_y, "aside")
-        shift_narrow(3, 2)
+        features(BANK, NARROW, "aside")
+        open_features(S - P, P, bank_y)
         last = S - NARROW
         for j0 in range(last, S, P):
             c0 = j0 - last
-            shift(3, j0, P, place(3, 3)[:, c0 : c0 + P], cell(13)[:, c0 : c0 + P])
+            shift(0, j0, P, place(3, 0)[:, c0 : c0 + P], scale[1, 0, 1][:, NARROW + c0 : NARROW + c0 + P])
         for j0 in range(last, S, P):
             round_second(nc.vector.tensor_copy, j0, P, "h_last%d" % j0)
         for j0 in range(last, S, P):
             quantise_h(1, j0, P, "h_codes1_%d" % j0)
         for j0 in range(last, S, P):
-            features(j0, P, bank_a if j0 == last else bank_y, "y%d" % j0)
+            features(j0, P, "y%d" % j0)

@@ -92,7 +92,7 @@ def tile_list_speaker_affine_flow_kernel(
         ]
 
         def load_g(half, t):
-            pool, name = (keep, "g_first") if (half, t) == (0, 0) else (ring, "ring")
+            pool, name = (keep, "g_held") if (half, t) == (0, 3) else (ring, "ring")
             window = pool.tile([P, T], F32, name=name, align_bytes=64)
             nc.sync.dma_start(out=window[:], in_=g_rows[half][t])
             return window
@@ -180,10 +180,10 @@ def tile_list_speaker_affine_flow_kernel(
                 )
             return a_sum
 
-        def speaker_scale(half, t, j0, dest):
+        def speaker_scale(half, t, j0, dest, bank):
             cols = slice(j0, j0 + BANK)
             codes, scales = (wb_words, wb_plane) if half == 0 else (wb_codes, wb_scales)
-            b_sum = bank_y([P, BANK])
+            b_sum = bank([P, BANK])
             nc.tensor.matmul_mx(
                 out=b_sum[:],
                 lhsT=codes[:, 2 * t * P : 2 * (t + 1) * P].bitcast(FP4X4),
@@ -195,12 +195,10 @@ def tile_list_speaker_affine_flow_kernel(
             )
             nc.scalar.activation(dest, b_sum[:], ACT.Exp)
 
-        def exponentials(units, name, spare=0):
-            cells = kept([P, (len(units) + spare) * BANK], F32, name)
+        def exponentials(units, cells, bank):
             for n, (half, t, b) in enumerate(units):
                 scale[half, t, b] = cells[:, n * BANK : (n + 1) * BANK]
-                speaker_scale(half, t, b * BANK, scale[half, t, b])
-            return cells
+                speaker_scale(half, t, b * BANK, scale[half, t, b], bank)
 
         def shift(t, j0, width, dest, product):
             nc.vector.tensor_tensor(dest, g_window[1, t][:].indirect(offsets(j0, width)), product, ALU.add)
@@ -266,15 +264,19 @@ def tile_list_speaker_affine_flow_kernel(
         )
         gather_words(0, (0, BANK, S))
         quantise_wa(0, 0, 0, wa_grouped[0, 0])
-        grouped_piece = [kept([P, NARROW * PACK], BF16, "grouped_piece%d" % u) for u in range(2)]
-        for u in range(2):
-            interleave(nc.scalar.copy, grouped_piece[u][:], wa_piece[u][:])
+        grouped_piece = [kept([P, NARROW * PACK], BF16, "grouped_piece")]
+        interleave(nc.scalar.copy, grouped_piece[0][:], wa_piece[0][:])
         quantise_wa(0, 1, 0, grouped_piece[0])
+        grouped_piece.append(kept([P, NARROW * PACK], BF16, "grouped_piece"))
+        round_on_gpsimd(
+            grouped_piece[1][:].rearrange("p (r i) -> p r i", i=PACK), wa_piece[1][:].rearrange("p i r -> p r i")
+        )
         gather_words(1, (0, BANK, S))
 
         first_units = [(0, 0), (1, 0), (0, 1), (1, 1), (2, 0), (3, 0), (2, 1), (3, 1)]
-        exponentials([(0, t, b) for t, b in first_units[:6]], "first_early")
-        early = exponentials([(0, t, b) for t, b in first_units[6:]] + [(1, 0, 0), (1, 0, 1)], "wa1_0")
+        exponentials([(0, t, b) for t, b in first_units[:7]], kept([P, 7 * BANK], F32, "first_early"), bank_y)
+        early = kept([P, 4 * BANK], F32, "wa1_0")
+        exponentials([(0, t, b) for t, b in first_units[7:]] + [(1, 3, 0), (1, 0, 0), (1, 0, 1)], early, bank_y)
 
         def first_products(units, bank, held=None):
             for n, (t, b) in enumerate(units):
@@ -285,17 +287,17 @@ def tile_list_speaker_affine_flow_kernel(
 
         first_products(first_units[0:2], bank_a)
         quantise_wa(0, 1, NARROW, grouped_piece[1])
-        first_products(first_units[2:4], bank_y, kept([P, S], F32, "wa1_256"))
-        first_products(first_units[4:6], bank_y)
+        first_products(first_units[2:4], bank_a, kept([P, S], F32, "wa1_256"))
+        first_products(first_units[4:6], bank_a)
         for g in range(K // PASS):
             wa_grouped[1, g] = kept([P, PASS * PACK], BF16, "grouped1%d" % g)
             nc.scalar.copy(
                 wa_grouped[1, g][:].rearrange("p (t m i) -> p m i t", t=PACK, i=PACK),
                 wa_raw[1, g][:].rearrange("p i (m t) -> p m i t", t=PACK),
             )
-        first_products(first_units[6:7], bank_y)
+        first_products(first_units[6:7], bank_a)
         quantise_wa(1, 0, 0, wa_grouped[1, 0])
-        first_products(first_units[7:8], bank_y, kept([P, BANK], F32, "wa0_512"))
+        first_products(first_units[7:8], bank_a, kept([P, BANK], F32, "wa0_512"))
         quantise_wa(1, 1, 0, wa_grouped[1, 1])
 
         aside = kept([P, 4 * BANK], F32, "aside")
@@ -307,46 +309,26 @@ def tile_list_speaker_affine_flow_kernel(
                 nc.scalar.copy(copies[:, n * BANK : (n + 1) * BANK], a_sum[:])
             nc.gpsimd.tensor_tensor(exps if product is None else product, exps, copies, ALU.mult)
 
-        share(early[:, S:], aside[:, 0:S], ((0, 0), (0, 1)))
-        late = exponentials([(1, 3, 0), (1, 3, 1), (1, 1, 0), (1, 2, 0), (1, 1, 1), (1, 2, 1)], "wa1_512")
-        last_sums = [frames(1, PACK - 1, b * BANK, bank_a) for b in range(S // BANK)]
-        middle = kept([P, S], F32, "middle")
-        share(late[:, S : 2 * S], aside[:, S:], ((1, 0), (2, 0)), middle[:])
-        scale[1, 1, 0], scale[1, 2, 0] = middle[:, 0:BANK], middle[:, BANK:]
-
-        picked = {}
-
-        def pick(t, name, cuts):
-            picked[t] = kept([P, S], F32, name)
-            for j0, j1 in zip(cuts, cuts[1:]):
-                nc.vector.tensor_copy(picked[t][:, j0:j1], g_window[0, t][:].indirect(offsets(j0, j1 - j0)))
-
-        pick(0, "grouped10", (0, S))
-        cells = kept([P, 13 * NARROW], F32, "g_first")
-
-        def cell(n, count=1):
-            return cells[:, n * NARROW : (n + count) * NARROW]
-
-        for b, first in enumerate((1, 11)):
-            nc.vector.tensor_tensor(cell(first, 2), scale[1, 3, b], last_sums[b][:], ALU.mult)
-            scale[1, 3, b] = cell(first, 2)
-        pick(1, "grouped11", (0, S))
-        pick(2, "picked", (0, S))
-        pick(3, "picked3", (0, BANK, S))
-
         turned = kept([P, S // P, 2, 2 * P], BF16, "tab2")
 
-        def add_turned(t, b):
-            h_sum = (bank_y if t == PACK - 1 else bank_a)([P, BANK // P, P])
-            for n, source in enumerate((scale[0, t, b], picked[t][:, b * BANK : (b + 1) * BANK])):
-                for c in range(BANK // P):
-                    nc.tensor.matmul(
-                        h_sum[:, c], source[:, c * P : (c + 1) * P], identity[:], is_transpose=True,
-                        start=(n, c) == (0, 0), stop=(n, c) == (1, BANK // P - 1),
-                    )
+        h_sums = {}
+
+        def turn(t, b, source, first):
+            for c in range(BANK // P):
+                nc.tensor.matmul(
+                    h_sums[t, b][:, c], source[:, c * P : (c + 1) * P], identity[:], is_transpose=True,
+                    start=first and c == 0, stop=not first and c == BANK // P - 1,
+                )
+
+        def turn_product(t, b, bank):
+            h_sums[t, b] = bank([P, BANK // P, P])
+            turn(t, b, scale[0, t, b], True)
+
+        def add_shift(t, b):
+            turn(t, b, picked[t][:, b * BANK : (b + 1) * BANK], False)
             nc.scalar.copy(
                 turned[:, 4 * b : 4 * b + 4, :, 64 * t : 64 * (t + 1)].rearrange("p c u (w e) -> p c u w e", e=2),
-                h_sum[:].rearrange("p c (w u e) -> p c u w e", u=2, e=2),
+                h_sums[t, b][:].rearrange("p c (w u e) -> p c u w e", u=2, e=2),
             )
 
         def turn_back(b):
@@ -362,21 +344,44 @@ def tile_list_speaker_affine_flow_kernel(
                     pairs[:].rearrange("p c u j -> p c j u"),
                 )
 
-        def set_aside(n):
-            a_sum = frames(1, n + 1, BANK, bank_a)
-            nc.scalar.copy(aside_late[:, n * BANK : (n + 1) * BANK], a_sum[:])
+        picked = {}
 
-        add_turned(0, 0)
-        add_turned(0, 1)
-        set_aside(0)
-        add_turned(1, 0)
-        set_aside(1)
-        nc.gpsimd.tensor_tensor(late[:, 2 * S :], late[:, 2 * S :], aside_late[:], ALU.mult)
-        add_turned(1, 1)
-        add_turned(2, 0)
-        add_turned(2, 1)
+        def pick(t, cuts):
+            picked[t] = kept([P, S], F32, "picked%d" % t)
+            for j0, j1 in zip(cuts, cuts[1:]):
+                nc.vector.tensor_copy(picked[t][:, j0:j1], g_window[0, t][:].indirect(offsets(j0, j1 - j0)))
+
+        for t, b in first_units[2:6]:
+            turn_product(t, b, bank_y)
+        late = kept([P, 5 * BANK], F32, "wa1_512")
+        exponentials([(1, 1, 0), (1, 2, 0), (1, 1, 1), (1, 2, 1)], late, bank_a)
+        share(early[:, S : 2 * S], aside[:, 0:S], ((0, 0), (0, 1)))
+        middle = kept([P, S], F32, "middle")
+        share(late[:, 0:S], aside[:, S:], ((1, 0), (2, 0)), middle[:])
+        scale[1, 1, 0], scale[1, 2, 0] = middle[:, 0:BANK], middle[:, BANK:]
+        pick(0, (0, S))
+        pick(1, (0, S))
+        pick(2, (0, S))
+        pick(3, (0, BANK, S))
+        turn_product(0, 0, bank_a)
         for b in range(S // BANK):
-            add_turned(PACK - 1, b)
+            add_shift(0, b)
+        share(late[:, S : 2 * S], aside_late[:], ((1, 1), (2, 1)))
+        exponentials([(1, 3, 1)], late[:, 2 * S :], bank_a)
+        for t, b in ((1, 0), (2, 1), (3, 1)):
+            turn_product(t, b, bank_a)
+        last_sums = [frames(1, PACK - 1, b * BANK, bank) for b, bank in enumerate((bank_y, bank_a))]
+        cells = kept([P, 13 * NARROW], F32, "g_held")
+
+        def cell(n, count=1):
+            return cells[:, n * NARROW : (n + count) * NARROW]
+
+        for b, first in enumerate((1, 11)):
+            nc.vector.tensor_tensor(cell(first, 2), scale[1, 3, b], last_sums[b][:], ALU.mult)
+            scale[1, 3, b] = cell(first, 2)
+        for t in range(1, PACK):
+            for b in range(S // BANK):
+                add_shift(t, b)
         for b in range(S // BANK):
             turn_back(b)
 

@@ -268,8 +268,10 @@ def tile_list_speaker_affine_flow_kernel(
         interleave(nc.scalar.copy, grouped_piece[0][:], wa_piece[0][:])
         quantise_wa(0, 1, 0, grouped_piece[0])
         grouped_piece.append(kept([P, NARROW * PACK], BF16, "grouped_piece"))
+        interleave(nc.scalar.copy, grouped_piece[1][:, 0:PASS], wa_piece[1][:, :, 0:P])
         round_on_gpsimd(
-            grouped_piece[1][:].rearrange("p (r i) -> p r i", i=PACK), wa_piece[1][:].rearrange("p i r -> p r i")
+            grouped_piece[1][:, PASS:].rearrange("p (r i) -> p r i", i=PACK),
+            wa_piece[1][:, :, P:].rearrange("p i r -> p r i"),
         )
         gather_words(1, (0, BANK, S))
 
@@ -289,16 +291,20 @@ def tile_list_speaker_affine_flow_kernel(
         quantise_wa(0, 1, NARROW, grouped_piece[1])
         first_products(first_units[2:4], bank_a, kept([P, S], F32, "wa1_256"))
         first_products(first_units[4:6], bank_a)
-        for g in range(K // PASS):
-            wa_grouped[1, g] = kept([P, PASS * PACK], BF16, "grouped1%d" % g)
+
+        def round_slots(g, t0, count):
+            grouped = kept([P, count * PASS], BF16, "grouped1%d%d" % (g, t0))
             nc.scalar.copy(
-                wa_grouped[1, g][:].rearrange("p (t m i) -> p m i t", t=PACK, i=PACK),
-                wa_raw[1, g][:].rearrange("p i (m t) -> p m i t", t=PACK),
+                grouped[:].rearrange("p (t m i) -> p m i t", t=count, i=PACK),
+                wa_raw[1, g][:].rearrange("p i (m t) -> p m i t", t=PACK)[:, :, :, t0 : t0 + count],
             )
-        first_products(first_units[6:7], bank_a)
-        quantise_wa(1, 0, 0, wa_grouped[1, 0])
-        first_products(first_units[7:8], bank_a, kept([P, BANK], F32, "wa0_512"))
-        quantise_wa(1, 1, 0, wa_grouped[1, 1])
+            return grouped
+
+        slots_of_wa = [round_slots(0, 0, PACK), round_slots(1, 0, 2), round_slots(1, 2, 2)]
+        quantise_wa(1, 0, 0, slots_of_wa[0])
+        first_products(first_units[6:8], bank_a, kept([P, S], F32, "wa0_512"))
+        quantise_wa(1, 1, 0, slots_of_wa[1])
+        quantise_wa(1, 1, 2 * P, slots_of_wa[2])
 
         aside = kept([P, 4 * BANK], F32, "aside")
         aside_late = kept([P, 2 * BANK], F32, "aside_late")
@@ -353,11 +359,13 @@ def tile_list_speaker_affine_flow_kernel(
 
         for t, b in first_units[2:6]:
             turn_product(t, b, bank_y)
-        late = kept([P, 5 * BANK], F32, "wa1_512")
-        exponentials([(1, 1, 0), (1, 2, 0), (1, 1, 1), (1, 2, 1)], late, bank_a)
+        later = kept([P, S], F32, "grouped110")
+        exponentials([(1, 1, 0), (1, 2, 0)], later, bank_a)
         share(early[:, S : 2 * S], aside[:, 0:S], ((0, 0), (0, 1)))
         middle = kept([P, S], F32, "middle")
-        share(late[:, 0:S], aside[:, S:], ((1, 0), (2, 0)), middle[:])
+        share(later[:], aside[:, S:], ((1, 0), (2, 0)), middle[:])
+        late = kept([P, 3 * BANK], F32, "wa1_512")
+        exponentials([(1, 1, 1), (1, 2, 1)], late, bank_a)
         scale[1, 1, 0], scale[1, 2, 0] = middle[:, 0:BANK], middle[:, BANK:]
         pick(0, (0, S))
         pick(1, (0, S))
@@ -366,8 +374,8 @@ def tile_list_speaker_affine_flow_kernel(
         turn_product(0, 0, bank_a)
         for b in range(S // BANK):
             add_shift(0, b)
-        share(late[:, S : 2 * S], aside_late[:], ((1, 1), (2, 1)))
-        exponentials([(1, 3, 1)], late[:, 2 * S :], bank_a)
+        share(late[:, 0:S], aside_late[:], ((1, 1), (2, 1)))
+        exponentials([(1, 3, 1)], late[:, S:], bank_a)
         for t, b in ((1, 0), (2, 1), (3, 1)):
             turn_product(t, b, bank_a)
         last_sums = [frames(1, PACK - 1, b * BANK, bank) for b, bank in enumerate((bank_y, bank_a))]
@@ -385,24 +393,17 @@ def tile_list_speaker_affine_flow_kernel(
         for b in range(S // BANK):
             turn_back(b)
 
-        places = ((3, 4, 2), (4, 4, 2), (0, 2, 1), (3, 2, 1))
+        places = ((3, 2), (4, 2), (0, 1), (3, 1))
 
         def place(n, t):
-            base, far, near = places[n]
-            return cell(base + far * (t // 2) + near * (t % 2))
-
-        def slots(n):
-            base, far, near = places[n]
-            return cell(base, 2 * far).rearrange("p (a b c) -> p a b c", a=2, c=NARROW)[:, :, 0 : near + 1 : near, :]
+            first, step = places[n]
+            return cell(first + step * t)
 
         def round_second(copy, j0, width, name):
-            n = j0 // NARROW
+            first, step = places[j0 // NARROW]
+            slots = cells[:].rearrange("p (n c) -> p n c", c=NARROW)[:, first : first + 3 * step + 1 : step]
             h_round[1, j0] = kept([P, width * PACK], BF16, name)
-            c0 = j0 % NARROW
-            copy(
-                h_round[1, j0][:].rearrange("p (c i a b) -> p c a b i", i=4, a=2, b=2),
-                slots(n)[:, :, :, c0 : c0 + width].rearrange("p a b (c i) -> p c a b i", i=4),
-            )
+            interleave(copy, h_round[1, j0][:], slots[:, :, j0 % NARROW : j0 % NARROW + width])
 
         def shift_narrow(n, t):
             b, c0 = divmod(n * NARROW, BANK)

@@ -23,7 +23,7 @@ PASS = P * PACK
 BANK = 512
 NARROW = BANK // 2
 HALVES = H // PASS
-RING = 6
+RING = 5
 TAB_ROW = 4
 
 
@@ -35,17 +35,13 @@ def tile_list_speaker_affine_flow_kernel(
     with ExitStack() as ctx:
         keep = ctx.enter_context(tc.tile_pool(name="keep", bufs=1))
         ring = ctx.enter_context(tc.tile_pool(name="ring", bufs=RING))
-        psum_a = ctx.enter_context(tc.psum_pool(name="psum_a", bufs=4))
-        psum_y = ctx.enter_context(tc.psum_pool(name="psum_y", bufs=4))
+        psum = ctx.enter_context(tc.psum_pool(name="psum", bufs=1))
 
         def kept(shape, dtype, name):
             return keep.tile(shape, dtype, name=name, align_bytes=64)
 
-        def bank_a(shape):
-            return psum_a.tile(shape, F32, name="a_sum")
-
-        def bank_y(shape):
-            return psum_y.tile(shape, F32, name="y_sum")
+        def in_bank(n, shape):
+            return psum.tile(shape, F32, name="bank%d" % n)
 
         idx = keep.tile([P, S // 16], U16, name="idx")
         idx2 = keep.tile([P, S // 16], U16, name="idx2")
@@ -166,7 +162,7 @@ def tile_list_speaker_affine_flow_kernel(
             )
 
         def frames(half, t, j0, bank):
-            a_sum = bank([P, BANK])
+            a_sum = in_bank(bank, [P, BANK])
             for g in range(K // PASS):
                 codes, scales = wa_q[half, g]
                 nc.tensor.matmul_mx(
@@ -183,7 +179,7 @@ def tile_list_speaker_affine_flow_kernel(
         def speaker_scale(half, t, j0, dest, bank):
             cols = slice(j0, j0 + BANK)
             codes, scales = (wb_words, wb_plane) if half == 0 else (wb_codes, wb_scales)
-            b_sum = bank([P, BANK])
+            b_sum = in_bank(bank, [P, BANK])
             nc.tensor.matmul_mx(
                 out=b_sum[:],
                 lhsT=codes[:, 2 * t * P : 2 * (t + 1) * P].bitcast(FP4X4),
@@ -195,10 +191,10 @@ def tile_list_speaker_affine_flow_kernel(
             )
             nc.scalar.activation(dest, b_sum[:], ACT.Exp)
 
-        def exponentials(units, cells, bank):
+        def exponentials(units, cells, banks):
             for n, (half, t, b) in enumerate(units):
                 scale[half, t, b] = cells[:, n * BANK : (n + 1) * BANK]
-                speaker_scale(half, t, b * BANK, scale[half, t, b], bank)
+                speaker_scale(half, t, b * BANK, scale[half, t, b], banks[n])
 
         def shift(t, j0, width, dest, product):
             nc.vector.tensor_tensor(dest, g_window[1, t][:].indirect(offsets(j0, width)), product, ALU.add)
@@ -224,7 +220,7 @@ def tile_list_speaker_affine_flow_kernel(
             )
 
         def open_features(j0, width, bank):
-            y_sums[j0] = [bank([P, width]) for q in range(N // P)]
+            y_sums[j0] = [in_bank(bank + q, [P, width]) for q in range(N // P)]
             for q in range(N // P):
                 feature_pass(0, j0, width, y_sums[j0][q], q)
 
@@ -265,32 +261,33 @@ def tile_list_speaker_affine_flow_kernel(
         gather_words(0, (0, BANK, S))
         quantise_wa(0, 0, 0, wa_grouped[0, 0])
         grouped_piece = [kept([P, NARROW * PACK], BF16, "grouped_piece")]
-        interleave(nc.scalar.copy, grouped_piece[0][:], wa_piece[0][:])
+        round_on_gpsimd(
+            grouped_piece[0][:].rearrange("p (r i) -> p r i", i=PACK), wa_piece[0][:].rearrange("p i r -> p r i")
+        )
         quantise_wa(0, 1, 0, grouped_piece[0])
         grouped_piece.append(kept([P, NARROW * PACK], BF16, "grouped_piece"))
-        interleave(nc.scalar.copy, grouped_piece[1][:, 0:PASS], wa_piece[1][:, :, 0:P])
         round_on_gpsimd(
-            grouped_piece[1][:, PASS:].rearrange("p (r i) -> p r i", i=PACK),
-            wa_piece[1][:, :, P:].rearrange("p i r -> p r i"),
+            grouped_piece[1][:].rearrange("p (r i) -> p r i", i=PACK), wa_piece[1][:].rearrange("p i r -> p r i")
         )
         gather_words(1, (0, BANK, S))
 
         first_units = [(0, 0), (1, 0), (0, 1), (1, 1), (2, 0), (3, 0), (2, 1), (3, 1)]
-        exponentials([(0, t, b) for t, b in first_units[:7]], kept([P, 7 * BANK], F32, "first_early"), bank_y)
-        early = kept([P, 4 * BANK], F32, "wa1_0")
-        exponentials([(0, t, b) for t, b in first_units[7:]] + [(1, 3, 0), (1, 0, 0), (1, 0, 1)], early, bank_y)
+        exponentials([(0, t, b) for t, b in first_units], kept([P, 8 * BANK], F32, "first_early"), (4, 5, 6, 7) * 2)
+        second = kept([P, 8 * BANK], F32, "second")
+        second_units = [(1, 0, 0), (1, 0, 1), (1, 1, 0), (1, 2, 0), (1, 1, 1), (1, 2, 1), (1, 3, 0), (1, 3, 1)]
+        exponentials(second_units[:7], second, (4, 5, 6, 7) * 2)
 
         def first_products(units, bank, held=None):
             for n, (t, b) in enumerate(units):
-                a_sum = frames(0, t, b * BANK, bank)
+                a_sum = frames(0, t, b * BANK, bank + n)
                 product = scale[0, t, b] if held is None else held[:, n * BANK : (n + 1) * BANK]
                 nc.vector.tensor_tensor(product, scale[0, t, b], a_sum[:], ALU.mult)
                 scale[0, t, b] = product
 
-        first_products(first_units[0:2], bank_a)
+        first_products(first_units[0:2], 0)
         quantise_wa(0, 1, NARROW, grouped_piece[1])
-        first_products(first_units[2:4], bank_a, kept([P, S], F32, "wa1_256"))
-        first_products(first_units[4:6], bank_a)
+        first_products(first_units[2:4], 2, kept([P, S], F32, "wa1_256"))
+        first_products(first_units[4:6], 0)
 
         def round_slots(g, t0, count):
             grouped = kept([P, count * PASS], BF16, "grouped1%d%d" % (g, t0))
@@ -302,16 +299,16 @@ def tile_list_speaker_affine_flow_kernel(
 
         slots_of_wa = [round_slots(0, 0, PACK), round_slots(1, 0, 2), round_slots(1, 2, 2)]
         quantise_wa(1, 0, 0, slots_of_wa[0])
-        first_products(first_units[6:8], bank_a, kept([P, S], F32, "wa0_512"))
+        first_products(first_units[6:8], 2, kept([P, S], F32, "wa0_512"))
         quantise_wa(1, 1, 0, slots_of_wa[1])
         quantise_wa(1, 1, 2 * P, slots_of_wa[2])
 
         aside = kept([P, 4 * BANK], F32, "aside")
         aside_late = kept([P, 2 * BANK], F32, "aside_late")
 
-        def share(exps, copies, units, product=None):
+        def share(exps, copies, units, bank, product=None):
             for n, (t, b) in enumerate(units):
-                a_sum = frames(1, t, b * BANK, bank_a)
+                a_sum = frames(1, t, b * BANK, bank + n)
                 nc.scalar.copy(copies[:, n * BANK : (n + 1) * BANK], a_sum[:])
             nc.gpsimd.tensor_tensor(exps if product is None else product, exps, copies, ALU.mult)
 
@@ -327,7 +324,7 @@ def tile_list_speaker_affine_flow_kernel(
                 )
 
         def turn_product(t, b, bank):
-            h_sums[t, b] = bank([P, BANK // P, P])
+            h_sums[t, b] = in_bank(bank, [P, BANK // P, P])
             turn(t, b, scale[0, t, b], True)
 
         def add_shift(t, b):
@@ -341,7 +338,7 @@ def tile_list_speaker_affine_flow_kernel(
             h_round[0, b * BANK] = kept([P, BANK * PACK], BF16, "h_first%d" % b)
             words = h_round[0, b * BANK][:].bitcast(F32)
             for n in range(2):
-                pairs = bank_y([P, 2, 2, P])
+                pairs = in_bank((3, 4, 5, 6)[2 * b + n], [P, 2, 2, P])
                 for c in range(2):
                     for u in range(2):
                         nc.tensor.transpose(pairs[:, c, u], turned[:, 4 * b + 2 * n + c, u].bitcast(F32), identity[:])
@@ -357,37 +354,40 @@ def tile_list_speaker_affine_flow_kernel(
             for j0, j1 in zip(cuts, cuts[1:]):
                 nc.vector.tensor_copy(picked[t][:, j0:j1], g_window[0, t][:].indirect(offsets(j0, j1 - j0)))
 
-        for t, b in first_units[2:6]:
-            turn_product(t, b, bank_y)
-        later = kept([P, S], F32, "grouped110")
-        exponentials([(1, 1, 0), (1, 2, 0)], later, bank_a)
-        share(early[:, S : 2 * S], aside[:, 0:S], ((0, 0), (0, 1)))
+        for (t, b), bank in zip(first_units[2:6], (7, 4, 5, 6)):
+            turn_product(t, b, bank)
+        share(second[:, 0:S], aside[:, 0:S], ((0, 0), (0, 1)), 0)
         middle = kept([P, S], F32, "middle")
-        share(later[:], aside[:, S:], ((1, 0), (2, 0)), middle[:])
-        late = kept([P, 3 * BANK], F32, "wa1_512")
-        exponentials([(1, 1, 1), (1, 2, 1)], late, bank_a)
+        share(second[:, S : 2 * S], aside[:, S:], ((1, 0), (2, 0)), 2, middle[:])
         scale[1, 1, 0], scale[1, 2, 0] = middle[:, 0:BANK], middle[:, BANK:]
         pick(0, (0, S))
         pick(1, (0, S))
         pick(2, (0, S))
         pick(3, (0, BANK, S))
-        turn_product(0, 0, bank_a)
+        turn_product(0, 0, 0)
         for b in range(S // BANK):
             add_shift(0, b)
-        share(late[:, 0:S], aside_late[:], ((1, 1), (2, 1)))
-        exponentials([(1, 3, 1)], late[:, S:], bank_a)
-        for t, b in ((1, 0), (2, 1), (3, 1)):
-            turn_product(t, b, bank_a)
-        last_sums = [frames(1, PACK - 1, b * BANK, bank) for b, bank in enumerate((bank_y, bank_a))]
-        cells = kept([P, 13 * NARROW], F32, "g_held")
+        share(second[:, 2 * S : 3 * S], aside_late[:], ((1, 1), (2, 1)), 1)
+        turn_product(1, 0, 3)
+        exponentials(second_units[7:], second[:, 7 * BANK :], (1,))
+        last_sums = [frames(1, PACK - 1, b * BANK, 7 * b) for b in range(S // BANK)]
+        aside_last = kept([P, NARROW], F32, "aside_last")
+        nc.scalar.copy(aside_last[:], last_sums[1][:, NARROW:])
+        last_range = scale[1, 3, 1][:, NARROW:]
+        nc.gpsimd.tensor_tensor(last_range, last_range, aside_last[:], ALU.mult)
+        turn_product(2, 1, 2)
+        turn_product(3, 1, 1)
+        for b in range(S // BANK):
+            add_shift(1, b)
+        cells = kept([P, 12 * NARROW], F32, "g_held")
 
         def cell(n, count=1):
             return cells[:, n * NARROW : (n + count) * NARROW]
 
-        for b, first in enumerate((1, 11)):
-            nc.vector.tensor_tensor(cell(first, 2), scale[1, 3, b], last_sums[b][:], ALU.mult)
-            scale[1, 3, b] = cell(first, 2)
-        for t in range(1, PACK):
+        nc.vector.tensor_tensor(cell(1, 2), scale[1, 3, 0], last_sums[0][:], ALU.mult)
+        nc.vector.tensor_tensor(cell(11), scale[1, 3, 1][:, 0:NARROW], last_sums[1][:, 0:NARROW], ALU.mult)
+        last_products = (cell(1), cell(2), cell(11), last_range)
+        for t in range(2, PACK):
             for b in range(S // BANK):
                 add_shift(t, b)
         for b in range(S // BANK):
@@ -407,14 +407,15 @@ def tile_list_speaker_affine_flow_kernel(
 
         def shift_narrow(n, t):
             b, c0 = divmod(n * NARROW, BANK)
-            shift(t, n * NARROW, NARROW, place(n, t), scale[1, t, b][:, c0 : c0 + NARROW])
+            product = last_products[n] if t == PACK - 1 else scale[1, t, b][:, c0 : c0 + NARROW]
+            shift(t, n * NARROW, NARROW, place(n, t), product)
 
         shift(0, 0, BANK, cell(3, 2), scale[1, 0, 0])
         shift_narrow(2, 0)
         shift(1, 0, BANK, cell(5, 2), scale[1, 1, 0])
         shift(2, 0, BANK, cell(7, 2), scale[1, 2, 0])
         quantise_h(0, 0, BANK, "middle")
-        open_features(0, NARROW, bank_y)
+        open_features(0, NARROW, 4)
         for n in range(2):
             shift_narrow(n, 3)
             round_second(nc.scalar.copy, n * NARROW, NARROW, "h_round%d" % n)
@@ -422,19 +423,19 @@ def tile_list_speaker_affine_flow_kernel(
         shift_narrow(2, 2)
         quantise_h(1, 0, NARROW, "h_codes1_0")
         features(0, NARROW, "first_early")
-        open_features(NARROW, NARROW, bank_a)
+        open_features(NARROW, NARROW, 0)
         shift_narrow(2, 3)
         round_second(nc.scalar.copy, BANK, NARROW, "h_codes1_0")
         quantise_h(0, BANK, BANK, "h_round0")
-        open_features(BANK, NARROW, bank_y)
+        open_features(BANK, NARROW, 4)
         quantise_h(1, NARROW, NARROW, "h_codes1_1")
         features(NARROW, NARROW, "wa0_0")
-        open_features(S - NARROW, P, bank_a)
+        open_features(S - NARROW, P, 0)
         for t in range(1, PACK):
             shift_narrow(3, t)
         quantise_h(1, BANK, NARROW, "h_codes1_2")
         features(BANK, NARROW, "aside")
-        open_features(S - P, P, bank_y)
+        open_features(S - P, P, 4)
         last = S - NARROW
         for j0 in range(last, S, P):
             c0 = j0 - last

@@ -25,6 +25,7 @@ NARROW = BANK // 2
 HALVES = H // PASS
 RING = 5
 TAB_ROW = 4
+RUN = 4
 
 
 def tile_list_speaker_affine_flow_kernel(
@@ -55,6 +56,7 @@ def tile_list_speaker_affine_flow_kernel(
         for plane in (tab2_plane, tab_plane, wb_plane, w8_plane):
             nc.gpsimd.memset(plane[:].bitcast(I32), 0)
         make_identity(nc, identity[:])
+
 
         def load_plane_by_quadrant(plane, scales):
             rows = 4 * scales.shape[0]
@@ -122,6 +124,7 @@ def tile_list_speaker_affine_flow_kernel(
         with nc.allow_non_contiguous_dma(reason="one bias value for each partition and tile of rows"):
             nc.sync.dma_start(out=bias_sb[:], in_=bias.rearrange("(q p) -> p q", p=P))
 
+
         v2_scales = kept([P, S], U8, "v2_scales")
         v2_codes = kept([P, S], U32, "v2_codes")
         v_scales = kept([P, S], U8, "v_scales")
@@ -136,21 +139,25 @@ def tile_list_speaker_affine_flow_kernel(
             for half in range(HALVES)
             for g in range(K // PASS)
         }
-        wa_grouped, h_round, h_codes, y_sums = {}, {}, {}, {}
+        scale, h_round, h_codes, y_sums = {}, {}, {}, {}
 
         def offsets(j0, width):
             return idx[:, j0 // 16 : (j0 + width) // 16]
 
-        def gather_words(g, cuts):
-            for j0, j1 in zip(cuts, cuts[1:]):
-                dest = v_codes[g][j0 // BANK][:, j0 % BANK : j0 % BANK + j1 - j0]
-                nc.vector.tensor_copy(dest, tab_window[g][:].indirect(offsets(j0, j1 - j0)))
+        def gather_words(g):
+            for b in range(S // BANK):
+                nc.vector.tensor_copy(v_codes[g][b][:], tab_window[g][:].indirect(offsets(b * BANK, BANK)))
 
         def interleave(copy, grouped, rows):
-            copy(grouped.rearrange("p (c i t) -> p c t i", i=4, t=PACK), rows.rearrange("p t (c i) -> p c t i", i=4))
+            copy(
+                grouped.rearrange("p (c i t) -> p c t i", i=RUN, t=PACK), rows.rearrange("p t (c i) -> p c t i", i=RUN)
+            )
 
         def round_on_gpsimd(grouped, rows):
-            nc.gpsimd.tensor_scalar(grouped, rows, 1.0, 0.0, ALU.mult, ALU.add)
+            nc.gpsimd.tensor_scalar(
+                grouped[:].rearrange("p (r i) -> p r i", i=PACK), rows.rearrange("p i r -> p r i"),
+                1.0, 0.0, ALU.mult, ALU.add,
+            )
 
         def quantise_wa(half, g, r0, grouped):
             codes, scales = wa_q[half, g]
@@ -238,7 +245,7 @@ def tile_list_speaker_affine_flow_kernel(
                     rows = slice(q - 1, q + 1)
                     nc.sync.dma_start(out=out.rearrange("(q p) j -> p q j", p=P)[:, rows, cols], in_=y[:, rows])
 
-        scale = {}
+
         nc.vector.tensor_copy(
             wb_codes[:].bitcast(U16).rearrange("p (t m) -> p t m", t=PACK),
             wb_words[:, 2 * PASS :].bitcast(U16).rearrange("p (m t) -> p t m", t=PACK),
@@ -254,28 +261,24 @@ def tile_list_speaker_affine_flow_kernel(
             wb_plane[:, PASS:].rearrange("p (m t) -> p t m", t=PACK),
         )
         nc.vector.tensor_copy(v_scales[:], tab_plane[:].indirect(idx[:]))
-        wa_grouped[0, 0] = kept([P, PASS * PACK], BF16, "tab2")
-        round_on_gpsimd(
-            wa_grouped[0, 0][:].rearrange("p (r i) -> p r i", i=PACK), wa_raw[0, 0][:].rearrange("p i r -> p r i")
-        )
-        gather_words(0, (0, BANK, S))
-        quantise_wa(0, 0, 0, wa_grouped[0, 0])
+        first_grouped = kept([P, PASS * PACK], BF16, "tab2")
+        round_on_gpsimd(first_grouped, wa_raw[0, 0][:])
+        gather_words(0)
+        quantise_wa(0, 0, 0, first_grouped)
         grouped_piece = [kept([P, NARROW * PACK], BF16, "grouped_piece")]
-        round_on_gpsimd(
-            grouped_piece[0][:].rearrange("p (r i) -> p r i", i=PACK), wa_piece[0][:].rearrange("p i r -> p r i")
-        )
+        round_on_gpsimd(grouped_piece[0], wa_piece[0][:])
         quantise_wa(0, 1, 0, grouped_piece[0])
         grouped_piece.append(kept([P, NARROW * PACK], BF16, "grouped_piece"))
-        round_on_gpsimd(
-            grouped_piece[1][:].rearrange("p (r i) -> p r i", i=PACK), wa_piece[1][:].rearrange("p i r -> p r i")
-        )
-        gather_words(1, (0, BANK, S))
+        round_on_gpsimd(grouped_piece[1], wa_piece[1][:])
+        gather_words(1)
+
 
         first_units = [(0, 0), (1, 0), (0, 1), (1, 1), (2, 0), (3, 0), (2, 1), (3, 1)]
         exponentials([(0, t, b) for t, b in first_units], kept([P, 8 * BANK], F32, "first_early"), (4, 5, 6, 7) * 2)
         second = kept([P, 8 * BANK], F32, "second")
         second_units = [(1, 0, 0), (1, 0, 1), (1, 1, 0), (1, 2, 0), (1, 1, 1), (1, 2, 1), (1, 3, 0), (1, 3, 1)]
         exponentials(second_units[:7], second, (4, 5, 6, 7) * 2)
+
 
         def first_products(units, bank, held=None):
             for n, (t, b) in enumerate(units):
@@ -297,11 +300,20 @@ def tile_list_speaker_affine_flow_kernel(
             )
             return grouped
 
-        slots_of_wa = [round_slots(0, 0, PACK), round_slots(1, 0, 2), round_slots(1, 2, 2)]
+        last_slot = kept([P, PASS], BF16, "grouped_piece")
+        round_on_gpsimd(last_slot, wa_raw[1, 0][:].rearrange("p i (m t) -> p t i m", t=PACK)[:, PACK - 1])
+        slots_of_wa = [round_slots(0, 0, PACK - 1), round_slots(1, 0, 2), round_slots(1, 2, 2)]
         quantise_wa(1, 0, 0, slots_of_wa[0])
-        first_products(first_units[6:8], 2, kept([P, S], F32, "wa0_512"))
+        quantise_wa(1, 0, (PACK - 1) * P, last_slot)
+        first_products(first_units[6:7], 2, kept([P, BANK], F32, "wa0_512"))
         quantise_wa(1, 1, 0, slots_of_wa[1])
         quantise_wa(1, 1, 2 * P, slots_of_wa[2])
+        first_aside = kept([P, BANK], F32, "grouped110")
+        nc.scalar.copy(first_aside[:], frames(0, PACK - 1, BANK, 3)[:])
+        first_last = kept([P, BANK], F32, "grouped112")
+        nc.gpsimd.tensor_tensor(first_last[:], scale[0, 3, 1], first_aside[:], ALU.mult)
+        scale[0, 3, 1] = first_last[:]
+
 
         aside = kept([P, 4 * BANK], F32, "aside")
         aside_late = kept([P, 2 * BANK], F32, "aside_late")
@@ -313,8 +325,7 @@ def tile_list_speaker_affine_flow_kernel(
             nc.gpsimd.tensor_tensor(exps if product is None else product, exps, copies, ALU.mult)
 
         turned = kept([P, S // P, 2, 2 * P], BF16, "tab2")
-
-        h_sums = {}
+        h_sums, picked = {}, {}
 
         def turn(t, b, source, first):
             for c in range(BANK // P):
@@ -347,8 +358,6 @@ def tile_list_speaker_affine_flow_kernel(
                     pairs[:].rearrange("p c u j -> p c j u"),
                 )
 
-        picked = {}
-
         def pick(t, cuts):
             picked[t] = kept([P, S], F32, "picked%d" % t)
             for j0, j1 in zip(cuts, cuts[1:]):
@@ -360,10 +369,9 @@ def tile_list_speaker_affine_flow_kernel(
         middle = kept([P, S], F32, "middle")
         share(second[:, S : 2 * S], aside[:, S:], ((1, 0), (2, 0)), 2, middle[:])
         scale[1, 1, 0], scale[1, 2, 0] = middle[:, 0:BANK], middle[:, BANK:]
-        pick(0, (0, S))
-        pick(1, (0, S))
-        pick(2, (0, S))
-        pick(3, (0, BANK, S))
+        for t in range(PACK - 1):
+            pick(t, (0, S))
+        pick(PACK - 1, (0, BANK, S))
         turn_product(0, 0, 0)
         for b in range(S // BANK):
             add_shift(0, b)
@@ -392,6 +400,7 @@ def tile_list_speaker_affine_flow_kernel(
                 add_shift(t, b)
         for b in range(S // BANK):
             turn_back(b)
+
 
         places = ((3, 2), (4, 2), (0, 1), (3, 1))
 

@@ -246,7 +246,7 @@ def tile_list_speaker_affine_flow_kernel(
                     nc.sync.dma_start(out=out.rearrange("(q p) j -> p q j", p=P)[:, rows, cols], in_=y[:, rows])
 
 
-        nc.vector.tensor_copy(
+        nc.scalar.copy(
             wb_codes[:].bitcast(U16).rearrange("p (t m) -> p t m", t=PACK),
             wb_words[:, 2 * PASS :].bitcast(U16).rearrange("p (m t) -> p t m", t=PACK),
         )
@@ -256,12 +256,12 @@ def tile_list_speaker_affine_flow_kernel(
                 v2_codes[:, j0 : j0 + BANK], tab2_window[:].indirect(idx2[:, j0 // 16 : (j0 + BANK) // 16])
             )
         wb_scales = kept([P, PASS], U8, "wb_scales")
-        nc.vector.tensor_copy(
+        nc.gpsimd.tensor_copy(
             wb_scales[:].rearrange("p (t m) -> p t m", t=PACK),
             wb_plane[:, PASS:].rearrange("p (m t) -> p t m", t=PACK),
         )
         nc.vector.tensor_copy(v_scales[:], tab_plane[:].indirect(idx[:]))
-        first_grouped = kept([P, PASS * PACK], BF16, "tab2")
+        first_grouped = kept([P, PASS * PACK], BF16, "picked0")
         round_on_gpsimd(first_grouped, wa_raw[0, 0][:])
         gather_words(0)
         quantise_wa(0, 0, 0, first_grouped)

@@ -90,8 +90,7 @@ def tile_list_speaker_affine_flow_kernel(
         ]
 
         def load_g(half, t):
-            pool, name = (keep, "g_held") if (half, t) == (0, 3) else (ring, "ring")
-            window = pool.tile([P, T], F32, name=name, align_bytes=64)
+            window = ring.tile([P, T], F32, name="ring", align_bytes=64)
             nc.sync.dma_start(out=window[:], in_=g_rows[half][t])
             return window
 
@@ -339,7 +338,7 @@ def tile_list_speaker_affine_flow_kernel(
             turn(t, b, scale[0, t, b], True)
 
         def add_shift(t, b):
-            turn(t, b, picked[t][:, b * BANK : (b + 1) * BANK], False)
+            turn(t, b, picked[t, b], False)
             nc.scalar.copy(
                 turned[:, 4 * b : 4 * b + 4, :, 64 * t : 64 * (t + 1)].rearrange("p c u (w e) -> p c u w e", e=2),
                 h_sums[t, b][:].rearrange("p c (w u e) -> p c u w e", u=2, e=2),
@@ -358,10 +357,11 @@ def tile_list_speaker_affine_flow_kernel(
                     pairs[:].rearrange("p c u j -> p c j u"),
                 )
 
-        def pick(t, cuts):
-            picked[t] = kept([P, S], F32, "picked%d" % t)
-            for j0, j1 in zip(cuts, cuts[1:]):
-                nc.vector.tensor_copy(picked[t][:, j0:j1], g_window[0, t][:].indirect(offsets(j0, j1 - j0)))
+        def pick(t, j0, width, name):
+            tile = kept([P, width], F32, name)
+            nc.vector.tensor_copy(tile[:], g_window[0, t][:].indirect(offsets(j0, width)))
+            for c0 in range(0, width, BANK):
+                picked[t, (j0 + c0) // BANK] = tile[:, c0 : c0 + BANK]
 
         for (t, b), bank in zip(first_units[2:6], (7, 4, 5, 6)):
             turn_product(t, b, bank)
@@ -370,8 +370,9 @@ def tile_list_speaker_affine_flow_kernel(
         share(second[:, S : 2 * S], aside[:, S:], ((1, 0), (2, 0)), 2, middle[:])
         scale[1, 1, 0], scale[1, 2, 0] = middle[:, 0:BANK], middle[:, BANK:]
         for t in range(PACK - 1):
-            pick(t, (0, S))
-        pick(PACK - 1, (0, BANK, S))
+            pick(t, 0, S, "picked%d" % t)
+        pick(PACK - 1, 0, BANK, "cells")
+        pick(PACK - 1, BANK, BANK, "picked3")
         turn_product(0, 0, 0)
         for b in range(S // BANK):
             add_shift(0, b)
@@ -387,17 +388,17 @@ def tile_list_speaker_affine_flow_kernel(
         turn_product(3, 1, 1)
         for b in range(S // BANK):
             add_shift(1, b)
-        cells = kept([P, 12 * NARROW], F32, "g_held")
+        for t in range(2, PACK):
+            for b in range(S // BANK):
+                add_shift(t, b)
+        cells = kept([P, 12 * NARROW], F32, "cells")
 
         def cell(n, count=1):
             return cells[:, n * NARROW : (n + count) * NARROW]
 
-        nc.vector.tensor_tensor(cell(1, 2), scale[1, 3, 0], last_sums[0][:], ALU.mult)
+        nc.vector.tensor_tensor(cell(0, 2), scale[1, 3, 0], last_sums[0][:], ALU.mult)
         nc.vector.tensor_tensor(cell(11), scale[1, 3, 1][:, 0:NARROW], last_sums[1][:, 0:NARROW], ALU.mult)
-        last_products = (cell(1), cell(2), cell(11), last_range)
-        for t in range(2, PACK):
-            for b in range(S // BANK):
-                add_shift(t, b)
+        last_products = (cell(0), cell(1), cell(11), last_range)
         for b in range(S // BANK):
             turn_back(b)
 
@@ -419,17 +420,16 @@ def tile_list_speaker_affine_flow_kernel(
             product = last_products[n] if t == PACK - 1 else scale[1, t, b][:, c0 : c0 + NARROW]
             shift(t, n * NARROW, NARROW, place(n, t), product)
 
-        shift(0, 0, BANK, cell(3, 2), scale[1, 0, 0])
-        shift_narrow(2, 0)
-        shift(1, 0, BANK, cell(5, 2), scale[1, 1, 0])
-        shift(2, 0, BANK, cell(7, 2), scale[1, 2, 0])
+        for t in range(PACK - 1):
+            shift(t, 0, BANK, cell(3 + 2 * t, 2), scale[1, t, 0])
+        shift_narrow(2, 2)
         quantise_h(0, 0, BANK, "middle")
         open_features(0, NARROW, 4)
         for n in range(2):
             shift_narrow(n, 3)
             round_second(nc.scalar.copy, n * NARROW, NARROW, "h_round%d" % n)
+        shift_narrow(2, 0)
         shift_narrow(2, 1)
-        shift_narrow(2, 2)
         quantise_h(1, 0, NARROW, "h_codes1_0")
         features(0, NARROW, "first_early")
         open_features(NARROW, NARROW, 0)

from contextlib import ExitStack

import concourse.mybir as mybir
from concourse.masks import make_identity

K, C, H, N, T, S = 1024, 512, 1024, 512, 2048, 1024
FLOPS = 2 * S * (K * H + C * H + H * N)

F32 = mybir.dt.float32
BF16 = mybir.dt.bfloat16
I32 = mybir.dt.int32
U32 = mybir.dt.uint32
U16 = mybir.dt.uint16
U8 = mybir.dt.uint8
FP8X4 = mybir.dt.float8_e4m3fn_x4
FP4X4 = mybir.dt.float4_e2m1fn_x4
ACT = mybir.ActivationFunctionType
ALU = mybir.AluOpType

P = 128
PACK = 4
PASS = P * PACK
BANK = 512
NARROW = BANK // 2
HALVES = H // PASS
RING = 5
TAB_ROW = 4
RUN = 4


def tile_list_speaker_affine_flow_kernel(
    tc, tab_words, tab_scales, tab2_words, tab2_scales, offs, offs2, wa,
    wb4_words, wb4_scales, gT, w8_words, w8_scales, bias, out,
):
    nc = tc.nc
    with ExitStack() as ctx:
        keep = ctx.enter_context(tc.tile_pool(name="keep", bufs=1))
        ring = ctx.enter_context(tc.tile_pool(name="ring", bufs=RING))
        psum = ctx.enter_context(tc.psum_pool(name="psum", bufs=1))

        def kept(shape, dtype, name):
            return keep.tile(shape, dtype, name=name, align_bytes=64)

        def in_bank(n, shape):
            return psum.tile(shape, F32, name="bank%d" % n)

        idx = keep.tile([P, S // 16], U16, name="idx")
        idx2 = keep.tile([P, S // 16], U16, name="idx2")
        tab_plane = kept([P, T], U8, "tab_plane")
        tab2_plane = kept([P, T], U8, "tab2_plane")
        wb_plane = kept([P, H], U8, "wb_plane")
        w8_plane = kept([P, N], U8, "w8_plane")
        bias_sb = kept([P, N // P], F32, "bias_sb")
        identity = kept([P, P], F32, "identity")

        for plane in (tab2_plane, tab_plane, wb_plane, w8_plane):
            nc.gpsimd.memset(plane[:].bitcast(I32), 0)
        make_identity(nc, identity[:])


        def load_plane_by_quadrant(plane, scales):
            rows = 4 * scales.shape[0]
            for q in range(4):
                nc.sync.dma_start(
                    out=plane[32 * q : 32 * q + rows, :].bitcast(I32),
                    in_=scales[:, 4 * q : 4 * q + 4, :].bitcast(I32),
                )

        def load_plane_by_row(plane, scales, rows, first=0):
            for r in rows:
                for g in range(scales.shape[0]):
                    nc.sync.dma_start(
                        out=plane[first + 4 * g + r : P : 32, :].bitcast(I32), in_=scales[g, r : 16 : 4, :].bitcast(I32)
                    )

        def load_words(words, pool, name):
            window = pool.tile([P, T], U32, name=name, align_bytes=64)
            nc.sync.dma_start(out=window[:].bitcast(I32), in_=words.rearrange("p t i -> p (t i)").bitcast(I32))
            return window

        def load_wa(g, r0, width):
            raw = kept([P, PACK, width], F32, "wa%d_%d" % (g, r0))
            rows = wa[g * PASS : (g + 1) * PASS, r0 : r0 + width]
            nc.sync.dma_start(out=raw[:], in_=rows.rearrange("(p i) r -> p i r", i=PACK))
            return raw

        g_rows = [
            gT[0:PASS].rearrange("(t p) c -> t p c", p=P),
            gT[PASS:H].rearrange("(p t) c -> t p c", t=PACK),
        ]

        def load_g(half, t):
            window = ring.tile([P, T], F32, name="ring", align_bytes=64)
            nc.sync.dma_start(out=window[:], in_=g_rows[half][t])
            return window

        tab_window, wa_raw, g_window = {}, {}, {}
        wb_words = kept([P, 2 * H], U8, "wb_words")
        nc.sync.dma_start(idx2[:], offs2)
        nc.sync.dma_start(idx[:], offs)
        nc.sync.dma_start(out=wb_words[:].bitcast(I32), in_=wb4_words[0].bitcast(I32))
        load_plane_by_row(tab2_plane, tab2_scales, range(4))
        tab2_window = load_words(tab2_words[0], keep, "tab2")
        load_plane_by_quadrant(wb_plane, wb4_scales)
        load_plane_by_row(tab_plane, tab_scales, (0,), TAB_ROW)
        wa_raw[0, 0] = load_wa(0, 0, PASS)
        load_plane_by_row(tab_plane, tab_scales, (1, 2, 3), TAB_ROW)
        tab_window[0] = load_words(tab_words[0], keep, "tab0")
        wa_piece = [load_wa(1, 0, NARROW)]
        tab_window[1] = load_words(tab_words[1], ring, "ring")
        wa_piece.append(load_wa(1, NARROW, NARROW))
        wa_raw[1, 0] = load_wa(0, PASS, PASS)
        wa_raw[1, 1] = load_wa(1, PASS, PASS)
        for half in range(HALVES):
            for t in range(PACK):
                g_window[half, t] = load_g(half, t)
        w8_codes = ring.tile([P, HALVES, N], U32, name="ring", align_bytes=64)
        nc.sync.dma_start(
            out=w8_codes[:].bitcast(I32),
            in_=w8_words.rearrange("a p n i -> p a (n i)").bitcast(I32),
        )
        load_plane_by_quadrant(w8_plane, w8_scales)
        with nc.allow_non_contiguous_dma(reason="one bias value for each partition and tile of rows"):
            nc.sync.dma_start(out=bias_sb[:], in_=bias.rearrange("(q p) -> p q", p=P))


        v2_scales = kept([P, S], U8, "v2_scales")
        v2_codes = kept([P, S], U32, "v2_codes")
        v_scales = kept([P, S], U8, "v_scales")
        v_codes = [[kept([P, BANK], U32, "v_codes%d%d" % (g, b)) for b in range(S // BANK)] for g in range(K // PASS)]
        wb_codes = kept([P, 2 * PASS], U8, "wb_codes")
        h_scales = [kept([P, S], U8, "h_scales%d" % half) for half in range(HALVES)]
        wa_q = {
            (half, g): (
                kept([P, PASS], U32, "wa_codes%d%d" % (half, g) if half + g else "tab0"),
                kept([P, PASS], U8, "wa_scales%d%d" % (half, g)),
            )
            for half in range(HALVES)
            for g in range(K // PASS)
        }
        scale, h_round, h_codes, y_sums = {}, {}, {}, {}

        def offsets(j0, width):
            return idx[:, j0 // 16 : (j0 + width) // 16]

        def gather_words(g):
            for b in range(S // BANK):
                nc.vector.tensor_copy(v_codes[g][b][:], tab_window[g][:].indirect(offsets(b * BANK, BANK)))

        def interleave(copy, grouped, rows):
            copy(
                grouped.rearrange("p (c i t) -> p c t i", i=RUN, t=PACK), rows.rearrange("p t (c i) -> p c t i", i=RUN)
            )

        def round_on_gpsimd(grouped, rows):
            nc.gpsimd.tensor_scalar(
                grouped[:].rearrange("p (r i) -> p r i", i=PACK), rows.rearrange("p i r -> p r i"),
                1.0, 0.0, ALU.mult, ALU.add,
            )

        def quantise_wa(half, g, r0, grouped):
            codes, scales = wa_q[half, g]
            width = grouped.shape[1] // PACK
            nc.vector.quantize_mx(
                out=codes[:, r0 : r0 + width].bitcast(FP8X4),
                scales=scales[:, r0 : r0 + width],
                in_=grouped[:],
            )

        def frames(half, t, j0, bank):
            a_sum = in_bank(bank, [P, BANK])
            for g in range(K // PASS):
                codes, scales = wa_q[half, g]
                nc.tensor.matmul_mx(
                    out=a_sum[:],
                    lhsT=codes[:, t * P : (t + 1) * P].bitcast(FP8X4),
                    lhsT_scale=scales[:, t * P : (t + 1) * P],
                    rhs=v_codes[g][j0 // BANK][:].bitcast(FP8X4),
                    rhs_scale=v_scales[TAB_ROW + 4 * g :, j0 : j0 + BANK],
                    start=(g == 0),
                    stop=(g == K // PASS - 1),
                )
            return a_sum

        def speaker_scale(half, t, j0, dest, bank):
            cols = slice(j0, j0 + BANK)
            codes, scales = (wb_words, wb_plane) if half == 0 else (wb_codes, wb_scales)
            b_sum = in_bank(bank, [P, BANK])
            nc.tensor.matmul_mx(
                out=b_sum[:],
                lhsT=codes[:, 2 * t * P : 2 * (t + 1) * P].bitcast(FP4X4),
                lhsT_scale=scales[:, t * P : (t + 1) * P],
                rhs=v2_codes[:, cols].bitcast(FP8X4),
                rhs_scale=v2_scales[:, cols],
                start=True,
                stop=True,
            )
            nc.scalar.activation(dest, b_sum[:], ACT.Exp)

        def exponentials(units, cells, banks):
            for n, (half, t, b) in enumerate(units):
                scale[half, t, b] = cells[:, n * BANK : (n + 1) * BANK]
                speaker_scale(half, t, b * BANK, scale[half, t, b], banks[n])

        def shift(t, j0, width, dest, product):
            nc.vector.tensor_tensor(dest, g_window[1, t][:].indirect(offsets(j0, width)), product, ALU.add)

        def quantise_h(half, j0, width, name):
            h_codes[half, j0] = kept([P, width], U32, name)
            nc.vector.quantize_mx(
                out=h_codes[half, j0][:].bitcast(FP8X4),
                scales=h_scales[half][:, j0 : j0 + width],
                in_=h_round[half, j0][:],
            )

        def feature_pass(half, j0, width, y_sum, q):
            base = j0 if half == 1 else j0 // BANK * BANK
            nc.tensor.matmul_mx(
                out=y_sum[:],
                lhsT=w8_codes[:, half, q * P : (q + 1) * P].bitcast(FP8X4),
                lhsT_scale=w8_plane[4 * half :, q * P : (q + 1) * P],
                rhs=h_codes[half, base][:, j0 - base : j0 - base + width].bitcast(FP8X4),
                rhs_scale=h_scales[half][:, j0 : j0 + width],
                start=(half == 0),
                stop=(half == HALVES - 1),
            )

        def open_features(j0, width, bank):
            y_sums[j0] = [in_bank(bank + q, [P, width]) for q in range(N // P)]
            for q in range(N // P):
                feature_pass(0, j0, width, y_sums[j0][q], q)

        def features(j0, width, name):
            cols = slice(j0, j0 + width)
            y = kept([P, N // P, width], F32, name)
            for q in range(N // P):
                y_sum = y_sums[j0][q]
                feature_pass(1, j0, width, y_sum, q)
                if width == P and q % 2 == 1:
                    nc.vector.tensor_scalar_add(y[:, q], y_sum[:], bias_sb[:, q : q + 1])
                else:
                    nc.scalar.activation(y[:, q], y_sum[:], ACT.Identity, bias=bias_sb[:, q : q + 1])
                if q % 2 == 1:
                    rows = slice(q - 1, q + 1)
                    nc.sync.dma_start(out=out.rearrange("(q p) j -> p q j", p=P)[:, rows, cols], in_=y[:, rows])


        nc.scalar.copy(
            wb_codes[:].bitcast(U16).rearrange("p (t m) -> p t m", t=PACK),
            wb_words[:, 2 * PASS :].bitcast(U16).rearrange("p (m t) -> p t m", t=PACK),
        )
        nc.vector.tensor_copy(v2_scales[:], tab2_plane[:].indirect(idx2[:]))
        for j0 in range(0, S, BANK):
            nc.vector.tensor_copy(
                v2_codes[:, j0 : j0 + BANK], tab2_window[:].indirect(idx2[:, j0 // 16 : (j0 + BANK) // 16])
            )
        wb_scales = kept([P, PASS], U8, "wb_scales")
        nc.gpsimd.tensor_copy(
            wb_scales[:].rearrange("p (t m) -> p t m", t=PACK),
            wb_plane[:, PASS:].rearrange("p (m t) -> p t m", t=PACK),
        )
        nc.vector.tensor_copy(v_scales[:], tab_plane[:].indirect(idx[:]))
        first_grouped = kept([P, PASS * PACK], BF16, "picked0")
        round_on_gpsimd(first_grouped, wa_raw[0, 0][:])
        gather_words(0)
        quantise_wa(0, 0, 0, first_grouped)
        grouped_piece = [kept([P, NARROW * PACK], BF16, "grouped_piece")]
        round_on_gpsimd(grouped_piece[0], wa_piece[0][:])
        quantise_wa(0, 1, 0, grouped_piece[0])
        grouped_piece.append(kept([P, NARROW * PACK], BF16, "grouped_piece"))
        round_on_gpsimd(grouped_piece[1], wa_piece[1][:])
        gather_words(1)


        first_units = [(0, 0), (1, 0), (0, 1), (1, 1), (2, 0), (3, 0), (2, 1), (3, 1)]
        exponentials([(0, t, b) for t, b in first_units], kept([P, 8 * BANK], F32, "first_early"), (4, 5, 6, 7) * 2)
        second = kept([P, 8 * BANK], F32, "second")
        second_units = [(1, 0, 0), (1, 0, 1), (1, 1, 0), (1, 2, 0), (1, 1, 1), (1, 2, 1), (1, 3, 0), (1, 3, 1)]
        exponentials(second_units[:7], second, (4, 5, 6, 7) * 2)


        def first_products(units, bank, held=None):
            for n, (t, b) in enumerate(units):
                a_sum = frames(0, t, b * BANK, bank + n)
                product = scale[0, t, b] if held is None else held[:, n * BANK : (n + 1) * BANK]
                nc.vector.tensor_tensor(product, scale[0, t, b], a_sum[:], ALU.mult)
                scale[0, t, b] = product

        first_products(first_units[0:2], 0)
        quantise_wa(0, 1, NARROW, grouped_piece[1])
        first_products(first_units[2:4], 2, kept([P, S], F32, "wa1_256"))
        first_products(first_units[4:6], 0)

        def round_slots(g, t0, count):
            grouped = kept([P, count * PASS], BF16, "grouped1%d%d" % (g, t0))
            nc.scalar.copy(
                grouped[:].rearrange("p (t m i) -> p m i t", t=count, i=PACK),
                wa_raw[1, g][:].rearrange("p i (m t) -> p m i t", t=PACK)[:, :, :, t0 : t0 + count],
            )
            return grouped

        last_slot = kept([P, PASS], BF16, "grouped_piece")
        round_on_gpsimd(last_slot, wa_raw[1, 0][:].rearrange("p i (m t) -> p t i m", t=PACK)[:, PACK - 1])
        slots_of_wa = [round_slots(0, 0, PACK - 1), round_slots(1, 0, 2), round_slots(1, 2, 2)]
        quantise_wa(1, 0, 0, slots_of_wa[0])
        quantise_wa(1, 0, (PACK - 1) * P, last_slot)
        first_products(first_units[6:7], 2, kept([P, BANK], F32, "wa0_512"))
        quantise_wa(1, 1, 0, slots_of_wa[1])
        quantise_wa(1, 1, 2 * P, slots_of_wa[2])
        first_aside = kept([P, BANK], F32, "grouped110")
        nc.scalar.copy(first_aside[:], frames(0, PACK - 1, BANK, 3)[:])
        first_last = kept([P, BANK], F32, "grouped112")
        nc.gpsimd.tensor_tensor(first_last[:], scale[0, 3, 1], first_aside[:], ALU.mult)
        scale[0, 3, 1] = first_last[:]


        aside = kept([P, 4 * BANK], F32, "aside")
        aside_late = kept([P, 2 * BANK], F32, "aside_late")

        def share(exps, copies, units, bank, product=None):
            for n, (t, b) in enumerate(units):
                a_sum = frames(1, t, b * BANK, bank + n)
                nc.scalar.copy(copies[:, n * BANK : (n + 1) * BANK], a_sum[:])
            nc.gpsimd.tensor_tensor(exps if product is None else product, exps, copies, ALU.mult)

        turned = kept([P, S // P, 2, 2 * P], BF16, "tab2")
        h_sums, picked = {}, {}

        def turn(t, b, source, first):
            for c in range(BANK // P):
                nc.tensor.matmul(
                    h_sums[t, b][:, c], source[:, c * P : (c + 1) * P], identity[:], is_transpose=True,
                    start=first and c == 0, stop=not first and c == BANK // P - 1,
                )

        def turn_product(t, b, bank):
            h_sums[t, b] = in_bank(bank, [P, BANK // P, P])
            turn(t, b, scale[0, t, b], True)

        def add_shift(t, b):
            turn(t, b, picked[t, b], False)
            nc.scalar.copy(
                turned[:, 4 * b : 4 * b + 4, :, 64 * t : 64 * (t + 1)].rearrange("p c u (w e) -> p c u w e", e=2),
                h_sums[t, b][:].rearrange("p c (w u e) -> p c u w e", u=2, e=2),
            )

        def turn_back(b):
            h_round[0, b * BANK] = kept([P, BANK * PACK], BF16, "h_first%d" % b)
            words = h_round[0, b * BANK][:].bitcast(F32)
            for n in range(2):
                pairs = in_bank((3, 4, 5, 6)[2 * b + n], [P, 2, 2, P])
                for c in range(2):
                    for u in range(2):
                        nc.tensor.transpose(pairs[:, c, u], turned[:, 4 * b + 2 * n + c, u].bitcast(F32), identity[:])
                nc.scalar.copy(
                    words[:, n * BANK : (n + 1) * BANK].rearrange("p (c j u) -> p c j u", c=2, u=2),
                    pairs[:].rearrange("p c u j -> p c j u"),
                )

        def pick(t, j0, width, name):
            tile = kept([P, width], F32, name)
            nc.vector.tensor_copy(tile[:], g_window[0, t][:].indirect(offsets(j0, width)))
            for c0 in range(0, width, BANK):
                picked[t, (j0 + c0) // BANK] = tile[:, c0 : c0 + BANK]

        for (t, b), bank in zip(first_units[2:6], (7, 4, 5, 6)):
            turn_product(t, b, bank)
        share(second[:, 0:S], aside[:, 0:S], ((0, 0), (0, 1)), 0)
        middle = kept([P, S], F32, "middle")
        share(second[:, S : 2 * S], aside[:, S:], ((1, 0), (2, 0)), 2, middle[:])
        scale[1, 1, 0], scale[1, 2, 0] = middle[:, 0:BANK], middle[:, BANK:]
        for t in range(PACK - 1):
            pick(t, 0, S, "picked%d" % t)
        pick(PACK - 1, 0, BANK, "cells")
        pick(PACK - 1, BANK, BANK, "picked3")
        turn_product(0, 0, 0)
        for b in range(S // BANK):
            add_shift(0, b)
        share(second[:, 2 * S : 3 * S], aside_late[:], ((1, 1), (2, 1)), 1)
        turn_product(1, 0, 3)
        exponentials(second_units[7:], second[:, 7 * BANK :], (1,))
        last_sums = [frames(1, PACK - 1, b * BANK, 7 * b) for b in range(S // BANK)]
        aside_last = kept([P, NARROW], F32, "aside_last")
        nc.scalar.copy(aside_last[:], last_sums[1][:, NARROW:])
        last_range = scale[1, 3, 1][:, NARROW:]
        nc.gpsimd.tensor_tensor(last_range, last_range, aside_last[:], ALU.mult)
        turn_product(2, 1, 2)
        turn_product(3, 1, 1)
        for b in range(S // BANK):
            add_shift(1, b)
        for t in range(2, PACK):
            for b in range(S // BANK):
                add_shift(t, b)
        cells = kept([P, 12 * NARROW], F32, "cells")

        def cell(n, count=1):
            return cells[:, n * NARROW : (n + count) * NARROW]

        nc.vector.tensor_tensor(cell(0, 2), scale[1, 3, 0], last_sums[0][:], ALU.mult)
        nc.vector.tensor_tensor(cell(11), scale[1, 3, 1][:, 0:NARROW], last_sums[1][:, 0:NARROW], ALU.mult)
        last_products = (cell(0), cell(1), cell(11), last_range)
        for b in range(S // BANK):
            turn_back(b)


        places = ((3, 2), (4, 2), (0, 1), (3, 1))

        def place(n, t):
            first, step = places[n]
            return cell(first + step * t)

        def round_second(copy, j0, width, name):
            first, step = places[j0 // NARROW]
            slots = cells[:].rearrange("p (n c) -> p n c", c=NARROW)[:, first : first + 3 * step + 1 : step]
            h_round[1, j0] = kept([P, width * PACK], BF16, name)
            interleave(copy, h_round[1, j0][:], slots[:, :, j0 % NARROW : j0 % NARROW + width])

        def shift_narrow(n, t):
            b, c0 = divmod(n * NARROW, BANK)
            product = last_products[n] if t == PACK - 1 else scale[1, t, b][:, c0 : c0 + NARROW]
            shift(t, n * NARROW, NARROW, place(n, t), product)

        for t in range(PACK - 1):
            shift(t, 0, BANK, cell(3 + 2 * t, 2), scale[1, t, 0])
        shift_narrow(2, 2)
        quantise_h(0, 0, BANK, "middle")
        open_features(0, NARROW, 4)
        for n in range(2):
            shift_narrow(n, 3)
            round_second(nc.scalar.copy, n * NARROW, NARROW, "h_round%d" % n)
        shift_narrow(2, 0)
        shift_narrow(2, 1)
        quantise_h(1, 0, NARROW, "h_codes1_0")
        features(0, NARROW, "first_early")
        open_features(NARROW, NARROW, 0)
        shift_narrow(2, 3)
        round_second(nc.scalar.copy, BANK, NARROW, "h_codes1_0")
        quantise_h(0, BANK, BANK, "h_round0")
        open_features(BANK, NARROW, 4)
        quantise_h(1, NARROW, NARROW, "h_codes1_1")
        features(NARROW, NARROW, "wa0_0")
        open_features(S - NARROW, P, 0)
        for t in range(1, PACK):
            shift_narrow(3, t)
        quantise_h(1, BANK, NARROW, "h_codes1_2")
        features(BANK, NARROW, "aside")
        open_features(S - P, P, 4)
        last = S - NARROW
        for j0 in range(last, S, P):
            c0 = j0 - last
            shift(0, j0, P, place(3, 0)[:, c0 : c0 + P], scale[1, 0, 1][:, NARROW + c0 : NARROW + c0 + P])
        for j0 in range(last, S, P):
            round_second(nc.vector.tensor_copy, j0, P, "h_last%d" % j0)
        for j0 in range(last, S, P):
            quantise_h(1, j0, P, "h_codes1_%d" % j0)
        for j0 in range(last, S, P):
            features(j0, P, "y%d" % j0)
